import numpy as np
import ml_dtypes


def mxq(x, axis, fmt="e4m3"):
    dtype, down = {"e4m3": (ml_dtypes.float8_e4m3fn, 7), "e5m2": (ml_dtypes.float8_e5m2, 14)}[fmt]
    v = np.moveaxis(np.asarray(x, np.float32).astype(ml_dtypes.bfloat16).astype(np.float64), axis, -1)
    blocks = v.reshape(v.shape[:-1] + (-1, 32))
    amax = np.abs(blocks).max(-1, keepdims=True)
    byte = np.maximum(np.where(amax > 0, np.frexp(amax)[1] - 1 + 127, 0) - down, 1)
    scale = np.exp2(byte - 127.0)
    codes = (blocks / scale).astype(np.float32).astype(dtype).astype(np.float64)
    return np.moveaxis((codes * scale).reshape(v.shape), -1, axis)


WIDE = False


def mx_kscale(k):
    if not WIDE:
        return np.ones(k)
    levels = np.array([10, -10, 5, -5, 0])
    if k % 512:
        return np.exp2(np.random.permutation(np.resize(levels, k // 32))).repeat(32)
    a = np.empty((k // 512, 16))
    for p in range(k // 512):
        a[p, :8] = np.random.permutation(np.resize(levels, 8))
        for g in range(8):
            far = levels[np.abs(levels - a[p, g]) >= 10]
            a[p, g + 8] = far[np.random.randint(len(far))]
    return np.exp2(a.ravel()).repeat(32)


def f64(x):
    return np.asarray(x).astype(np.float64)


def striped(idx):
    return np.tile(idx.reshape(-1, 16).T, (8, 1)).astype(np.uint16)


def unstriped(offs):
    return offs[:16].T.reshape(-1).astype(np.int64)


E2M1 = np.array([0.0, 0.5, 1.0, 1.5, 2.0, 3.0, 4.0, 6.0, -0.0, -0.5, -1.0, -1.5, -2.0, -3.0, -4.0, -6.0])


def pack_weight(w, fmt):
    k, n = w.shape
    w = f64(np.asarray(w, np.float32).astype(ml_dtypes.bfloat16)).reshape(k // 32, 32, n)
    amax = np.abs(w).max(1)
    if fmt == "e4m3":
        byte = np.frexp(amax)[1] - 1 + 127 - 7
    else:
        mant, ex = np.frexp(amax / 6.0)
        byte = np.where(mant > 0.5, ex, ex - 1) + 127
    byte = np.clip(np.where(amax > 0, byte, 1), 1, 254)
    scaled = (w * np.exp2(127.0 - byte)[:, None, :]).reshape(k, n).astype(np.float32)
    by_word = np.ascontiguousarray(scaled.reshape(k // 512, 128, 4, n).transpose(0, 1, 3, 2))
    if fmt == "e4m3":
        words = by_word.astype(ml_dtypes.float8_e4m3fn).view(np.uint8)
    else:
        c = by_word.astype(ml_dtypes.float4_e2m1fn).view(np.uint8) & 0xF
        words = (c[..., 0::2] | (c[..., 1::2] << 4)).reshape(k // 512, 128, 2 * n)
    return np.ascontiguousarray(words), np.ascontiguousarray(byte.astype(np.uint8).reshape(k // 512, 16, n))


def unpack_weight(words, scales, fmt):
    g, _, n = scales.shape
    words = np.ascontiguousarray(words).reshape(g, 128, n, -1)
    if fmt == "e4m3":
        vals = words.view(ml_dtypes.float8_e4m3fn).astype(np.float64)
    else:
        nib = np.empty((g, 128, n, 4), np.uint8)
        nib[..., 0::2] = words & 0xF
        nib[..., 1::2] = words >> 4
        vals = E2M1[nib]
    vals = vals * np.repeat(np.exp2(scales.astype(np.float64) - 127.0), 8, axis=1)[..., None]
    return vals.transpose(0, 1, 3, 2).reshape(g * 512, n)


def gelu(v):
    return 0.5 * v * (1.0 + np.tanh(np.sqrt(2.0 / np.pi) * (v + 0.044715 * v**3)))


K, H, N, T, S, T2, P = 1024, 512, 384, 2048, 1024, 2048, 1024

def setup_inputs():
    n = np.random.standard_normal
    s = mx_kscale(K)[:, None]
    u = mx_kscale(H)[:, None]
    ru = np.sqrt(u)
    tab_words, tab_scales = pack_weight(n((K, T)) * s, "e4m3")
    w2_words, w2_scales = pack_weight(0.8 * n((K, H)) / np.sqrt(K) / s * ru.T, "e2m1")
    w3_words, w3_scales = pack_weight(n((H, N)) / np.sqrt(H) / u, "e4m3")
    return {
        "tab_words": tab_words, "tab_scales": tab_scales,
        "offs": striped(np.random.permutation(T)[:S]),
        "w1": (0.8 * n((K, H)) / np.sqrt(K) / s * ru.T).astype(np.float32),
        "w2_words": w2_words, "w2_scales": w2_scales,
        "wgs": np.exp(0.3 * n((128, S))).astype(np.float32),
        "offs2": striped(np.random.permutation(T2)[:S]),
        "board": (n((H, T2)) * u).astype(np.float32),
        "w3_words": w3_words, "w3_scales": w3_scales,
        "offs3": striped(np.random.permutation(T2)[:P]),
        "prio": n((N, P)).astype(np.float32),
        "wgo": np.exp(0.3 * n((128, P))).astype(np.float32),
        "offs4": striped(np.random.permutation(T2)[:P]),
    }

def reference(tab_words, tab_scales, offs, w1, w2_words, w2_scales, wgs, offs2, board,
              w3_words, w3_scales, offs3, prio, wgo, offs4):
    v = unpack_weight(tab_words, tab_scales, "e4m3")[:, unstriped(offs)]
    a = mxq(f64(w1), 0, "e4m3").T @ v
    b = unpack_weight(w2_words, w2_scales, "e2m1").T @ v
    h = (a + b) * (a - b)
    page = np.zeros((H, T2))
    page[:, unstriped(offs2)] = np.tile(f64(wgs), (H // 128, 1)) * h
    z = page + f64(board)
    y = unpack_weight(w3_words, w3_scales, "e4m3").T @ mxq(z, 0, "e4m3")
    x = y[:, unstriped(offs3)]
    x = f64(prio) * (1.0 / (1.0 + np.exp(-x)))
    out = np.zeros((N, T2))
    out[:, unstriped(offs4)] = np.tile(f64(wgo), (N // 128, 1)) * x
    return out

@@ -1,0 +1,287 @@
+from contextlib import ExitStack
+
+import concourse.mybir as mybir
+from concourse.masks import make_identity
+
+K, H, N, T, S = 1024, 512, 384, 2048, 1024
+FLOPS = 2 * (2 * K * H * S + H * N * T)
+
+F32 = mybir.dt.float32
+BF16 = mybir.dt.bfloat16
+I32 = mybir.dt.int32
+U32 = mybir.dt.uint32
+U16 = mybir.dt.uint16
+U8 = mybir.dt.uint8
+FP8X4 = mybir.dt.float8_e4m3fn_x4
+FP4X4 = mybir.dt.float4_e2m1fn_x4
+ACT = mybir.ActivationFunctionType
+ALU = mybir.AluOpType
+
+P = 128
+BANK = 512
+PASSES = K // 512
+ROW_BLOCKS = H // P
+OUT_BLOCKS = N // P
+HALVES = S // BANK
+CHUNKS = T // BANK
+HALF_COLS = BANK // 16
+PIECES = (2, 1, 1, 1)
+
+
+def tile_list_pass_arbitration_scores_kernel(
+    tc, tab_words, tab_scales, offs, w1, w2_words, w2_scales, wgs, offs2, board,
+    w3_words, w3_scales, offs3, prio, wgo, offs4, out,
+):
+    nc = tc.nc
+    with ExitStack() as ctx:
+        sb = ctx.enter_context(tc.tile_pool(name="sb", bufs=1))
+        ps = ctx.enter_context(tc.psum_pool(name="ps", bufs=1))
+
+        def alloc(shape, dtype, name, tag=None):
+            return sb.tile(shape, dtype, name=name, tag=tag or name, align_bytes=64)
+
+        def bank(index, name):
+            return ps.tile([P, BANK], F32, name=name, tag="bank%d" % index)
+
+        def load_list(src, name):
+            dst = alloc([P, S // 16], U16, name)
+            nc.sync.dma_start(dst[:], src)
+            return dst
+
+        def load(src, shape, name, tag=None):
+            dst = alloc(shape, F32, name, tag)
+            nc.sync.dma_start(dst[:], src)
+            return dst
+
+        def zeroed_plane(width, name):
+            plane = alloc([P, width], U8, name)
+            nc.vector.memset(plane[:].bitcast(I32), 0)
+            return plane
+
+        def load_table_pass(a):
+            words = alloc([P, T], U32, "tab_words_%d" % a, "wide%d" % a)
+            nc.sync.dma_start(words[:].bitcast(I32), tab_words[a].rearrange("p t i -> p (t i)").bitcast(I32))
+            return words
+
+        def load_w1(first, last):
+            raws = []
+            for a in range(PASSES):
+                rows = w1[512 * a : 512 * (a + 1), first:last].rearrange("(p j) c -> p j c", j=4)
+                raws.append(load(rows, [P, 4, last - first], "w1_raw_%d_%d" % (first, a), "w1_raw_%d" % a))
+            return raws
+
+        idx = load_list(offs, "idx")
+        tab_plane = alloc([P, T], U8, "tab_plane", "weights")
+        nc.sync.dma_start(tab_plane[96:P, :].bitcast(I32), tab_scales.rearrange("a q c -> q a c").bitcast(I32))
+        nc.vector.memset(tab_plane[0:96, :].bitcast(I32), 0)
+        tab_tiles = [load_table_pass(0)]
+        w1_raw = load_w1(0, P)
+        idx2 = load_list(offs2, "idx2")
+        tab_tiles.append(load_table_pass(1))
+        w2_codes = alloc([P, PASSES, 2 * H], U8, "w2_codes")
+        nc.sync.dma_start(w2_codes[:].bitcast(I32), w2_words.rearrange("a p c -> p a c").bitcast(I32))
+
+        ident = alloc([P, P], F32, "ident")
+        make_identity(nc, ident[:])
+        warm = alloc([P, 1], F32, "warm")
+        nc.scalar.activation(warm[:], ident[:, 0:1], ACT.Sigmoid)
+
+        v_plane = zeroed_plane(PASSES * S, "v_plane")
+        picked_plane = alloc([P, S], U8, "picked_plane")
+        nc.vector.tensor_copy(picked_plane[:], tab_plane[:].indirect(idx[:]))
+        for q in range(4):
+            nc.sync.dma_start(
+                v_plane[32 * q : 32 * q + 4, :].bitcast(I32),
+                picked_plane[96 + 8 * q : 96 + 8 * (q + 1), :].bitcast(I32),
+            )
+
+        w2_plane = zeroed_plane(PASSES * H, "w2_plane")
+        for q in range(4):
+            nc.gpsimd.dma_start(
+                w2_plane[32 * q : 32 * q + 4, :].rearrange("p (a c) -> p a c", a=PASSES).bitcast(I32),
+                w2_scales[:, 4 * q : 4 * q + 4, :].rearrange("a r c -> r a c").bitcast(I32),
+            )
+        wgs_sb = load(wgs, [P, S], "wgs_sb", "weights")
+        idx3 = load_list(offs3, "idx3")
+        idx4 = load_list(offs4, "idx4")
+
+        v_words = {}
+        for a in range(PASSES):
+            for h in range(HALVES):
+                picked = alloc([P, BANK], U32, "v_words_%d_%d" % (a, h))
+                nc.vector.tensor_copy(picked[:], tab_tiles[a][:].indirect(idx[:, HALF_COLS * h : HALF_COLS * (h + 1)]))
+                v_words[(a, h)] = picked
+
+        squares = []
+        for b in range(ROW_BLOCKS):
+            if b == 1:
+                w1_raw = load_w1(P, H)
+            first = P * max(b - 1, 0)
+            width = S // PIECES[b]
+            squares.append(
+                [
+                    (alloc([P, width], F32, "a_sq_%d_%d" % (b, i)), alloc([P, width], F32, "b_sq_%d_%d" % (b, i)))
+                    for i in range(PIECES[b])
+                ]
+            )
+            grouped = alloc([P, PASSES, P, 4], BF16, "w1_grouped_%d" % b, "late%d" % b)
+            for a in range(PASSES):
+                nc.scalar.copy(
+                    grouped[:, a, :, :].rearrange("p (c i) j -> p c j i", i=4),
+                    w1_raw[a][:, :, first : first + P].rearrange("p j (c i) -> p c j i", i=4),
+                )
+            w1_codes = alloc([P, PASSES * P], U32, "w1_codes_%d" % b)
+            w1_plane = alloc([P, PASSES * P], U8, "w1_plane_%d" % b)
+            nc.vector.quantize_mx(
+                out=w1_codes[:].bitcast(FP8X4), scales=w1_plane[:], in_=grouped[:].rearrange("p a c j -> p (a c j)")
+            )
+            for h in range(HALVES):
+                a_ps = bank(4 + 2 * h, "a_ps")
+                b_ps = bank(5 + 2 * h, "b_ps")
+                for a in range(PASSES):
+                    nc.tensor.matmul_mx(
+                        out=a_ps[:],
+                        lhsT=w1_codes[:, P * a : P * (a + 1)].bitcast(FP8X4),
+                        lhsT_scale=w1_plane[:, P * a : P * (a + 1)],
+                        rhs=v_words[(a, h)][:].bitcast(FP8X4),
+                        rhs_scale=v_plane[:, S * a + BANK * h : S * a + BANK * (h + 1)],
+                        start=(a == 0),
+                        stop=(a == PASSES - 1),
+                    )
+                for a in range(PASSES):
+                    nc.tensor.matmul_mx(
+                        out=b_ps[:],
+                        lhsT=w2_codes[:, a, 2 * P * b : 2 * P * (b + 1)].bitcast(FP4X4),
+                        lhsT_scale=w2_plane[:, H * a + P * b : H * a + P * (b + 1)],
+                        rhs=v_words[(a, h)][:].bitcast(FP8X4),
+                        rhs_scale=v_plane[:, S * a + BANK * h : S * a + BANK * (h + 1)],
+                        start=(a == 0),
+                        stop=(a == PASSES - 1),
+                    )
+                piece, start = divmod(BANK * h, width)
+                a_sq, b_sq = squares[b][piece]
+                nc.scalar.activation(a_sq[:, start : start + BANK], a_ps[:], ACT.Square)
+                nc.scalar.activation(b_sq[:, start : start + BANK], b_ps[:], ACT.Square)
+
+        board_tags = ("w1_raw_0", "w1_raw_1", "v_words_0_1", "v_words_1_1")
+        boards = [load(board[P * b : P * (b + 1), :], [P, T], "board_%d" % b, board_tags[b]) for b in range(ROW_BLOCKS)]
+        w3_codes = alloc([P, N], U32, "w3_codes", "v_words_0_0")
+        nc.sync.dma_start(w3_codes[:].bitcast(I32), w3_words[0].rearrange("p c i -> p (c i)").bitcast(I32))
+        w3_plane = alloc([P, N], U8, "w3_plane", "v_words_1_0")
+        nc.gpsimd.memset(w3_plane[:].bitcast(I32), 0)
+        for q in range(4):
+            nc.sync.dma_start(
+                w3_plane[32 * q : 32 * q + 4, :].bitcast(I32), w3_scales[0, 4 * q : 4 * q + 4, :].bitcast(I32)
+            )
+
+        page_tags = ("page_0", "a_sq_0_0", "a_sq_0_1", "a_sq_1_0")
+        z_turned = [alloc([P, 4, 2, P, 2], BF16, "z_turned_%d" % c) for c in range(CHUNKS)]
+        for b in range(ROW_BLOCKS):
+            page = alloc([P, T], F32, "page_%d" % b, page_tags[b])
+            (nc.vector if b == 0 else nc.gpsimd).memset(page[:], 0.0)
+            pieces = PIECES[b]
+            width = S // pieces
+            for h in range(pieces):
+                a_sq, b_sq = squares[b][h]
+                tag = "late%d" % (b + 1) if h == pieces - 1 else "contest_first"
+                contest = alloc([P, width], F32, "contest_%d_%d" % (b, h), tag)
+                cols = slice(width * h, width * (h + 1))
+                nc.vector.tensor_tensor(contest[:], a_sq[:], b_sq[:], ALU.subtract)
+                nc.vector.tensor_tensor(
+                    page[:].indirect(idx2[:, width // 16 * h : width // 16 * (h + 1)]), contest[:], wgs_sb[:, cols], ALU.mult
+                )
+            sums = [bank(c, "z_ps") for c in range(CHUNKS)]
+            for c in range(CHUNKS):
+                for s in range(4):
+                    slots = slice(BANK * c + P * s, BANK * c + P * (s + 1))
+                    nc.tensor.matmul(
+                        sums[c][:, P * s : P * (s + 1)], boards[b][:, slots], ident[:],
+                        start=(s == 0), stop=False, is_transpose=True,
+                    )
+            for c in range(CHUNKS):
+                for s in range(4):
+                    slots = slice(BANK * c + P * s, BANK * c + P * (s + 1))
+                    nc.tensor.matmul(
+                        sums[c][:, P * s : P * (s + 1)], page[:, slots], ident[:],
+                        start=False, stop=(s == 3), is_transpose=True,
+                    )
+                nc.scalar.copy(
+                    z_turned[c][:, :, :, 32 * b : 32 * (b + 1), :],
+                    sums[c][:].rearrange("p (s i u e) -> p s u i e", s=4, u=2, e=2),
+                )
+
+        wgo_sb = load(wgo, [P, S], "wgo_sb", "b_sq_0_0")
+        prios = [
+            load(prio[P * n : P * (n + 1), :], [P, S], "prio_%d" % n, ("b_sq_0_1", "late1", "late2")[n])
+            for n in range(OUT_BLOCKS)
+        ]
+
+        z_codes, z_planes = [], []
+        scores = [alloc([P, T], F32, "scores_0", "wide0")]
+
+        def score(n, c, index):
+            y_ps = bank(index, "y_ps")
+            nc.tensor.matmul_mx(
+                out=y_ps[:],
+                lhsT=w3_codes[:, P * n : P * (n + 1)].bitcast(FP8X4),
+                lhsT_scale=w3_plane[:, P * n : P * (n + 1)],
+                rhs=z_codes[c][:].bitcast(FP8X4),
+                rhs_scale=z_planes[c][:],
+                start=True,
+                stop=True,
+            )
+            nc.scalar.activation(scores[n][:, BANK * c : BANK * (c + 1)], y_ps[:], ACT.Sigmoid)
+
+        for c in range(CHUNKS):
+            z_grouped = alloc([P, BANK, 4], BF16, "z_grouped_%d" % c, "z_grouped_%d" % (c % 2))
+            z_pairs = z_turned[c][:].rearrange("p s u r e -> p (s u r e)").bitcast(F32)
+            for half in range(2):
+                back = bank(4 + 2 * (c % 2) + half, "back_ps")
+                for i in range(4):
+                    nc.tensor.transpose(
+                        back[:, P * i : P * (i + 1)], z_pairs[:, BANK * half + P * i : BANK * half + P * (i + 1)], ident[:]
+                    )
+                dst = z_grouped[:, 256 * half : 256 * (half + 1), :].rearrange("p c j -> p (c j)").bitcast(F32)
+                dst = dst.rearrange("p (s c u) -> p s c u", s=2, u=2)
+                src = back[:].rearrange("p (s u c) -> p s c u", s=2, u=2)
+                if half == 0:
+                    nc.scalar.copy(dst, src)
+                else:
+                    nc.vector.tensor_copy(dst, src)
+            codes = alloc([P, BANK], U32, "z_codes_%d" % c)
+            plane = alloc([P, BANK], U8, "z_plane_%d" % c)
+            nc.vector.quantize_mx(
+                out=codes[:].bitcast(FP8X4), scales=plane[:], in_=z_grouped[:].rearrange("p c j -> p (c j)")
+            )
+            z_codes.append(codes)
+            z_planes.append(plane)
+            score(0, c, c)
+
+        gains = alloc([P, OUT_BLOCKS, S], F32, "gains", "weights")
+        for n in range(OUT_BLOCKS):
+            nc.vector.tensor_tensor(gains[:, n, :], prios[n][:], wgo_sb[:], ALU.mult)
+        scores.append(alloc([P, T], F32, "scores_1", "z_grouped_1"))
+        scores.append(alloc([P, T], F32, "scores_2", "wide1"))
+        for n in range(1, OUT_BLOCKS):
+            for c in range(CHUNKS):
+                score(n, c, c)
+
+        rows = []
+        for n in range(OUT_BLOCKS):
+            row = alloc([P, T], F32, "rows_%d" % n, ("b_sq_1_0", "a_sq_2_0", "b_sq_2_0")[n])
+            nc.gpsimd.memset(row[:], 0.0)
+            rows.append(row)
+
+        gates = []
+
+        def pick(n):
+            gate = alloc([P, S], F32, "gate_%d" % n, ("a_sq_3_0", "b_sq_3_0")[n % 2])
+            nc.vector.tensor_copy(gate[:], scores[n][:].indirect(idx3[:]))
+            gates.append(gate)
+
+        pick(0)
+        for n in range(OUT_BLOCKS):
+            if n + 1 < OUT_BLOCKS:
+                pick(n + 1)
+            nc.vector.tensor_tensor(rows[n][:].indirect(idx4[:]), gates[n][:], gains[:, n, :], ALU.mult)
+            nc.sync.dma_start(out[P * n : P * (n + 1), :], rows[n][:])

@@ -71,15 +71,14 @@ def tile_list_pass_arbitration_scores_kernel(
             return raws
 
         idx = load_list(offs, "idx")
-        tab_plane = alloc([P, T], U8, "tab_plane", "weights")
+        tab_plane = alloc([P, T], U8, "tab_plane", "wide1")
         nc.sync.dma_start(tab_plane[96:P, :].bitcast(I32), tab_scales.rearrange("a q c -> q a c").bitcast(I32))
         nc.vector.memset(tab_plane[0:96, :].bitcast(I32), 0)
-        tab_tiles = [load_table_pass(0)]
-        w1_raw = load_w1(0, P)
         idx2 = load_list(offs2, "idx2")
-        tab_tiles.append(load_table_pass(1))
-        w2_codes = alloc([P, PASSES, 2 * H], U8, "w2_codes")
-        nc.sync.dma_start(w2_codes[:].bitcast(I32), w2_words.rearrange("a p c -> p a c").bitcast(I32))
+        idx3 = load_list(offs3, "idx3")
+        tab_tiles = [load_table_pass(0)]
+        idx4 = load_list(offs4, "idx4")
+        w1_raw = load_w1(0, P)
 
         ident = alloc([P, P], F32, "ident")
         make_identity(nc, ident[:])
@@ -94,6 +93,9 @@ def tile_list_pass_arbitration_scores_kernel(
                 v_plane[32 * q : 32 * q + 4, :].bitcast(I32),
                 picked_plane[96 + 8 * q : 96 + 8 * (q + 1), :].bitcast(I32),
             )
+        tab_tiles.append(load_table_pass(1))
+        w2_codes = alloc([P, PASSES, 2 * H], U8, "w2_codes", "picked_plane")
+        nc.sync.dma_start(w2_codes[:].bitcast(I32), w2_words.rearrange("a p c -> p a c").bitcast(I32))
 
         w2_plane = zeroed_plane(PASSES * H, "w2_plane")
         for q in range(4):
@@ -101,9 +103,6 @@ def tile_list_pass_arbitration_scores_kernel(
                 w2_plane[32 * q : 32 * q + 4, :].rearrange("p (a c) -> p a c", a=PASSES).bitcast(I32),
                 w2_scales[:, 4 * q : 4 * q + 4, :].rearrange("a r c -> r a c").bitcast(I32),
             )
-        wgs_sb = load(wgs, [P, S], "wgs_sb", "weights")
-        idx3 = load_list(offs3, "idx3")
-        idx4 = load_list(offs4, "idx4")
 
         v_words = {}
         for a in range(PASSES):
@@ -111,6 +110,8 @@ def tile_list_pass_arbitration_scores_kernel(
                 picked = alloc([P, BANK], U32, "v_words_%d_%d" % (a, h))
                 nc.vector.tensor_copy(picked[:], tab_tiles[a][:].indirect(idx[:, HALF_COLS * h : HALF_COLS * (h + 1)]))
                 v_words[(a, h)] = picked
+
+        wgs_sb = load(wgs, [P, S], "wgs_sb", "wide0")
 
         squares = []
         for b in range(ROW_BLOCKS):
@@ -148,7 +149,6 @@ def tile_list_pass_arbitration_scores_kernel(
                         start=(a == 0),
                         stop=(a == PASSES - 1),
                     )
-                for a in range(PASSES):
                     nc.tensor.matmul_mx(
                         out=b_ps[:],
                         lhsT=w2_codes[:, a, 2 * P * b : 2 * P * (b + 1)].bitcast(FP4X4),
@@ -165,14 +165,8 @@ def tile_list_pass_arbitration_scores_kernel(
 
         board_tags = ("w1_raw_0", "w1_raw_1", "v_words_0_1", "v_words_1_1")
         boards = [load(board[P * b : P * (b + 1), :], [P, T], "board_%d" % b, board_tags[b]) for b in range(ROW_BLOCKS)]
-        w3_codes = alloc([P, N], U32, "w3_codes", "v_words_0_0")
+        w3_codes = alloc([P, N], U32, "w3_codes", "v_words_1_0")
         nc.sync.dma_start(w3_codes[:].bitcast(I32), w3_words[0].rearrange("p c i -> p (c i)").bitcast(I32))
-        w3_plane = alloc([P, N], U8, "w3_plane", "v_words_1_0")
-        nc.gpsimd.memset(w3_plane[:].bitcast(I32), 0)
-        for q in range(4):
-            nc.sync.dma_start(
-                w3_plane[32 * q : 32 * q + 4, :].bitcast(I32), w3_scales[0, 4 * q : 4 * q + 4, :].bitcast(I32)
-            )
 
         page_tags = ("page_0", "a_sq_0_0", "a_sq_0_1", "a_sq_1_0")
         z_turned = [alloc([P, 4, 2, P, 2], BF16, "z_turned_%d" % c) for c in range(CHUNKS)]
@@ -190,7 +184,7 @@ def tile_list_pass_arbitration_scores_kernel(
                 nc.vector.tensor_tensor(
                     page[:].indirect(idx2[:, width // 16 * h : width // 16 * (h + 1)]), contest[:], wgs_sb[:, cols], ALU.mult
                 )
-            sums = [bank(c, "z_ps") for c in range(CHUNKS)]
+            sums = [bank(4 * (b % 2) + c, "z_ps") for c in range(CHUNKS)]
             for c in range(CHUNKS):
                 for s in range(4):
                     slots = slice(BANK * c + P * s, BANK * c + P * (s + 1))
@@ -210,6 +204,31 @@ def tile_list_pass_arbitration_scores_kernel(
                     sums[c][:].rearrange("p (s i u e) -> p s u i e", s=4, u=2, e=2),
                 )
 
+        w3_plane = alloc([P, N], U8, "w3_plane", "b_sq_3_0")
+        nc.gpsimd.memset(w3_plane[:].bitcast(I32), 0)
+        for q in range(4):
+            nc.sync.dma_start(
+                w3_plane[32 * q : 32 * q + 4, :].bitcast(I32), w3_scales[0, 4 * q : 4 * q + 4, :].bitcast(I32)
+            )
+
+        rows = []
+        for n in range(OUT_BLOCKS):
+            row = alloc([P, T], F32, "rows_%d" % n, ("b_sq_1_0", "a_sq_2_0", "a_sq_3_0")[n])
+            nc.gpsimd.memset(row[:], 0.0)
+            rows.append(row)
+
+        warm_ps = bank(0, "warm_ps")
+        for i in range(4):
+            nc.tensor.matmul_mx(
+                out=warm_ps[:],
+                lhsT=w3_codes[:, 0:P].bitcast(FP8X4),
+                lhsT_scale=w3_plane[:, 0:P],
+                rhs=v_words[(0, 0)][:].bitcast(FP8X4),
+                rhs_scale=v_plane[:, 0:BANK],
+                start=True,
+                stop=True,
+            )
+
         wgo_sb = load(wgo, [P, S], "wgo_sb", "b_sq_0_0")
         prios = [
             load(prio[P * n : P * (n + 1), :], [P, S], "prio_%d" % n, ("b_sq_0_1", "late1", "late2")[n])
@@ -217,7 +236,7 @@ def tile_list_pass_arbitration_scores_kernel(
         ]
 
         z_codes, z_planes = [], []
-        scores = [alloc([P, T], F32, "scores_0", "wide0")]
+        scores = [alloc([P, T], F32, "scores_0")]
 
         def score(n, c, index):
             y_ps = bank(index, "y_ps")
@@ -236,7 +255,7 @@ def tile_list_pass_arbitration_scores_kernel(
             z_grouped = alloc([P, BANK, 4], BF16, "z_grouped_%d" % c, "z_grouped_%d" % (c % 2))
             z_pairs = z_turned[c][:].rearrange("p s u r e -> p (s u r e)").bitcast(F32)
             for half in range(2):
-                back = bank(4 + 2 * (c % 2) + half, "back_ps")
+                back = bank(2 * (c % 2) + half, "back_ps")
                 for i in range(4):
                     nc.tensor.transpose(
                         back[:, P * i : P * (i + 1)], z_pairs[:, BANK * half + P * i : BANK * half + P * (i + 1)], ident[:]
@@ -255,27 +274,21 @@ def tile_list_pass_arbitration_scores_kernel(
             )
             z_codes.append(codes)
             z_planes.append(plane)
-            score(0, c, c)
+            score(0, c, 4 + c)
 
-        gains = alloc([P, OUT_BLOCKS, S], F32, "gains", "weights")
+        gains = alloc([P, OUT_BLOCKS, S], F32, "gains", "wide0")
         for n in range(OUT_BLOCKS):
             nc.vector.tensor_tensor(gains[:, n, :], prios[n][:], wgo_sb[:], ALU.mult)
         scores.append(alloc([P, T], F32, "scores_1", "z_grouped_1"))
         scores.append(alloc([P, T], F32, "scores_2", "wide1"))
         for n in range(1, OUT_BLOCKS):
             for c in range(CHUNKS):
-                score(n, c, c)
-
-        rows = []
-        for n in range(OUT_BLOCKS):
-            row = alloc([P, T], F32, "rows_%d" % n, ("b_sq_1_0", "a_sq_2_0", "b_sq_2_0")[n])
-            nc.gpsimd.memset(row[:], 0.0)
-            rows.append(row)
+                score(n, c, 4 + c)
 
         gates = []
 
         def pick(n):
-            gate = alloc([P, S], F32, "gate_%d" % n, ("a_sq_3_0", "b_sq_3_0")[n % 2])
+            gate = alloc([P, S], F32, "gate_%d" % n, ("late3", "late4")[n % 2])
             nc.vector.tensor_copy(gate[:], scores[n][:].indirect(idx3[:]))
             gates.append(gate)
 

@@ -63,22 +63,26 @@ def tile_list_pass_arbitration_scores_kernel(
             nc.sync.dma_start(words[:].bitcast(I32), tab_words[a].rearrange("p t i -> p (t i)").bitcast(I32))
             return words
 
-        def load_w1(first, last):
+        def load_w1(dst, first, last):
             raws = []
             for a in range(PASSES):
                 rows = w1[512 * a : 512 * (a + 1), first:last].rearrange("(p j) c -> p j c", j=4)
-                raws.append(load(rows, [P, 4, last - first], "w1_raw_%d_%d" % (first, a), "w1_raw_%d" % a))
+                size = 4 * (last - first)
+                raw = dst[:, size * a : size * (a + 1)].rearrange("p (j c) -> p j c", j=4)
+                nc.sync.dma_start(raw, rows)
+                raws.append(raw)
             return raws
 
         idx = load_list(offs, "idx")
         tab_plane = alloc([P, T], U8, "tab_plane", "wide1")
         nc.sync.dma_start(tab_plane[96:P, :].bitcast(I32), tab_scales.rearrange("a q c -> q a c").bitcast(I32))
         nc.vector.memset(tab_plane[0:96, :].bitcast(I32), 0)
+        w1_first = alloc([P, PASSES * 4 * P], F32, "w1_first")
+        w1_raw = load_w1(w1_first, 0, P)
         idx2 = load_list(offs2, "idx2")
-        idx3 = load_list(offs3, "idx3")
         tab_tiles = [load_table_pass(0)]
+        idx3 = load_list(offs3, "idx3")
         idx4 = load_list(offs4, "idx4")
-        w1_raw = load_w1(0, P)
 
         ident = alloc([P, P], F32, "ident")
         make_identity(nc, ident[:])
@@ -111,12 +115,14 @@ def tile_list_pass_arbitration_scores_kernel(
                 nc.vector.tensor_copy(picked[:], tab_tiles[a][:].indirect(idx[:, HALF_COLS * h : HALF_COLS * (h + 1)]))
                 v_words[(a, h)] = picked
 
-        wgs_sb = load(wgs, [P, S], "wgs_sb", "wide0")
+        second = alloc([P, S + PASSES * 4 * (H - P)], F32, "second", "wide0")
+        wgs_sb = second[:, 0:S]
+        nc.sync.dma_start(wgs_sb, wgs)
 
         squares = []
         for b in range(ROW_BLOCKS):
             if b == 1:
-                w1_raw = load_w1(P, H)
+                w1_raw = load_w1(second[:, S:], P, H)
             first = P * max(b - 1, 0)
             width = S // PIECES[b]
             squares.append(
@@ -163,10 +169,13 @@ def tile_list_pass_arbitration_scores_kernel(
                 nc.scalar.activation(a_sq[:, start : start + BANK], a_ps[:], ACT.Square)
                 nc.scalar.activation(b_sq[:, start : start + BANK], b_ps[:], ACT.Square)
 
-        board_tags = ("w1_raw_0", "w1_raw_1", "v_words_0_1", "v_words_1_1")
-        boards = [load(board[P * b : P * (b + 1), :], [P, T], "board_%d" % b, board_tags[b]) for b in range(ROW_BLOCKS)]
-        w3_codes = alloc([P, N], U32, "w3_codes", "v_words_1_0")
-        nc.sync.dma_start(w3_codes[:].bitcast(I32), w3_words[0].rearrange("p c i -> p (c i)").bitcast(I32))
+        board_tags = ("late3", "b_sq_0_1", "v_words_0_1", "v_words_1_1")
+        w3_plane = alloc([P, N], U8, "w3_plane", "v_words_1_0")
+        nc.gpsimd.memset(w3_plane[:].bitcast(I32), 0)
+        for q in range(4):
+            nc.sync.dma_start(
+                w3_plane[32 * q : 32 * q + 4, :].bitcast(I32), w3_scales[0, 4 * q : 4 * q + 4, :].bitcast(I32)
+            )
 
         page_tags = ("page_0", "a_sq_0_0", "a_sq_0_1", "a_sq_1_0")
         z_turned = [alloc([P, 4, 2, P, 2], BF16, "z_turned_%d" % c) for c in range(CHUNKS)]
@@ -177,19 +186,34 @@ def tile_list_pass_arbitration_scores_kernel(
             width = S // pieces
             for h in range(pieces):
                 a_sq, b_sq = squares[b][h]
-                tag = "late%d" % (b + 1) if h == pieces - 1 else "contest_first"
+                tag = "late%d" % (b + 1) if h == pieces - 1 and b < 2 else "contest_%d" % b
                 contest = alloc([P, width], F32, "contest_%d_%d" % (b, h), tag)
                 cols = slice(width * h, width * (h + 1))
                 nc.vector.tensor_tensor(contest[:], a_sq[:], b_sq[:], ALU.subtract)
                 nc.vector.tensor_tensor(
                     page[:].indirect(idx2[:, width // 16 * h : width // 16 * (h + 1)]), contest[:], wgs_sb[:, cols], ALU.mult
                 )
+            board_sb = load(board[P * b : P * (b + 1), :], [P, T], "board_%d" % b, board_tags[b])
+            if b == ROW_BLOCKS - 1:
+                w3_codes = alloc([P, N], U32, "w3_codes", "contest_2")
+                nc.sync.dma_start(w3_codes[:].bitcast(I32), w3_words[0].rearrange("p c i -> p (c i)").bitcast(I32))
+                for c in range(CHUNKS):
+                    warm_ps = bank(4 + c, "warm_ps")
+                    nc.tensor.matmul_mx(
+                        out=warm_ps[:],
+                        lhsT=w3_codes[:, 0:P].bitcast(FP8X4),
+                        lhsT_scale=w3_plane[:, 0:P],
+                        rhs=v_words[(0, 0)][:].bitcast(FP8X4),
+                        rhs_scale=v_plane[:, 0:BANK],
+                        start=True,
+                        stop=True,
+                    )
             sums = [bank(4 * (b % 2) + c, "z_ps") for c in range(CHUNKS)]
             for c in range(CHUNKS):
                 for s in range(4):
                     slots = slice(BANK * c + P * s, BANK * c + P * (s + 1))
                     nc.tensor.matmul(
-                        sums[c][:, P * s : P * (s + 1)], boards[b][:, slots], ident[:],
+                        sums[c][:, P * s : P * (s + 1)], board_sb[:, slots], ident[:],
                         start=(s == 0), stop=False, is_transpose=True,
                     )
             for c in range(CHUNKS):
@@ -204,34 +228,15 @@ def tile_list_pass_arbitration_scores_kernel(
                     sums[c][:].rearrange("p (s i u e) -> p s u i e", s=4, u=2, e=2),
                 )
 
-        w3_plane = alloc([P, N], U8, "w3_plane", "b_sq_3_0")
-        nc.gpsimd.memset(w3_plane[:].bitcast(I32), 0)
-        for q in range(4):
-            nc.sync.dma_start(
-                w3_plane[32 * q : 32 * q + 4, :].bitcast(I32), w3_scales[0, 4 * q : 4 * q + 4, :].bitcast(I32)
-            )
-
         rows = []
         for n in range(OUT_BLOCKS):
             row = alloc([P, T], F32, "rows_%d" % n, ("b_sq_1_0", "a_sq_2_0", "a_sq_3_0")[n])
             nc.gpsimd.memset(row[:], 0.0)
             rows.append(row)
 
-        warm_ps = bank(0, "warm_ps")
-        for i in range(4):
-            nc.tensor.matmul_mx(
-                out=warm_ps[:],
-                lhsT=w3_codes[:, 0:P].bitcast(FP8X4),
-                lhsT_scale=w3_plane[:, 0:P],
-                rhs=v_words[(0, 0)][:].bitcast(FP8X4),
-                rhs_scale=v_plane[:, 0:BANK],
-                start=True,
-                stop=True,
-            )
-
         wgo_sb = load(wgo, [P, S], "wgo_sb", "b_sq_0_0")
         prios = [
-            load(prio[P * n : P * (n + 1), :], [P, S], "prio_%d" % n, ("b_sq_0_1", "late1", "late2")[n])
+            load(prio[P * n : P * (n + 1), :], [P, S], "prio_%d" % n, ("contest_0", "late1", "late2")[n])
             for n in range(OUT_BLOCKS)
         ]
 
@@ -288,7 +293,7 @@ def tile_list_pass_arbitration_scores_kernel(
         gates = []
 
         def pick(n):
-            gate = alloc([P, S], F32, "gate_%d" % n, ("late3", "late4")[n % 2])
+            gate = alloc([P, S], F32, "gate_%d" % n, ("b_sq_3_0", "contest_3")[n % 2])
             nc.vector.tensor_copy(gate[:], scores[n][:].indirect(idx3[:]))
             gates.append(gate)
 

@@ -74,15 +74,24 @@ def tile_list_pass_arbitration_scores_kernel(
             return raws
 
         idx = load_list(offs, "idx")
-        tab_plane = alloc([P, T], U8, "tab_plane", "wide1")
+        tab_plane = alloc([P, T], U8, "tab_plane")
         nc.sync.dma_start(tab_plane[96:P, :].bitcast(I32), tab_scales.rearrange("a q c -> q a c").bitcast(I32))
         nc.vector.memset(tab_plane[0:96, :].bitcast(I32), 0)
         w1_first = alloc([P, PASSES * 4 * P], F32, "w1_first")
         w1_raw = load_w1(w1_first, 0, P)
         idx2 = load_list(offs2, "idx2")
-        tab_tiles = [load_table_pass(0)]
         idx3 = load_list(offs3, "idx3")
         idx4 = load_list(offs4, "idx4")
+        tab_tiles = [load_table_pass(0)]
+        w2_plane = zeroed_plane(PASSES * H, "w2_plane")
+        for q in range(4):
+            nc.sync.dma_start(
+                w2_plane[32 * q : 32 * q + 4, :].rearrange("p (a c) -> p a c", a=PASSES).bitcast(I32),
+                w2_scales[:, 4 * q : 4 * q + 4, :].rearrange("a r c -> r a c").bitcast(I32),
+            )
+        tab_tiles.append(load_table_pass(1))
+        w2_codes = alloc([P, PASSES, 2 * H], U8, "w2_codes")
+        nc.sync.dma_start(w2_codes[:].bitcast(I32), w2_words.rearrange("a p c -> p a c").bitcast(I32))
 
         ident = alloc([P, P], F32, "ident")
         make_identity(nc, ident[:])
@@ -96,16 +105,6 @@ def tile_list_pass_arbitration_scores_kernel(
             nc.sync.dma_start(
                 v_plane[32 * q : 32 * q + 4, :].bitcast(I32),
                 picked_plane[96 + 8 * q : 96 + 8 * (q + 1), :].bitcast(I32),
-            )
-        tab_tiles.append(load_table_pass(1))
-        w2_codes = alloc([P, PASSES, 2 * H], U8, "w2_codes", "picked_plane")
-        nc.sync.dma_start(w2_codes[:].bitcast(I32), w2_words.rearrange("a p c -> p a c").bitcast(I32))
-
-        w2_plane = zeroed_plane(PASSES * H, "w2_plane")
-        for q in range(4):
-            nc.gpsimd.dma_start(
-                w2_plane[32 * q : 32 * q + 4, :].rearrange("p (a c) -> p a c", a=PASSES).bitcast(I32),
-                w2_scales[:, 4 * q : 4 * q + 4, :].rearrange("a r c -> r a c").bitcast(I32),
             )
 
         v_words = {}
@@ -143,8 +142,9 @@ def tile_list_pass_arbitration_scores_kernel(
                 out=w1_codes[:].bitcast(FP8X4), scales=w1_plane[:], in_=grouped[:].rearrange("p a c j -> p (a c j)")
             )
             for h in range(HALVES):
-                a_ps = bank(4 + 2 * h, "a_ps")
-                b_ps = bank(5 + 2 * h, "b_ps")
+                base = 0 if b == 2 else 4
+                a_ps = bank(base + 2 * h, "a_ps")
+                b_ps = bank(base + 2 * h + 1, "b_ps")
                 for a in range(PASSES):
                     nc.tensor.matmul_mx(
                         out=a_ps[:],
@@ -171,17 +171,19 @@ def tile_list_pass_arbitration_scores_kernel(
 
         board_tags = ("late3", "b_sq_0_1", "v_words_0_1", "v_words_1_1")
         w3_plane = alloc([P, N], U8, "w3_plane", "v_words_1_0")
-        nc.gpsimd.memset(w3_plane[:].bitcast(I32), 0)
+        nc.vector.memset(w3_plane[:].bitcast(I32), 0)
         for q in range(4):
             nc.sync.dma_start(
                 w3_plane[32 * q : 32 * q + 4, :].bitcast(I32), w3_scales[0, 4 * q : 4 * q + 4, :].bitcast(I32)
             )
 
-        page_tags = ("page_0", "a_sq_0_0", "a_sq_0_1", "a_sq_1_0")
+        pages = [alloc([P, T], F32, "page_0"), alloc([P, T], F32, "page_1", "wide1")]
+        nc.vector.memset(pages[0][:], 0.0)
         z_turned = [alloc([P, 4, 2, P, 2], BF16, "z_turned_%d" % c) for c in range(CHUNKS)]
         for b in range(ROW_BLOCKS):
-            page = alloc([P, T], F32, "page_%d" % b, page_tags[b])
-            (nc.vector if b == 0 else nc.gpsimd).memset(page[:], 0.0)
+            page = pages[b % 2]
+            if b == 1:
+                nc.vector.memset(page[:], 0.0)
             pieces = PIECES[b]
             width = S // pieces
             for h in range(pieces):
@@ -209,30 +211,25 @@ def tile_list_pass_arbitration_scores_kernel(
                         stop=True,
                     )
             sums = [bank(4 * (b % 2) + c, "z_ps") for c in range(CHUNKS)]
+            early, late = (board_sb, page) if b == ROW_BLOCKS - 1 else (page, board_sb)
             for c in range(CHUNKS):
                 for s in range(4):
                     slots = slice(BANK * c + P * s, BANK * c + P * (s + 1))
                     nc.tensor.matmul(
-                        sums[c][:, P * s : P * (s + 1)], board_sb[:, slots], ident[:],
+                        sums[c][:, P * s : P * (s + 1)], early[:, slots], ident[:],
                         start=(s == 0), stop=False, is_transpose=True,
                     )
             for c in range(CHUNKS):
                 for s in range(4):
                     slots = slice(BANK * c + P * s, BANK * c + P * (s + 1))
                     nc.tensor.matmul(
-                        sums[c][:, P * s : P * (s + 1)], page[:, slots], ident[:],
+                        sums[c][:, P * s : P * (s + 1)], late[:, slots], ident[:],
                         start=False, stop=(s == 3), is_transpose=True,
                     )
                 nc.scalar.copy(
                     z_turned[c][:, :, :, 32 * b : 32 * (b + 1), :],
                     sums[c][:].rearrange("p (s i u e) -> p s u i e", s=4, u=2, e=2),
                 )
-
-        rows = []
-        for n in range(OUT_BLOCKS):
-            row = alloc([P, T], F32, "rows_%d" % n, ("b_sq_1_0", "a_sq_2_0", "a_sq_3_0")[n])
-            nc.gpsimd.memset(row[:], 0.0)
-            rows.append(row)
 
         wgo_sb = load(wgo, [P, S], "wgo_sb", "b_sq_0_0")
         prios = [
@@ -257,7 +254,7 @@ def tile_list_pass_arbitration_scores_kernel(
             nc.scalar.activation(scores[n][:, BANK * c : BANK * (c + 1)], y_ps[:], ACT.Sigmoid)
 
         for c in range(CHUNKS):
-            z_grouped = alloc([P, BANK, 4], BF16, "z_grouped_%d" % c, "z_grouped_%d" % (c % 2))
+            z_grouped = alloc([P, BANK, 4], BF16, "z_grouped_%d" % c)
             z_pairs = z_turned[c][:].rearrange("p s u r e -> p (s u r e)").bitcast(F32)
             for half in range(2):
                 back = bank(2 * (c % 2) + half, "back_ps")
@@ -268,7 +265,7 @@ def tile_list_pass_arbitration_scores_kernel(
                 dst = z_grouped[:, 256 * half : 256 * (half + 1), :].rearrange("p c j -> p (c j)").bitcast(F32)
                 dst = dst.rearrange("p (s c u) -> p s c u", s=2, u=2)
                 src = back[:].rearrange("p (s u c) -> p s c u", s=2, u=2)
-                if half == 0:
+                if half == 0 or c in (1, 2):
                     nc.scalar.copy(dst, src)
                 else:
                     nc.vector.tensor_copy(dst, src)
@@ -281,19 +278,24 @@ def tile_list_pass_arbitration_scores_kernel(
             z_planes.append(plane)
             score(0, c, 4 + c)
 
-        gains = alloc([P, OUT_BLOCKS, S], F32, "gains", "wide0")
+        gains_first = alloc([P, 2 * S], F32, "gains_first", "wide0")
+        gains_last = alloc([P, S], F32, "gains_last", "z_grouped_1")
+        gains = [gains_first[:, 0:S], gains_first[:, S : 2 * S], gains_last[:]]
+        rows = [alloc([P, T], F32, "rows_0", "contest_3"), alloc([P, T], F32, "rows_1", "z_grouped_3")]
         for n in range(OUT_BLOCKS):
-            nc.vector.tensor_tensor(gains[:, n, :], prios[n][:], wgo_sb[:], ALU.mult)
-        scores.append(alloc([P, T], F32, "scores_1", "z_grouped_1"))
-        scores.append(alloc([P, T], F32, "scores_2", "wide1"))
+            nc.vector.tensor_tensor(gains[n], prios[n][:], wgo_sb[:], ALU.mult)
+            if n < 2:
+                nc.vector.memset(rows[n][:], 0.0)
+        scores.append(alloc([P, T], F32, "scores_1", "a_sq_0_0"))
+        scores.append(alloc([P, T], F32, "scores_2", "page_0"))
         for n in range(1, OUT_BLOCKS):
             for c in range(CHUNKS):
-                score(n, c, 4 + c)
+                score(n, c, (2, 3, 7, 6)[c])
 
         gates = []
 
         def pick(n):
-            gate = alloc([P, S], F32, "gate_%d" % n, ("b_sq_3_0", "contest_3")[n % 2])
+            gate = alloc([P, S], F32, "gate_%d" % n, ("b_sq_3_0", "a_sq_3_0")[n % 2])
             nc.vector.tensor_copy(gate[:], scores[n][:].indirect(idx3[:]))
             gates.append(gate)
 
@@ -301,5 +303,5 @@ def tile_list_pass_arbitration_scores_kernel(
         for n in range(OUT_BLOCKS):
             if n + 1 < OUT_BLOCKS:
                 pick(n + 1)
-            nc.vector.tensor_tensor(rows[n][:].indirect(idx4[:]), gates[n][:], gains[:, n, :], ALU.mult)
-            nc.sync.dma_start(out[P * n : P * (n + 1), :], rows[n][:])
+            nc.vector.tensor_tensor(rows[n % 2][:].indirect(idx4[:]), gates[n][:], gains[n], ALU.mult)
+            nc.sync.dma_start(out[P * n : P * (n + 1), :], rows[n % 2][:])

@@ -18,13 +18,20 @@ ACT = mybir.ActivationFunctionType
 ALU = mybir.AluOpType
 
 P = 128
+PACK = 4
+K_PASS = P * PACK
+PASSES = K // K_PASS
+QUADRANT = 32
+QUADRANTS = P // QUADRANT
+GROUP = 16
 BANK = 512
-PASSES = K // 512
 ROW_BLOCKS = H // P
 OUT_BLOCKS = N // P
 HALVES = S // BANK
 CHUNKS = T // BANK
-HALF_COLS = BANK // 16
+TILES = BANK // P
+SCALE_ROW0 = P - PASSES * K_PASS // 32
+LOW, HIGH = 0, 4
 PIECES = (2, 1, 1, 1)
 
 
@@ -34,22 +41,24 @@ def tile_list_pass_arbitration_scores_kernel(
 ):
     nc = tc.nc
     with ExitStack() as ctx:
-        sb = ctx.enter_context(tc.tile_pool(name="sb", bufs=1))
-        ps = ctx.enter_context(tc.psum_pool(name="ps", bufs=1))
+        sbuf = ctx.enter_context(tc.tile_pool(name="sbuf", bufs=1))
+        psum = ctx.enter_context(tc.psum_pool(name="psum", bufs=1))
+        place = {}
 
-        def alloc(shape, dtype, name, tag=None):
-            return sb.tile(shape, dtype, name=name, tag=tag or name, align_bytes=64)
+        def alloc(shape, dtype, name, after=None):
+            place[name] = place[after] if after else name
+            return sbuf.tile(shape, dtype, name=name, tag=place[name], align_bytes=64)
 
         def bank(index, name):
-            return ps.tile([P, BANK], F32, name=name, tag="bank%d" % index)
+            return psum.tile([P, BANK], F32, name=name, tag="bank%d" % index)
 
         def load_list(src, name):
-            dst = alloc([P, S // 16], U16, name)
+            dst = alloc([P, S // GROUP], U16, name)
             nc.sync.dma_start(dst[:], src)
             return dst
 
-        def load(src, shape, name, tag=None):
-            dst = alloc(shape, F32, name, tag)
+        def load(src, shape, name, after):
+            dst = alloc(shape, F32, name, after)
             nc.sync.dma_start(dst[:], src)
             return dst
 
@@ -58,36 +67,41 @@ def tile_list_pass_arbitration_scores_kernel(
             nc.vector.memset(plane[:].bitcast(I32), 0)
             return plane
 
+        def live_rows(plane, q):
+            return plane[QUADRANT * q : QUADRANT * q + PACK, :]
+
         def load_table_pass(a):
-            words = alloc([P, T], U32, "tab_words_%d" % a, "wide%d" % a)
+            words = alloc([P, T], U32, "tab_words_%d" % a)
             nc.sync.dma_start(words[:].bitcast(I32), tab_words[a].rearrange("p t i -> p (t i)").bitcast(I32))
             return words
 
         def load_w1(dst, first, last):
-            raws = []
+            views = []
             for a in range(PASSES):
-                rows = w1[512 * a : 512 * (a + 1), first:last].rearrange("(p j) c -> p j c", j=4)
-                size = 4 * (last - first)
-                raw = dst[:, size * a : size * (a + 1)].rearrange("p (j c) -> p j c", j=4)
-                nc.sync.dma_start(raw, rows)
-                raws.append(raw)
-            return raws
+                src = w1[K_PASS * a : K_PASS * (a + 1), first:last].rearrange("(p j) c -> p j c", j=PACK)
+                size = PACK * (last - first)
+                view = dst[:, size * a : size * (a + 1)].rearrange("p (j c) -> p j c", j=PACK)
+                nc.sync.dma_start(view, src)
+                views.append(view)
+            return views
 
         idx = load_list(offs, "idx")
         tab_plane = alloc([P, T], U8, "tab_plane")
-        nc.sync.dma_start(tab_plane[96:P, :].bitcast(I32), tab_scales.rearrange("a q c -> q a c").bitcast(I32))
-        nc.vector.memset(tab_plane[0:96, :].bitcast(I32), 0)
-        w1_first = alloc([P, PASSES * 4 * P], F32, "w1_first")
-        w1_raw = load_w1(w1_first, 0, P)
+        nc.sync.dma_start(
+            tab_plane[SCALE_ROW0:P, :].bitcast(I32), tab_scales.rearrange("a q c -> q a c").bitcast(I32)
+        )
+        nc.vector.memset(tab_plane[0:SCALE_ROW0, :].bitcast(I32), 0)
+        w1_first = alloc([P, PASSES * PACK * P], F32, "w1_first")
+        w1_views = load_w1(w1_first, 0, P)
         idx2 = load_list(offs2, "idx2")
         idx3 = load_list(offs3, "idx3")
         idx4 = load_list(offs4, "idx4")
         tab_tiles = [load_table_pass(0)]
         w2_plane = zeroed_plane(PASSES * H, "w2_plane")
-        for q in range(4):
+        for q in range(QUADRANTS):
             nc.sync.dma_start(
-                w2_plane[32 * q : 32 * q + 4, :].rearrange("p (a c) -> p a c", a=PASSES).bitcast(I32),
-                w2_scales[:, 4 * q : 4 * q + 4, :].rearrange("a r c -> r a c").bitcast(I32),
+                live_rows(w2_plane, q).rearrange("p (a c) -> p a c", a=PASSES).bitcast(I32),
+                w2_scales[:, PACK * q : PACK * (q + 1), :].rearrange("a r c -> r a c").bitcast(I32),
             )
         tab_tiles.append(load_table_pass(1))
         w2_codes = alloc([P, PASSES, 2 * H], U8, "w2_codes")
@@ -95,34 +109,40 @@ def tile_list_pass_arbitration_scores_kernel(
 
         ident = alloc([P, P], F32, "ident")
         make_identity(nc, ident[:])
-        warm = alloc([P, 1], F32, "warm")
-        nc.scalar.activation(warm[:], ident[:, 0:1], ACT.Sigmoid)
+        table_warmup = alloc([P, 1], F32, "table_warmup")
+        nc.scalar.activation(table_warmup[:], ident[:, 0:1], ACT.Sigmoid)
 
         v_plane = zeroed_plane(PASSES * S, "v_plane")
-        picked_plane = alloc([P, S], U8, "picked_plane")
-        nc.vector.tensor_copy(picked_plane[:], tab_plane[:].indirect(idx[:]))
-        for q in range(4):
+        picked_scales = alloc([P, S], U8, "picked_scales")
+        nc.vector.tensor_copy(picked_scales[:], tab_plane[:].indirect(idx[:]))
+        quadrant_rows = PASSES * PACK
+        for q in range(QUADRANTS):
             nc.sync.dma_start(
-                v_plane[32 * q : 32 * q + 4, :].bitcast(I32),
-                picked_plane[96 + 8 * q : 96 + 8 * (q + 1), :].bitcast(I32),
+                live_rows(v_plane, q).bitcast(I32),
+                picked_scales[SCALE_ROW0 + quadrant_rows * q : SCALE_ROW0 + quadrant_rows * (q + 1), :].bitcast(I32),
             )
 
         v_words = {}
+        half_columns = BANK // GROUP
         for a in range(PASSES):
             for h in range(HALVES):
                 picked = alloc([P, BANK], U32, "v_words_%d_%d" % (a, h))
-                nc.vector.tensor_copy(picked[:], tab_tiles[a][:].indirect(idx[:, HALF_COLS * h : HALF_COLS * (h + 1)]))
+                entries = idx[:, half_columns * h : half_columns * (h + 1)]
+                nc.vector.tensor_copy(picked[:], tab_tiles[a][:].indirect(entries))
                 v_words[(a, h)] = picked
 
-        second = alloc([P, S + PASSES * 4 * (H - P)], F32, "second", "wide0")
-        wgs_sb = second[:, 0:S]
+        second_loads = alloc([P, S + PASSES * PACK * (H - P)], F32, "second_loads", "tab_words_0")
+        wgs_sb = second_loads[:, 0:S]
         nc.sync.dma_start(wgs_sb, wgs)
+        w1_block = PASSES * PACK * P
 
         squares = []
         for b in range(ROW_BLOCKS):
             if b == 1:
-                w1_raw = load_w1(second[:, S:], P, H)
-            first = P * max(b - 1, 0)
+                w1_views = load_w1(second_loads[:, S : S + w1_block], P, 2 * P)
+            if b == 2:
+                w1_views = load_w1(second_loads[:, S + w1_block :], 2 * P, H)
+            column0 = P * max(b - 2, 0)
             width = S // PIECES[b]
             squares.append(
                 [
@@ -130,24 +150,25 @@ def tile_list_pass_arbitration_scores_kernel(
                     for i in range(PIECES[b])
                 ]
             )
-            grouped = alloc([P, PASSES, P, 4], BF16, "w1_grouped_%d" % b, "late%d" % b)
+            w1_grouped = alloc([P, PASSES, P, PACK], BF16, "w1_grouped_%d" % b)
             for a in range(PASSES):
                 nc.scalar.copy(
-                    grouped[:, a, :, :].rearrange("p (c i) j -> p c j i", i=4),
-                    w1_raw[a][:, :, first : first + P].rearrange("p j (c i) -> p c j i", i=4),
+                    w1_grouped[:, a, :, :].rearrange("p (c i) j -> p c j i", i=4),
+                    w1_views[a][:, :, column0 : column0 + P].rearrange("p j (c i) -> p c j i", i=4),
                 )
             w1_codes = alloc([P, PASSES * P], U32, "w1_codes_%d" % b)
             w1_plane = alloc([P, PASSES * P], U8, "w1_plane_%d" % b)
             nc.vector.quantize_mx(
-                out=w1_codes[:].bitcast(FP8X4), scales=w1_plane[:], in_=grouped[:].rearrange("p a c j -> p (a c j)")
+                out=w1_codes[:].bitcast(FP8X4),
+                scales=w1_plane[:],
+                in_=w1_grouped[:].rearrange("p a c j -> p (a c j)"),
             )
             for h in range(HALVES):
-                base = 0 if b == 2 else 4
-                a_ps = bank(base + 2 * h, "a_ps")
-                b_ps = bank(base + 2 * h + 1, "b_ps")
+                a_bank = bank(HIGH + 2 * h, "a_bank")
+                b_bank = bank(HIGH + 2 * h + 1, "b_bank")
                 for a in range(PASSES):
                     nc.tensor.matmul_mx(
-                        out=a_ps[:],
+                        out=a_bank[:],
                         lhsT=w1_codes[:, P * a : P * (a + 1)].bitcast(FP8X4),
                         lhsT_scale=w1_plane[:, P * a : P * (a + 1)],
                         rhs=v_words[(a, h)][:].bitcast(FP8X4),
@@ -156,7 +177,7 @@ def tile_list_pass_arbitration_scores_kernel(
                         stop=(a == PASSES - 1),
                     )
                     nc.tensor.matmul_mx(
-                        out=b_ps[:],
+                        out=b_bank[:],
                         lhsT=w2_codes[:, a, 2 * P * b : 2 * P * (b + 1)].bitcast(FP4X4),
                         lhsT_scale=w2_plane[:, H * a + P * b : H * a + P * (b + 1)],
                         rhs=v_words[(a, h)][:].bitcast(FP8X4),
@@ -164,45 +185,43 @@ def tile_list_pass_arbitration_scores_kernel(
                         start=(a == 0),
                         stop=(a == PASSES - 1),
                     )
-                piece, start = divmod(BANK * h, width)
+                piece, offset = divmod(BANK * h, width)
                 a_sq, b_sq = squares[b][piece]
-                nc.scalar.activation(a_sq[:, start : start + BANK], a_ps[:], ACT.Square)
-                nc.scalar.activation(b_sq[:, start : start + BANK], b_ps[:], ACT.Square)
+                nc.scalar.activation(a_sq[:, offset : offset + BANK], a_bank[:], ACT.Square)
+                nc.scalar.activation(b_sq[:, offset : offset + BANK], b_bank[:], ACT.Square)
 
-        board_tags = ("late3", "b_sq_0_1", "v_words_0_1", "v_words_1_1")
         w3_plane = alloc([P, N], U8, "w3_plane", "v_words_1_0")
-        nc.vector.memset(w3_plane[:].bitcast(I32), 0)
-        for q in range(4):
+        nc.gpsimd.memset(w3_plane[:].bitcast(I32), 0)
+        for q in range(QUADRANTS):
             nc.sync.dma_start(
-                w3_plane[32 * q : 32 * q + 4, :].bitcast(I32), w3_scales[0, 4 * q : 4 * q + 4, :].bitcast(I32)
+                live_rows(w3_plane, q).bitcast(I32), w3_scales[0, PACK * q : PACK * (q + 1), :].bitcast(I32)
             )
 
-        pages = [alloc([P, T], F32, "page_0"), alloc([P, T], F32, "page_1", "wide1")]
-        nc.vector.memset(pages[0][:], 0.0)
-        z_turned = [alloc([P, 4, 2, P, 2], BF16, "z_turned_%d" % c) for c in range(CHUNKS)]
+        page_after = (None, "a_sq_0_0", "a_sq_0_1", "a_sq_1_0")
+        board_after = ("w1_grouped_3", "b_sq_0_1", "v_words_0_1", "v_words_1_1")
+        z_turned = [alloc([P, TILES, 2, P, 2], BF16, "z_turned_%d" % c) for c in range(CHUNKS)]
         for b in range(ROW_BLOCKS):
-            page = pages[b % 2]
-            if b == 1:
-                nc.vector.memset(page[:], 0.0)
-            pieces = PIECES[b]
-            width = S // pieces
-            for h in range(pieces):
-                a_sq, b_sq = squares[b][h]
-                tag = "late%d" % (b + 1) if h == pieces - 1 and b < 2 else "contest_%d" % b
-                contest = alloc([P, width], F32, "contest_%d_%d" % (b, h), tag)
-                cols = slice(width * h, width * (h + 1))
+            page = alloc([P, T], F32, "page_%d" % b, page_after[b])
+            (nc.vector if b == 0 else nc.gpsimd).memset(page[:], 0.0)
+            width = S // PIECES[b]
+            for i in range(PIECES[b]):
+                a_sq, b_sq = squares[b][i]
+                after = "w1_grouped_%d" % (b + 1) if i == PIECES[b] - 1 and b < 2 else None
+                contest = alloc([P, width], F32, "contest_%d_%d" % (b, i), after)
                 nc.vector.tensor_tensor(contest[:], a_sq[:], b_sq[:], ALU.subtract)
+                entries = idx2[:, width // GROUP * i : width // GROUP * (i + 1)]
                 nc.vector.tensor_tensor(
-                    page[:].indirect(idx2[:, width // 16 * h : width // 16 * (h + 1)]), contest[:], wgs_sb[:, cols], ALU.mult
+                    page[:].indirect(entries), contest[:], wgs_sb[:, width * i : width * (i + 1)], ALU.mult
                 )
-            board_sb = load(board[P * b : P * (b + 1), :], [P, T], "board_%d" % b, board_tags[b])
+            board_sb = load(board[P * b : P * (b + 1), :], [P, T], "board_%d" % b, board_after[b])
+            banks = HIGH if b % 2 else LOW
             if b == ROW_BLOCKS - 1:
-                w3_codes = alloc([P, N], U32, "w3_codes", "contest_2")
+                w3_codes = alloc([P, N], U32, "w3_codes", "contest_2_0")
                 nc.sync.dma_start(w3_codes[:].bitcast(I32), w3_words[0].rearrange("p c i -> p (c i)").bitcast(I32))
                 for c in range(CHUNKS):
-                    warm_ps = bank(4 + c, "warm_ps")
+                    clock_warmup = bank(banks + c, "clock_warmup")
                     nc.tensor.matmul_mx(
-                        out=warm_ps[:],
+                        out=clock_warmup[:],
                         lhsT=w3_codes[:, 0:P].bitcast(FP8X4),
                         lhsT_scale=w3_plane[:, 0:P],
                         rhs=v_words[(0, 0)][:].bitcast(FP8X4),
@@ -210,98 +229,110 @@ def tile_list_pass_arbitration_scores_kernel(
                         start=True,
                         stop=True,
                     )
-            sums = [bank(4 * (b % 2) + c, "z_ps") for c in range(CHUNKS)]
-            early, late = (board_sb, page) if b == ROW_BLOCKS - 1 else (page, board_sb)
+            sums = [bank(banks + c, "z_bank") for c in range(CHUNKS)]
             for c in range(CHUNKS):
-                for s in range(4):
+                for s in range(TILES):
                     slots = slice(BANK * c + P * s, BANK * c + P * (s + 1))
                     nc.tensor.matmul(
-                        sums[c][:, P * s : P * (s + 1)], early[:, slots], ident[:],
+                        sums[c][:, P * s : P * (s + 1)], board_sb[:, slots], ident[:],
                         start=(s == 0), stop=False, is_transpose=True,
                     )
             for c in range(CHUNKS):
-                for s in range(4):
+                for s in range(TILES):
                     slots = slice(BANK * c + P * s, BANK * c + P * (s + 1))
                     nc.tensor.matmul(
-                        sums[c][:, P * s : P * (s + 1)], late[:, slots], ident[:],
-                        start=False, stop=(s == 3), is_transpose=True,
+                        sums[c][:, P * s : P * (s + 1)], page[:, slots], ident[:],
+                        start=False, stop=(s == TILES - 1), is_transpose=True,
                     )
                 nc.scalar.copy(
-                    z_turned[c][:, :, :, 32 * b : 32 * (b + 1), :],
-                    sums[c][:].rearrange("p (s i u e) -> p s u i e", s=4, u=2, e=2),
+                    z_turned[c][:, :, :, P // PACK * b : P // PACK * (b + 1), :],
+                    sums[c][:].rearrange("p (s i u e) -> p s u i e", s=TILES, u=2, e=2),
                 )
 
+        result_after = ("b_sq_1_0", "a_sq_2_0", "a_sq_3_0")
+        results = []
+        for n in range(OUT_BLOCKS):
+            result = alloc([P, T], F32, "result_%d" % n, result_after[n])
+            nc.gpsimd.memset(result[:], 0.0)
+            results.append(result)
+
         wgo_sb = load(wgo, [P, S], "wgo_sb", "b_sq_0_0")
-        prios = [
-            load(prio[P * n : P * (n + 1), :], [P, S], "prio_%d" % n, ("contest_0", "late1", "late2")[n])
-            for n in range(OUT_BLOCKS)
-        ]
+        prio_after = ("contest_0_0", "contest_0_1", "contest_1_0")
+        prios = [load(prio[P * n : P * (n + 1), :], [P, S], "prio_%d" % n, prio_after[n]) for n in range(OUT_BLOCKS)]
 
         z_codes, z_planes = [], []
-        scores = [alloc([P, T], F32, "scores_0")]
+        gates = [alloc([P, T], F32, "gates_0")]
 
-        def score(n, c, index):
-            y_ps = bank(index, "y_ps")
+        def score(n, c, index, first=0, count=BANK):
+            y_bank = bank(index, "y_bank")
+            slots = slice(first, first + count)
             nc.tensor.matmul_mx(
-                out=y_ps[:],
+                out=y_bank[:, 0:count],
                 lhsT=w3_codes[:, P * n : P * (n + 1)].bitcast(FP8X4),
                 lhsT_scale=w3_plane[:, P * n : P * (n + 1)],
-                rhs=z_codes[c][:].bitcast(FP8X4),
-                rhs_scale=z_planes[c][:],
+                rhs=z_codes[c][:, slots].bitcast(FP8X4),
+                rhs_scale=z_planes[c][:, slots],
                 start=True,
                 stop=True,
             )
-            nc.scalar.activation(scores[n][:, BANK * c : BANK * (c + 1)], y_ps[:], ACT.Sigmoid)
+            nc.scalar.activation(
+                gates[n][:, BANK * c + first : BANK * c + first + count], y_bank[:, 0:count], ACT.Sigmoid
+            )
 
+        half_chunk = BANK // 2
         for c in range(CHUNKS):
-            z_grouped = alloc([P, BANK, 4], BF16, "z_grouped_%d" % c)
+            z_grouped = alloc([P, BANK, PACK], BF16, "z_grouped_%d" % c, "z_grouped_%d" % (c - 2) if c >= 2 else None)
             z_pairs = z_turned[c][:].rearrange("p s u r e -> p (s u r e)").bitcast(F32)
             for half in range(2):
-                back = bank(2 * (c % 2) + half, "back_ps")
-                for i in range(4):
+                pair_bank = bank(LOW + 2 * (c % 2) + half, "pair_bank")
+                for i in range(TILES):
                     nc.tensor.transpose(
-                        back[:, P * i : P * (i + 1)], z_pairs[:, BANK * half + P * i : BANK * half + P * (i + 1)], ident[:]
+                        pair_bank[:, P * i : P * (i + 1)],
+                        z_pairs[:, BANK * half + P * i : BANK * half + P * (i + 1)],
+                        ident[:],
                     )
-                dst = z_grouped[:, 256 * half : 256 * (half + 1), :].rearrange("p c j -> p (c j)").bitcast(F32)
-                dst = dst.rearrange("p (s c u) -> p s c u", s=2, u=2)
-                src = back[:].rearrange("p (s u c) -> p s c u", s=2, u=2)
-                if half == 0 or c in (1, 2):
+                dst = z_grouped[:, half_chunk * half : half_chunk * (half + 1), :]
+                dst = dst.rearrange("p c j -> p (c j)").bitcast(F32).rearrange("p (s c u) -> p s c u", s=2, u=2)
+                src = pair_bank[:].rearrange("p (s u c) -> p s c u", s=2, u=2)
+                if half == 0:
                     nc.scalar.copy(dst, src)
                 else:
                     nc.vector.tensor_copy(dst, src)
             codes = alloc([P, BANK], U32, "z_codes_%d" % c)
             plane = alloc([P, BANK], U8, "z_plane_%d" % c)
-            nc.vector.quantize_mx(
-                out=codes[:].bitcast(FP8X4), scales=plane[:], in_=z_grouped[:].rearrange("p c j -> p (c j)")
-            )
             z_codes.append(codes)
             z_planes.append(plane)
-            score(0, c, 4 + c)
+            parts = 2 if c == CHUNKS - 1 else 1
+            count = BANK // parts
+            for i in range(parts):
+                slots = slice(count * i, count * (i + 1))
+                nc.vector.quantize_mx(
+                    out=codes[:, slots].bitcast(FP8X4),
+                    scales=plane[:, slots],
+                    in_=z_grouped[:, slots, :].rearrange("p c j -> p (c j)"),
+                )
+                score(0, c, HIGH + c if i == 0 else LOW, count * i, count)
 
-        gains_first = alloc([P, 2 * S], F32, "gains_first", "wide0")
-        gains_last = alloc([P, S], F32, "gains_last", "z_grouped_1")
-        gains = [gains_first[:, 0:S], gains_first[:, S : 2 * S], gains_last[:]]
-        rows = [alloc([P, T], F32, "rows_0", "contest_3"), alloc([P, T], F32, "rows_1", "z_grouped_3")]
+        weights = alloc([P, OUT_BLOCKS, S], F32, "weights", "second_loads")
         for n in range(OUT_BLOCKS):
-            nc.vector.tensor_tensor(gains[n], prios[n][:], wgo_sb[:], ALU.mult)
-            if n < 2:
-                nc.vector.memset(rows[n][:], 0.0)
-        scores.append(alloc([P, T], F32, "scores_1", "a_sq_0_0"))
-        scores.append(alloc([P, T], F32, "scores_2", "page_0"))
+            nc.vector.tensor_tensor(weights[:, n, :], prios[n][:], wgo_sb[:], ALU.mult)
+        gates.append(alloc([P, T], F32, "gates_1", "z_grouped_3"))
+        gates.append(alloc([P, T], F32, "gates_2", "tab_words_1"))
         for n in range(1, OUT_BLOCKS):
             for c in range(CHUNKS):
-                score(n, c, (2, 3, 7, 6)[c])
+                score(n, c, HIGH + c)
 
-        gates = []
+        picked_gates = []
 
         def pick(n):
-            gate = alloc([P, S], F32, "gate_%d" % n, ("b_sq_3_0", "a_sq_3_0")[n % 2])
-            nc.vector.tensor_copy(gate[:], scores[n][:].indirect(idx3[:]))
-            gates.append(gate)
+            after = ("b_sq_3_0", "contest_3_0", "picked_gates_0")[n]
+            picked_gate = alloc([P, S], F32, "picked_gates_%d" % n, after)
+            nc.vector.tensor_copy(picked_gate[:], gates[n][:].indirect(idx3[:]))
+            picked_gates.append(picked_gate)
 
         pick(0)
         for n in range(OUT_BLOCKS):
             if n + 1 < OUT_BLOCKS:
                 pick(n + 1)
-            nc.vector.tensor_tensor(rows[n % 2][:].indirect(idx4[:]), gates[n][:], gains[n], ALU.mult)
-            nc.sync.dma_start(out[P * n : P * (n + 1), :], rows[n % 2][:])
+            nc.vector.tensor_tensor(results[n][:].indirect(idx4[:]), picked_gates[n][:], weights[:, n, :], ALU.mult)
+            nc.sync.dma_start(out[P * n : P * (n + 1), :], results[n][:])

@@ -327,12 +327,12 @@ def tile_list_pass_arbitration_scores_kernel(
         def pick(n):
             after = ("b_sq_3_0", "contest_3_0", "picked_gates_0")[n]
             picked_gate = alloc([P, S], F32, "picked_gates_%d" % n, after)
-            nc.vector.tensor_copy(picked_gate[:], gates[n][:].indirect(idx3[:]))
+            nc.vector.tensor_tensor(picked_gate[:], gates[n][:].indirect(idx3[:]), weights[:, n, :], ALU.mult)
             picked_gates.append(picked_gate)
 
         pick(0)
         for n in range(OUT_BLOCKS):
             if n + 1 < OUT_BLOCKS:
                 pick(n + 1)
-            nc.vector.tensor_tensor(results[n][:].indirect(idx4[:]), picked_gates[n][:], weights[:, n, :], ALU.mult)
+            nc.vector.tensor_copy(results[n][:].indirect(idx4[:]), picked_gates[n][:])
             nc.sync.dma_start(out[P * n : P * (n + 1), :], results[n][:])

@@ -190,15 +190,15 @@ def tile_list_pass_arbitration_scores_kernel(
                 nc.scalar.activation(a_sq[:, offset : offset + BANK], a_bank[:], ACT.Square)
                 nc.scalar.activation(b_sq[:, offset : offset + BANK], b_bank[:], ACT.Square)
 
-        w3_plane = alloc([P, N], U8, "w3_plane", "v_words_1_0")
+        w3_plane = alloc([P, N], U8, "w3_plane", "w1_codes_2")
         nc.gpsimd.memset(w3_plane[:].bitcast(I32), 0)
         for q in range(QUADRANTS):
             nc.sync.dma_start(
                 live_rows(w3_plane, q).bitcast(I32), w3_scales[0, PACK * q : PACK * (q + 1), :].bitcast(I32)
             )
 
-        page_after = (None, "a_sq_0_0", "a_sq_0_1", "a_sq_1_0")
-        board_after = ("w1_grouped_3", "b_sq_0_1", "v_words_0_1", "v_words_1_1")
+        page_after = (None, "b_sq_0_0", "b_sq_0_1", "a_sq_1_0")
+        board_after = ("w1_grouped_3", "w1_codes_0", "v_words_0_1", "v_words_1_1")
         z_turned = [alloc([P, TILES, 2, P, 2], BF16, "z_turned_%d" % c) for c in range(CHUNKS)]
         for b in range(ROW_BLOCKS):
             page = alloc([P, T], F32, "page_%d" % b, page_after[b])
@@ -244,7 +244,7 @@ def tile_list_pass_arbitration_scores_kernel(
                         sums[c][:, P * s : P * (s + 1)], page[:, slots], ident[:],
                         start=False, stop=(s == TILES - 1), is_transpose=True,
                     )
-                nc.scalar.copy(
+                (nc.vector.tensor_copy if b == ROW_BLOCKS - 1 and c % 2 else nc.scalar.copy)(
                     z_turned[c][:, :, :, P // PACK * b : P // PACK * (b + 1), :],
                     sums[c][:].rearrange("p (s i u e) -> p s u i e", s=TILES, u=2, e=2),
                 )
@@ -256,7 +256,7 @@ def tile_list_pass_arbitration_scores_kernel(
             nc.gpsimd.memset(result[:], 0.0)
             results.append(result)
 
-        wgo_sb = load(wgo, [P, S], "wgo_sb", "b_sq_0_0")
+        wgo_sb = load(wgo, [P, S], "wgo_sb", "w1_codes_1")
         prio_after = ("contest_0_0", "contest_0_1", "contest_1_0")
         prios = [load(prio[P * n : P * (n + 1), :], [P, S], "prio_%d" % n, prio_after[n]) for n in range(OUT_BLOCKS)]
 
@@ -281,10 +281,10 @@ def tile_list_pass_arbitration_scores_kernel(
 
         half_chunk = BANK // 2
         for c in range(CHUNKS):
-            z_grouped = alloc([P, BANK, PACK], BF16, "z_grouped_%d" % c, "z_grouped_%d" % (c - 2) if c >= 2 else None)
+            z_grouped = alloc([P, BANK, PACK], BF16, "z_grouped_%d" % c, ("a_sq_0_0", "a_sq_0_1", "v_words_1_0", "w1_first")[c])
             z_pairs = z_turned[c][:].rearrange("p s u r e -> p (s u r e)").bitcast(F32)
             for half in range(2):
-                pair_bank = bank(LOW + 2 * (c % 2) + half, "pair_bank")
+                pair_bank = bank(LOW + 2 * c + half, "pair_bank")
                 for i in range(TILES):
                     nc.tensor.transpose(
                         pair_bank[:, P * i : P * (i + 1)],
@@ -294,7 +294,7 @@ def tile_list_pass_arbitration_scores_kernel(
                 dst = z_grouped[:, half_chunk * half : half_chunk * (half + 1), :]
                 dst = dst.rearrange("p c j -> p (c j)").bitcast(F32).rearrange("p (s c u) -> p s c u", s=2, u=2)
                 src = pair_bank[:].rearrange("p (s u c) -> p s c u", s=2, u=2)
-                if half == 0:
+                if half == 0 or c == 1:
                     nc.scalar.copy(dst, src)
                 else:
                     nc.vector.tensor_copy(dst, src)
@@ -311,28 +311,25 @@ def tile_list_pass_arbitration_scores_kernel(
                     scales=plane[:, slots],
                     in_=z_grouped[:, slots, :].rearrange("p c j -> p (c j)"),
                 )
-                score(0, c, HIGH + c if i == 0 else LOW, count * i, count)
+                score(0, c, LOW + c if i == 0 else LOW, count * i, count)
 
-        weights = alloc([P, OUT_BLOCKS, S], F32, "weights", "second_loads")
-        for n in range(OUT_BLOCKS):
-            nc.vector.tensor_tensor(weights[:, n, :], prios[n][:], wgo_sb[:], ALU.mult)
-        gates.append(alloc([P, T], F32, "gates_1", "z_grouped_3"))
+        gates.append(alloc([P, T], F32, "gates_1", "z_turned_3"))
         gates.append(alloc([P, T], F32, "gates_2", "tab_words_1"))
         for n in range(1, OUT_BLOCKS):
             for c in range(CHUNKS):
-                score(n, c, HIGH + c)
+                score(n, c, (HIGH if n == 1 else LOW) + c)
 
         picked_gates = []
 
         def pick(n):
             after = ("b_sq_3_0", "contest_3_0", "picked_gates_0")[n]
             picked_gate = alloc([P, S], F32, "picked_gates_%d" % n, after)
-            nc.vector.tensor_tensor(picked_gate[:], gates[n][:].indirect(idx3[:]), weights[:, n, :], ALU.mult)
+            nc.vector.tensor_tensor(picked_gate[:], gates[n][:].indirect(idx3[:]), prios[n][:], ALU.mult)
             picked_gates.append(picked_gate)
 
         pick(0)
         for n in range(OUT_BLOCKS):
             if n + 1 < OUT_BLOCKS:
                 pick(n + 1)
-            nc.vector.tensor_copy(results[n][:].indirect(idx4[:]), picked_gates[n][:])
+            nc.vector.tensor_tensor(results[n][:].indirect(idx4[:]), picked_gates[n][:], wgo_sb[:], ALU.mult)
             nc.sync.dma_start(out[P * n : P * (n + 1), :], results[n][:])

@@ -32,7 +32,7 @@ CHUNKS = T // BANK
 TILES = BANK // P
 SCALE_ROW0 = P - PASSES * K_PASS // 32
 LOW, HIGH = 0, 4
-PIECES = (2, 1, 1, 1)
+PIECES = ((256, 256, 512), (512, 512), (512, 512), (512, 512))
 
 
 def tile_list_pass_arbitration_scores_kernel(
@@ -75,9 +75,9 @@ def tile_list_pass_arbitration_scores_kernel(
             nc.sync.dma_start(words[:].bitcast(I32), tab_words[a].rearrange("p t i -> p (t i)").bitcast(I32))
             return words
 
-        def load_w1(dst, first, last):
+        def load_w1(dst, first, last, passes=(0, 1)):
             views = []
-            for a in range(PASSES):
+            for a in passes:
                 src = w1[K_PASS * a : K_PASS * (a + 1), first:last].rearrange("(p j) c -> p j c", j=PACK)
                 size = PACK * (last - first)
                 view = dst[:, size * a : size * (a + 1)].rearrange("p (j c) -> p j c", j=PACK)
@@ -85,83 +85,98 @@ def tile_list_pass_arbitration_scores_kernel(
                 views.append(view)
             return views
 
+        w2_plane = zeroed_plane(PASSES * H, "w2_plane")
+        for q in range(QUADRANTS):
+            nc.gpsimd.dma_start(
+                live_rows(w2_plane, q).rearrange("p (a c) -> p a c", a=PASSES).bitcast(I32),
+                w2_scales[:, PACK * q : PACK * (q + 1), :].rearrange("a r c -> r a c").bitcast(I32),
+            )
+        warmup_in = alloc([P, 1], F32, "warmup_in")
+        nc.vector.memset(warmup_in[:], 0.0)
+        table_warmup = alloc([P, 1], F32, "table_warmup")
+        nc.scalar.activation(table_warmup[:], warmup_in[:], ACT.Sigmoid)
+
         idx = load_list(offs, "idx")
         tab_plane = alloc([P, T], U8, "tab_plane")
         nc.sync.dma_start(
             tab_plane[SCALE_ROW0:P, :].bitcast(I32), tab_scales.rearrange("a q c -> q a c").bitcast(I32)
         )
         nc.vector.memset(tab_plane[0:SCALE_ROW0, :].bitcast(I32), 0)
+        tab_tiles = [load_table_pass(a) for a in range(PASSES)]
         w1_first = alloc([P, PASSES * PACK * P], F32, "w1_first")
-        w1_views = load_w1(w1_first, 0, P)
-        idx2 = load_list(offs2, "idx2")
-        idx3 = load_list(offs3, "idx3")
-        idx4 = load_list(offs4, "idx4")
-        tab_tiles = [load_table_pass(0)]
-        w2_plane = zeroed_plane(PASSES * H, "w2_plane")
-        for q in range(QUADRANTS):
-            nc.sync.dma_start(
-                live_rows(w2_plane, q).rearrange("p (a c) -> p a c", a=PASSES).bitcast(I32),
-                w2_scales[:, PACK * q : PACK * (q + 1), :].rearrange("a r c -> r a c").bitcast(I32),
-            )
-        tab_tiles.append(load_table_pass(1))
+        w1_loads = [load_w1(w1_first, 0, P)]
         w2_codes = alloc([P, PASSES, 2 * H], U8, "w2_codes")
         nc.sync.dma_start(w2_codes[:].bitcast(I32), w2_words.rearrange("a p c -> p a c").bitcast(I32))
+        idx2 = load_list(offs2, "idx2")
 
+        first_page = alloc([P, T], F32, "page_0")
+        nc.gpsimd.memset(first_page[:], 0.0)
         ident = alloc([P, P], F32, "ident")
         make_identity(nc, ident[:])
-        table_warmup = alloc([P, 1], F32, "table_warmup")
-        nc.scalar.activation(table_warmup[:], ident[:, 0:1], ACT.Sigmoid)
 
         v_plane = zeroed_plane(PASSES * S, "v_plane")
         picked_scales = alloc([P, S], U8, "picked_scales")
         nc.vector.tensor_copy(picked_scales[:], tab_plane[:].indirect(idx[:]))
         quadrant_rows = PASSES * PACK
         for q in range(QUADRANTS):
-            nc.sync.dma_start(
+            nc.scalar.dma_start(
                 live_rows(v_plane, q).bitcast(I32),
                 picked_scales[SCALE_ROW0 + quadrant_rows * q : SCALE_ROW0 + quadrant_rows * (q + 1), :].bitcast(I32),
             )
 
         v_words = {}
         half_columns = BANK // GROUP
-        for a in range(PASSES):
-            for h in range(HALVES):
-                picked = alloc([P, BANK], U32, "v_words_%d_%d" % (a, h))
-                entries = idx[:, half_columns * h : half_columns * (h + 1)]
-                nc.vector.tensor_copy(picked[:], tab_tiles[a][:].indirect(entries))
-                v_words[(a, h)] = picked
 
-        second_loads = alloc([P, S + PASSES * PACK * (H - P)], F32, "second_loads", "tab_words_0")
+        def pick_words(a, h, after=None):
+            picked = alloc([P, BANK], U32, "v_words_%d_%d" % (a, h), after)
+            entries = idx[:, half_columns * h : half_columns * (h + 1)]
+            nc.vector.tensor_copy(picked[:], tab_tiles[a][:].indirect(entries))
+            v_words[(a, h)] = picked
+
+        def cast_w1(views, name, after=None):
+            grouped = alloc([P, len(views), views[0].shape[2], PACK], BF16, name, after)
+            for i, view in enumerate(views):
+                nc.scalar.copy(
+                    grouped[:, i, :, :].rearrange("p (c i) j -> p c j i", i=4),
+                    view.rearrange("p j (c i) -> p c j i", i=4),
+                )
+            return grouped
+
+        def quantise(codes, plane, grouped):
+            nc.vector.quantize_mx(out=codes.bitcast(FP8X4), scales=plane, in_=grouped[:].rearrange("p a c j -> p (a c j)"))
+
+        first_codes = alloc([P, PASSES * P], U32, "w1_codes_0")
+        first_plane = alloc([P, PASSES * P], U8, "w1_plane_0")
+        pick_words(0, 0)
+        pick_words(1, 0)
+        for a, name in enumerate(("w1_grouped_0a", "w1_grouped_0")):
+            columns = slice(P * a, P * (a + 1))
+            quantise(first_codes[:, columns], first_plane[:, columns], cast_w1(w1_loads[0][a : a + 1], name))
+        pick_words(0, 1, "w1_grouped_0")
+        pick_words(1, 1, "w1_grouped_0a")
+
+        w1_block = PASSES * PACK * P
+        second_loads = alloc([P, S + 3 * w1_block], F32, "second_loads", "tab_plane")
         wgs_sb = second_loads[:, 0:S]
         nc.sync.dma_start(wgs_sb, wgs)
-        w1_block = PASSES * PACK * P
+        w1_loads.append(load_w1(second_loads[:, S : S + w1_block], P, 2 * P))
+        w1_loads.append(load_w1(second_loads[:, S + w1_block :], 2 * P, H))
+        idx3 = load_list(offs3, "idx3")
+        idx4 = load_list(offs4, "idx4")
+
+        pages = [first_page]
+        for a in range(PASSES):
+            pages.append(alloc([P, T], F32, "page_%d" % (a + 1), "tab_words_%d" % a))
+            nc.gpsimd.memset(pages[a + 1][:], 0.0)
 
         squares = []
-        for b in range(ROW_BLOCKS):
-            if b == 1:
-                w1_views = load_w1(second_loads[:, S : S + w1_block], P, 2 * P)
-            if b == 2:
-                w1_views = load_w1(second_loads[:, S + w1_block :], 2 * P, H)
-            column0 = P * max(b - 2, 0)
-            width = S // PIECES[b]
+
+        def project(b, codes, plane, stride, column0):
             squares.append(
                 [
                     (alloc([P, width], F32, "a_sq_%d_%d" % (b, i)), alloc([P, width], F32, "b_sq_%d_%d" % (b, i)))
-                    for i in range(PIECES[b])
+                    for i, width in enumerate(PIECES[b])
                 ]
-            )
-            w1_grouped = alloc([P, PASSES, P, PACK], BF16, "w1_grouped_%d" % b)
-            for a in range(PASSES):
-                nc.scalar.copy(
-                    w1_grouped[:, a, :, :].rearrange("p (c i) j -> p c j i", i=4),
-                    w1_views[a][:, :, column0 : column0 + P].rearrange("p j (c i) -> p c j i", i=4),
-                )
-            w1_codes = alloc([P, PASSES * P], U32, "w1_codes_%d" % b)
-            w1_plane = alloc([P, PASSES * P], U8, "w1_plane_%d" % b)
-            nc.vector.quantize_mx(
-                out=w1_codes[:].bitcast(FP8X4),
-                scales=w1_plane[:],
-                in_=w1_grouped[:].rearrange("p a c j -> p (a c j)"),
             )
             for h in range(HALVES):
                 a_bank = bank(HIGH + 2 * h, "a_bank")
@@ -169,8 +184,8 @@ def tile_list_pass_arbitration_scores_kernel(
                 for a in range(PASSES):
                     nc.tensor.matmul_mx(
                         out=a_bank[:],
-                        lhsT=w1_codes[:, P * a : P * (a + 1)].bitcast(FP8X4),
-                        lhsT_scale=w1_plane[:, P * a : P * (a + 1)],
+                        lhsT=codes[:, stride * a + column0 : stride * a + column0 + P].bitcast(FP8X4),
+                        lhsT_scale=plane[:, stride * a + column0 : stride * a + column0 + P],
                         rhs=v_words[(a, h)][:].bitcast(FP8X4),
                         rhs_scale=v_plane[:, S * a + BANK * h : S * a + BANK * (h + 1)],
                         start=(a == 0),
@@ -185,38 +200,72 @@ def tile_list_pass_arbitration_scores_kernel(
                         start=(a == 0),
                         stop=(a == PASSES - 1),
                     )
-                piece, offset = divmod(BANK * h, width)
-                a_sq, b_sq = squares[b][piece]
-                nc.scalar.activation(a_sq[:, offset : offset + BANK], a_bank[:], ACT.Square)
-                nc.scalar.activation(b_sq[:, offset : offset + BANK], b_bank[:], ACT.Square)
+                for i, width in enumerate(PIECES[b]):
+                    start = sum(PIECES[b][:i])
+                    first, last = max(start, BANK * h), min(start + width, BANK * (h + 1))
+                    if first < last:
+                        for square, source in zip(squares[b][i], (a_bank, b_bank)):
+                            nc.scalar.activation(
+                                square[:, first - start : last - start],
+                                source[:, first - BANK * h : last - BANK * h],
+                                ACT.Square,
+                            )
 
-        w3_plane = alloc([P, N], U8, "w3_plane", "w1_codes_2")
+        def place_piece(b, i, contest_after, placed_after):
+            width, start = PIECES[b][i], sum(PIECES[b][:i])
+            engine = nc.vector if b == 0 else nc.gpsimd
+            a_sq, b_sq = squares[b][i]
+            contest = alloc([P, width], F32, "contest_%d_%d" % (b, i), contest_after)
+            engine.tensor_tensor(contest[:], a_sq[:], b_sq[:], ALU.subtract)
+            entries = idx2[:, start // GROUP : (start + width) // GROUP]
+            window, weight = pages[b % 3][:].indirect(entries), wgs_sb[:, start : start + width]
+            if b == 0 and i < 2:
+                nc.vector.tensor_tensor(window, contest[:], weight, ALU.mult)
+            else:
+                placed = alloc([P, width], F32, "placed_%d_%d" % (b, i), placed_after)
+                engine.tensor_tensor(placed[:], contest[:], weight, ALU.mult)
+                nc.vector.tensor_copy(window, placed[:])
+
+        def quantise_block(grouped, b, codes_after):
+            columns = PASSES * grouped.shape[2]
+            codes = alloc([P, columns], U32, "w1_codes_%d" % b, codes_after)
+            plane = alloc([P, columns], U8, "w1_plane_%d" % b)
+            quantise(codes[:], plane[:], grouped)
+            return codes, plane
+
+        project(0, first_codes, first_plane, P, 0)
+        place_piece(0, 0, None, None)
+        place_piece(0, 1, None, None)
+        second_grouped = cast_w1(w1_loads[1], "w1_grouped_1", "a_sq_0_0")
+        last_grouped = cast_w1(w1_loads[2], "w1_grouped_2", "b_sq_0_0")
+        project(1, *quantise_block(second_grouped, 1, None), P, 0)
+        place_piece(0, 2, "w1_grouped_1", None)
+        last_codes, last_plane = quantise_block(last_grouped, 2, "placed_0_2")
+        project(2, last_codes, last_plane, 2 * P, 0)
+        project(3, last_codes, last_plane, 2 * P, P)
+
+        w3_plane = alloc([P, N], U8, "w3_plane", "a_sq_0_1")
         nc.gpsimd.memset(w3_plane[:].bitcast(I32), 0)
         for q in range(QUADRANTS):
             nc.sync.dma_start(
                 live_rows(w3_plane, q).bitcast(I32), w3_scales[0, PACK * q : PACK * (q + 1), :].bitcast(I32)
             )
 
-        page_after = (None, "b_sq_0_0", "b_sq_0_1", "a_sq_1_0")
-        board_after = ("w1_grouped_3", "w1_codes_0", "v_words_0_1", "v_words_1_1")
+        board_after = ("w1_codes_0", "w1_plane_1", "v_words_0_1", "v_words_1_1")
+        contest_after = {(1, 0): "contest_0_2", (1, 1): "w1_grouped_2", (2, 0): "contest_1_0",
+                         (2, 1): "contest_1_1", (3, 0): "contest_2_0", (3, 1): "contest_2_1"}
+        placed_after = {(1, 0): None, (1, 1): None, (2, 0): None,
+                        (2, 1): "placed_1_0", (3, 0): "placed_1_1", (3, 1): "placed_2_0"}
         z_turned = [alloc([P, TILES, 2, P, 2], BF16, "z_turned_%d" % c) for c in range(CHUNKS)]
         for b in range(ROW_BLOCKS):
-            page = alloc([P, T], F32, "page_%d" % b, page_after[b])
-            (nc.vector if b == 0 else nc.gpsimd).memset(page[:], 0.0)
-            width = S // PIECES[b]
-            for i in range(PIECES[b]):
-                a_sq, b_sq = squares[b][i]
-                after = "w1_grouped_%d" % (b + 1) if i == PIECES[b] - 1 and b < 2 else None
-                contest = alloc([P, width], F32, "contest_%d_%d" % (b, i), after)
-                nc.vector.tensor_tensor(contest[:], a_sq[:], b_sq[:], ALU.subtract)
-                entries = idx2[:, width // GROUP * i : width // GROUP * (i + 1)]
-                nc.vector.tensor_tensor(
-                    page[:].indirect(entries), contest[:], wgs_sb[:, width * i : width * (i + 1)], ALU.mult
-                )
+            page = pages[b % 3]
+            if b > 0:
+                for i in range(len(PIECES[b])):
+                    place_piece(b, i, contest_after[(b, i)], placed_after[(b, i)])
             board_sb = load(board[P * b : P * (b + 1), :], [P, T], "board_%d" % b, board_after[b])
-            banks = HIGH if b % 2 else LOW
+            banks = HIGH if b == ROW_BLOCKS - 1 else LOW
             if b == ROW_BLOCKS - 1:
-                w3_codes = alloc([P, N], U32, "w3_codes", "contest_2_0")
+                w3_codes = alloc([P, N], U32, "w3_codes", "placed_2_1")
                 nc.sync.dma_start(w3_codes[:].bitcast(I32), w3_words[0].rearrange("p c i -> p (c i)").bitcast(I32))
                 for c in range(CHUNKS):
                     clock_warmup = bank(banks + c, "clock_warmup")
@@ -249,15 +298,17 @@ def tile_list_pass_arbitration_scores_kernel(
                     sums[c][:].rearrange("p (s i u e) -> p s u i e", s=TILES, u=2, e=2),
                 )
 
-        result_after = ("b_sq_1_0", "a_sq_2_0", "a_sq_3_0")
         results = []
-        for n in range(OUT_BLOCKS):
-            result = alloc([P, T], F32, "result_%d" % n, result_after[n])
+
+        def zeroed_result(n, after):
+            result = alloc([P, T], F32, "result_%d" % n, after)
             nc.gpsimd.memset(result[:], 0.0)
             results.append(result)
 
-        wgo_sb = load(wgo, [P, S], "wgo_sb", "w1_codes_1")
-        prio_after = ("contest_0_0", "contest_0_1", "contest_1_0")
+        zeroed_result(0, "contest_3_1")
+        zeroed_result(1, "second_loads")
+        wgo_sb = load(wgo, [P, S], "wgo_sb", "w1_plane_2")
+        prio_after = ("board_0", "board_1", "board_2")
         prios = [load(prio[P * n : P * (n + 1), :], [P, S], "prio_%d" % n, prio_after[n]) for n in range(OUT_BLOCKS)]
 
         z_codes, z_planes = [], []
@@ -281,7 +332,7 @@ def tile_list_pass_arbitration_scores_kernel(
 
         half_chunk = BANK // 2
         for c in range(CHUNKS):
-            z_grouped = alloc([P, BANK, PACK], BF16, "z_grouped_%d" % c, ("a_sq_0_0", "a_sq_0_1", "v_words_1_0", "w1_first")[c])
+            z_grouped = alloc([P, BANK, PACK], BF16, "z_grouped_%d" % c, ("a_sq_2_0", "a_sq_2_1", "v_words_1_0", "w1_first")[c])
             z_pairs = z_turned[c][:].rearrange("p s u r e -> p (s u r e)").bitcast(F32)
             for half in range(2):
                 pair_bank = bank(LOW + 2 * c + half, "pair_bank")
@@ -314,7 +365,7 @@ def tile_list_pass_arbitration_scores_kernel(
                 score(0, c, LOW + c if i == 0 else LOW, count * i, count)
 
         gates.append(alloc([P, T], F32, "gates_1", "z_turned_3"))
-        gates.append(alloc([P, T], F32, "gates_2", "tab_words_1"))
+        gates.append(alloc([P, T], F32, "gates_2", "page_2"))
         for n in range(1, OUT_BLOCKS):
             for c in range(CHUNKS):
                 score(n, c, (HIGH if n == 1 else LOW) + c)
@@ -322,12 +373,13 @@ def tile_list_pass_arbitration_scores_kernel(
         picked_gates = []
 
         def pick(n):
-            after = ("b_sq_3_0", "contest_3_0", "picked_gates_0")[n]
+            after = ("b_sq_3_0", "b_sq_3_1", "picked_gates_0")[n]
             picked_gate = alloc([P, S], F32, "picked_gates_%d" % n, after)
             nc.vector.tensor_tensor(picked_gate[:], gates[n][:].indirect(idx3[:]), prios[n][:], ALU.mult)
             picked_gates.append(picked_gate)
 
         pick(0)
+        zeroed_result(2, "gates_0")
         for n in range(OUT_BLOCKS):
             if n + 1 < OUT_BLOCKS:
                 pick(n + 1)

@@ -27,12 +27,13 @@ GROUP = 16
 BANK = 512
 ROW_BLOCKS = H // P
 OUT_BLOCKS = N // P
-HALVES = S // BANK
 CHUNKS = T // BANK
 TILES = BANK // P
 SCALE_ROW0 = P - PASSES * K_PASS // 32
 LOW, HIGH = 0, 4
 PIECES = ((256, 256, 512), (512, 512), (512, 512), (512, 512))
+FUSED_PIECES = 2
+PAGES = 3
 
 
 def tile_list_pass_arbitration_scores_kernel(
@@ -62,10 +63,15 @@ def tile_list_pass_arbitration_scores_kernel(
             nc.sync.dma_start(dst[:], src)
             return dst
 
-        def zeroed_plane(width, name):
-            plane = alloc([P, width], U8, name)
-            nc.vector.memset(plane[:].bitcast(I32), 0)
+        def zeroed_plane(engine, width, name, after=None):
+            plane = alloc([P, width], U8, name, after)
+            engine.memset(plane[:].bitcast(I32), 0)
             return plane
+
+        def zeroed_window(name, after=None):
+            window = alloc([P, T], F32, name, after)
+            nc.gpsimd.memset(window[:], 0.0)
+            return window
 
         def live_rows(plane, q):
             return plane[QUADRANT * q : QUADRANT * q + PACK, :]
@@ -75,9 +81,9 @@ def tile_list_pass_arbitration_scores_kernel(
             nc.sync.dma_start(words[:].bitcast(I32), tab_words[a].rearrange("p t i -> p (t i)").bitcast(I32))
             return words
 
-        def load_w1(dst, first, last, passes=(0, 1)):
+        def load_w1(dst, first, last):
             views = []
-            for a in passes:
+            for a in range(PASSES):
                 src = w1[K_PASS * a : K_PASS * (a + 1), first:last].rearrange("(p j) c -> p j c", j=PACK)
                 size = PACK * (last - first)
                 view = dst[:, size * a : size * (a + 1)].rearrange("p (j c) -> p j c", j=PACK)
@@ -85,7 +91,7 @@ def tile_list_pass_arbitration_scores_kernel(
                 views.append(view)
             return views
 
-        w2_plane = zeroed_plane(PASSES * H, "w2_plane")
+        w2_plane = zeroed_plane(nc.gpsimd, PASSES * H, "w2_plane")
         for q in range(QUADRANTS):
             nc.gpsimd.dma_start(
                 live_rows(w2_plane, q).rearrange("p (a c) -> p a c", a=PASSES).bitcast(I32),
@@ -109,12 +115,11 @@ def tile_list_pass_arbitration_scores_kernel(
         nc.sync.dma_start(w2_codes[:].bitcast(I32), w2_words.rearrange("a p c -> p a c").bitcast(I32))
         idx2 = load_list(offs2, "idx2")
 
-        first_page = alloc([P, T], F32, "page_0")
-        nc.gpsimd.memset(first_page[:], 0.0)
+        pages = [zeroed_window("page_0")]
         ident = alloc([P, P], F32, "ident")
         make_identity(nc, ident[:])
 
-        v_plane = zeroed_plane(PASSES * S, "v_plane")
+        v_plane = zeroed_plane(nc.vector, PASSES * S, "v_plane")
         picked_scales = alloc([P, S], U8, "picked_scales")
         nc.vector.tensor_copy(picked_scales[:], tab_plane[:].indirect(idx[:]))
         quadrant_rows = PASSES * PACK
@@ -142,18 +147,20 @@ def tile_list_pass_arbitration_scores_kernel(
                 )
             return grouped
 
-        def quantise(codes, plane, grouped):
-            nc.vector.quantize_mx(out=codes.bitcast(FP8X4), scales=plane, in_=grouped[:].rearrange("p a c j -> p (a c j)"))
+        def quantise_w1(codes, plane, grouped):
+            nc.vector.quantize_mx(
+                out=codes.bitcast(FP8X4), scales=plane, in_=grouped[:].rearrange("p a c j -> p (a c j)")
+            )
 
         first_codes = alloc([P, PASSES * P], U32, "w1_codes_0")
         first_plane = alloc([P, PASSES * P], U8, "w1_plane_0")
         pick_words(0, 0)
+        pick_words(0, 1)
         pick_words(1, 0)
         for a, name in enumerate(("w1_grouped_0a", "w1_grouped_0")):
             columns = slice(P * a, P * (a + 1))
-            quantise(first_codes[:, columns], first_plane[:, columns], cast_w1(w1_loads[0][a : a + 1], name))
-        pick_words(0, 1, "w1_grouped_0")
-        pick_words(1, 1, "w1_grouped_0a")
+            quantise_w1(first_codes[:, columns], first_plane[:, columns], cast_w1(w1_loads[0][a : a + 1], name))
+        pick_words(1, 1, "w1_grouped_0")
 
         w1_block = PASSES * PACK * P
         second_loads = alloc([P, S + 3 * w1_block], F32, "second_loads", "tab_plane")
@@ -164,120 +171,98 @@ def tile_list_pass_arbitration_scores_kernel(
         idx3 = load_list(offs3, "idx3")
         idx4 = load_list(offs4, "idx4")
 
-        pages = [first_page]
-        for a in range(PASSES):
-            pages.append(alloc([P, T], F32, "page_%d" % (a + 1), "tab_words_%d" % a))
-            nc.gpsimd.memset(pages[a + 1][:], 0.0)
+        pages.append(zeroed_window("page_1", "tab_words_1"))
 
         squares = []
 
         def project(b, codes, plane, stride, column0):
-            squares.append(
-                [
-                    (alloc([P, width], F32, "a_sq_%d_%d" % (b, i)), alloc([P, width], F32, "b_sq_%d_%d" % (b, i)))
-                    for i, width in enumerate(PIECES[b])
-                ]
-            )
-            for h in range(HALVES):
-                a_bank = bank(HIGH + 2 * h, "a_bank")
-                b_bank = bank(HIGH + 2 * h + 1, "b_bank")
+            squares.append([])
+            for i, width in enumerate(PIECES[b]):
+                start = sum(PIECES[b][:i])
+                h, first = divmod(start, BANK)
+                bank0 = HIGH + 2 * (sum(len(block) for block in squares) % 2)
+                a_bank, b_bank = bank(bank0, "a_bank"), bank(bank0 + 1, "b_bank")
                 for a in range(PASSES):
                     nc.tensor.matmul_mx(
-                        out=a_bank[:],
+                        out=a_bank[:, 0:width],
                         lhsT=codes[:, stride * a + column0 : stride * a + column0 + P].bitcast(FP8X4),
                         lhsT_scale=plane[:, stride * a + column0 : stride * a + column0 + P],
-                        rhs=v_words[(a, h)][:].bitcast(FP8X4),
-                        rhs_scale=v_plane[:, S * a + BANK * h : S * a + BANK * (h + 1)],
+                        rhs=v_words[(a, h)][:, first : first + width].bitcast(FP8X4),
+                        rhs_scale=v_plane[:, S * a + start : S * a + start + width],
                         start=(a == 0),
                         stop=(a == PASSES - 1),
                     )
-                    nc.tensor.matmul_mx(
-                        out=b_bank[:],
-                        lhsT=w2_codes[:, a, 2 * P * b : 2 * P * (b + 1)].bitcast(FP4X4),
-                        lhsT_scale=w2_plane[:, H * a + P * b : H * a + P * (b + 1)],
-                        rhs=v_words[(a, h)][:].bitcast(FP8X4),
-                        rhs_scale=v_plane[:, S * a + BANK * h : S * a + BANK * (h + 1)],
-                        start=(a == 0),
-                        stop=(a == PASSES - 1),
-                    )
-                for i, width in enumerate(PIECES[b]):
-                    start = sum(PIECES[b][:i])
-                    first, last = max(start, BANK * h), min(start + width, BANK * (h + 1))
-                    if first < last:
-                        for square, source in zip(squares[b][i], (a_bank, b_bank)):
-                            nc.scalar.activation(
-                                square[:, first - start : last - start],
-                                source[:, first - BANK * h : last - BANK * h],
-                                ACT.Square,
-                            )
+                step = BANK if width == BANK else P
+                for offset in range(0, width, step):
+                    for a in range(PASSES):
+                        nc.tensor.matmul_mx(
+                            out=b_bank[:, offset : offset + step],
+                            lhsT=w2_codes[:, a, 2 * P * b : 2 * P * (b + 1)].bitcast(FP4X4),
+                            lhsT_scale=w2_plane[:, H * a + P * b : H * a + P * (b + 1)],
+                            rhs=v_words[(a, h)][:, first + offset : first + offset + step].bitcast(FP8X4),
+                            rhs_scale=v_plane[:, S * a + start + offset : S * a + start + offset + step],
+                            start=(a == 0),
+                            stop=(a == PASSES - 1),
+                        )
+                piece_squares = tuple(alloc([P, width], F32, "%s_sq_%d_%d" % (x, b, i)) for x in "ab")
+                for square, source in zip(piece_squares, (a_bank, b_bank)):
+                    nc.scalar.activation(square[:], source[:, 0:width], ACT.Square)
+                squares[b].append(piece_squares)
 
-        def place_piece(b, i, contest_after, placed_after):
+        def place_piece(b, i, contest_after=None, placed_after=None):
             width, start = PIECES[b][i], sum(PIECES[b][:i])
             engine = nc.vector if b == 0 else nc.gpsimd
             a_sq, b_sq = squares[b][i]
             contest = alloc([P, width], F32, "contest_%d_%d" % (b, i), contest_after)
             engine.tensor_tensor(contest[:], a_sq[:], b_sq[:], ALU.subtract)
             entries = idx2[:, start // GROUP : (start + width) // GROUP]
-            window, weight = pages[b % 3][:].indirect(entries), wgs_sb[:, start : start + width]
-            if b == 0 and i < 2:
+            window, weight = pages[b % PAGES][:].indirect(entries), wgs_sb[:, start : start + width]
+            if b == 0 and i < FUSED_PIECES:
                 nc.vector.tensor_tensor(window, contest[:], weight, ALU.mult)
             else:
                 placed = alloc([P, width], F32, "placed_%d_%d" % (b, i), placed_after)
                 engine.tensor_tensor(placed[:], contest[:], weight, ALU.mult)
                 nc.vector.tensor_copy(window, placed[:])
 
-        def quantise_block(grouped, b, codes_after):
+        def quantised_w1(grouped, b, codes_after=None):
             columns = PASSES * grouped.shape[2]
             codes = alloc([P, columns], U32, "w1_codes_%d" % b, codes_after)
             plane = alloc([P, columns], U8, "w1_plane_%d" % b)
-            quantise(codes[:], plane[:], grouped)
+            quantise_w1(codes[:], plane[:], grouped)
             return codes, plane
 
         project(0, first_codes, first_plane, P, 0)
-        place_piece(0, 0, None, None)
-        place_piece(0, 1, None, None)
+        place_piece(0, 0)
+        pages.append(zeroed_window("page_2", "b_sq_0_0"))
+        place_piece(0, 1)
         second_grouped = cast_w1(w1_loads[1], "w1_grouped_1", "a_sq_0_0")
-        last_grouped = cast_w1(w1_loads[2], "w1_grouped_2", "b_sq_0_0")
-        project(1, *quantise_block(second_grouped, 1, None), P, 0)
-        place_piece(0, 2, "w1_grouped_1", None)
-        last_codes, last_plane = quantise_block(last_grouped, 2, "placed_0_2")
+        last_grouped = cast_w1(w1_loads[2], "w1_grouped_2")
+        project(1, *quantised_w1(second_grouped, 1), P, 0)
+        place_piece(0, 2, "w1_grouped_1")
+        last_codes, last_plane = quantised_w1(last_grouped, 2, "placed_0_2")
         project(2, last_codes, last_plane, 2 * P, 0)
         project(3, last_codes, last_plane, 2 * P, P)
 
-        w3_plane = alloc([P, N], U8, "w3_plane", "a_sq_0_1")
-        nc.gpsimd.memset(w3_plane[:].bitcast(I32), 0)
+        w3_plane = zeroed_plane(nc.gpsimd, N, "w3_plane", "a_sq_0_1")
         for q in range(QUADRANTS):
             nc.sync.dma_start(
                 live_rows(w3_plane, q).bitcast(I32), w3_scales[0, PACK * q : PACK * (q + 1), :].bitcast(I32)
             )
 
+        contest_chain = ["contest_0_2", "w1_grouped_2"]
+        placed_chain = [None, None, None]
         board_after = ("w1_codes_0", "w1_plane_1", "v_words_0_1", "v_words_1_1")
-        contest_after = {(1, 0): "contest_0_2", (1, 1): "w1_grouped_2", (2, 0): "contest_1_0",
-                         (2, 1): "contest_1_1", (3, 0): "contest_2_0", (3, 1): "contest_2_1"}
-        placed_after = {(1, 0): None, (1, 1): None, (2, 0): None,
-                        (2, 1): "placed_1_0", (3, 0): "placed_1_1", (3, 1): "placed_2_0"}
         z_turned = [alloc([P, TILES, 2, P, 2], BF16, "z_turned_%d" % c) for c in range(CHUNKS)]
         for b in range(ROW_BLOCKS):
-            page = pages[b % 3]
+            page = pages[b % PAGES]
+            last_block = b == ROW_BLOCKS - 1
             if b > 0:
                 for i in range(len(PIECES[b])):
-                    place_piece(b, i, contest_after[(b, i)], placed_after[(b, i)])
+                    place_piece(b, i, contest_chain[-2], placed_chain[-3])
+                    contest_chain.append("contest_%d_%d" % (b, i))
+                    placed_chain.append("placed_%d_%d" % (b, i))
             board_sb = load(board[P * b : P * (b + 1), :], [P, T], "board_%d" % b, board_after[b])
-            banks = HIGH if b == ROW_BLOCKS - 1 else LOW
-            if b == ROW_BLOCKS - 1:
-                w3_codes = alloc([P, N], U32, "w3_codes", "placed_2_1")
-                nc.sync.dma_start(w3_codes[:].bitcast(I32), w3_words[0].rearrange("p c i -> p (c i)").bitcast(I32))
-                for c in range(CHUNKS):
-                    clock_warmup = bank(banks + c, "clock_warmup")
-                    nc.tensor.matmul_mx(
-                        out=clock_warmup[:],
-                        lhsT=w3_codes[:, 0:P].bitcast(FP8X4),
-                        lhsT_scale=w3_plane[:, 0:P],
-                        rhs=v_words[(0, 0)][:].bitcast(FP8X4),
-                        rhs_scale=v_plane[:, 0:BANK],
-                        start=True,
-                        stop=True,
-                    )
+            banks = HIGH if last_block else LOW
             sums = [bank(banks + c, "z_bank") for c in range(CHUNKS)]
             for c in range(CHUNKS):
                 for s in range(TILES):
@@ -293,23 +278,17 @@ def tile_list_pass_arbitration_scores_kernel(
                         sums[c][:, P * s : P * (s + 1)], page[:, slots], ident[:],
                         start=False, stop=(s == TILES - 1), is_transpose=True,
                     )
-                (nc.vector.tensor_copy if b == ROW_BLOCKS - 1 and c % 2 else nc.scalar.copy)(
+                copy_out = nc.vector.tensor_copy if last_block and c % 2 else nc.scalar.copy
+                copy_out(
                     z_turned[c][:, :, :, P // PACK * b : P // PACK * (b + 1), :],
                     sums[c][:].rearrange("p (s i u e) -> p s u i e", s=TILES, u=2, e=2),
                 )
 
-        results = []
-
-        def zeroed_result(n, after):
-            result = alloc([P, T], F32, "result_%d" % n, after)
-            nc.gpsimd.memset(result[:], 0.0)
-            results.append(result)
-
-        zeroed_result(0, "contest_3_1")
-        zeroed_result(1, "second_loads")
+        results = [zeroed_window("result_0", "contest_3_1"), zeroed_window("result_1", "second_loads")]
         wgo_sb = load(wgo, [P, S], "wgo_sb", "w1_plane_2")
-        prio_after = ("board_0", "board_1", "board_2")
-        prios = [load(prio[P * n : P * (n + 1), :], [P, S], "prio_%d" % n, prio_after[n]) for n in range(OUT_BLOCKS)]
+        prios = [load(prio[P * n : P * (n + 1), :], [P, S], "prio_%d" % n, "board_%d" % n) for n in range(OUT_BLOCKS)]
+        w3_codes = alloc([P, N], U32, "w3_codes", "w1_codes_2")
+        nc.sync.dma_start(w3_codes[:].bitcast(I32), w3_words[0].rearrange("p c i -> p (c i)").bitcast(I32))
 
         z_codes, z_planes = [], []
         gates = [alloc([P, T], F32, "gates_0")]
@@ -331,8 +310,10 @@ def tile_list_pass_arbitration_scores_kernel(
             )
 
         half_chunk = BANK // 2
+        grouped_after = ("a_sq_2_0", "a_sq_2_1", "v_words_1_0", "w1_first")
+        scalar_chunk = 1
         for c in range(CHUNKS):
-            z_grouped = alloc([P, BANK, PACK], BF16, "z_grouped_%d" % c, ("a_sq_2_0", "a_sq_2_1", "v_words_1_0", "w1_first")[c])
+            z_grouped = alloc([P, BANK, PACK], BF16, "z_grouped_%d" % c, grouped_after[c])
             z_pairs = z_turned[c][:].rearrange("p s u r e -> p (s u r e)").bitcast(F32)
             for half in range(2):
                 pair_bank = bank(LOW + 2 * c + half, "pair_bank")
@@ -345,7 +326,7 @@ def tile_list_pass_arbitration_scores_kernel(
                 dst = z_grouped[:, half_chunk * half : half_chunk * (half + 1), :]
                 dst = dst.rearrange("p c j -> p (c j)").bitcast(F32).rearrange("p (s c u) -> p s c u", s=2, u=2)
                 src = pair_bank[:].rearrange("p (s u c) -> p s c u", s=2, u=2)
-                if half == 0 or c == 1:
+                if half == 0 or c == scalar_chunk:
                     nc.scalar.copy(dst, src)
                 else:
                     nc.vector.tensor_copy(dst, src)
@@ -365,7 +346,7 @@ def tile_list_pass_arbitration_scores_kernel(
                 score(0, c, LOW + c if i == 0 else LOW, count * i, count)
 
         gates.append(alloc([P, T], F32, "gates_1", "z_turned_3"))
-        gates.append(alloc([P, T], F32, "gates_2", "page_2"))
+        gates.append(alloc([P, T], F32, "gates_2", "tab_words_0"))
         for n in range(1, OUT_BLOCKS):
             for c in range(CHUNKS):
                 score(n, c, (HIGH if n == 1 else LOW) + c)
@@ -379,7 +360,7 @@ def tile_list_pass_arbitration_scores_kernel(
             picked_gates.append(picked_gate)
 
         pick(0)
-        zeroed_result(2, "gates_0")
+        results.append(zeroed_window("result_2", "gates_0"))
         for n in range(OUT_BLOCKS):
             if n + 1 < OUT_BLOCKS:
                 pick(n + 1)

@@ -43,6 +43,7 @@ def tile_list_pass_arbitration_scores_kernel(
     nc = tc.nc
     with ExitStack() as ctx:
         sbuf = ctx.enter_context(tc.tile_pool(name="sbuf", bufs=1))
+        placed_by_hand = ctx.enter_context(tc.tile_pool(name="placed_by_hand", bufs=1))
         psum = ctx.enter_context(tc.psum_pool(name="psum", bufs=1))
         place = {}
 
@@ -68,10 +69,12 @@ def tile_list_pass_arbitration_scores_kernel(
             engine.memset(plane[:].bitcast(I32), 0)
             return plane
 
-        def zeroed_window(name, after=None):
-            window = alloc([P, T], F32, name, after)
+        def zeroed(window):
             nc.gpsimd.memset(window[:], 0.0)
             return window
+
+        def zeroed_window(name, after=None):
+            return zeroed(alloc([P, T], F32, name, after))
 
         def live_rows(plane, q):
             return plane[QUADRANT * q : QUADRANT * q + PACK, :]
@@ -284,7 +287,7 @@ def tile_list_pass_arbitration_scores_kernel(
                     sums[c][:].rearrange("p (s i u e) -> p s u i e", s=TILES, u=2, e=2),
                 )
 
-        results = [zeroed_window("result_0", "contest_3_1"), zeroed_window("result_1", "second_loads")]
+        second_result = zeroed_window("result_1", "contest_3_1")
         wgo_sb = load(wgo, [P, S], "wgo_sb", "w1_plane_2")
         prios = [load(prio[P * n : P * (n + 1), :], [P, S], "prio_%d" % n, "board_%d" % n) for n in range(OUT_BLOCKS)]
         w3_codes = alloc([P, N], U32, "w3_codes", "w1_codes_2")
@@ -310,22 +313,30 @@ def tile_list_pass_arbitration_scores_kernel(
             )
 
         half_chunk = BANK // 2
-        grouped_after = ("a_sq_2_0", "a_sq_2_1", "v_words_1_0", "w1_first")
+        grouped_after = ("a_sq_2_0", "a_sq_2_1", "v_words_1_0")
+        row_bytes = 4 * T
         scalar_chunk = 1
-        for c in range(CHUNKS):
-            z_grouped = alloc([P, BANK, PACK], BF16, "z_grouped_%d" % c, grouped_after[c])
+        pair_banks = [bank(index, "pair_bank") for index in range(2 * CHUNKS)]
+        for index, pair_bank in enumerate(pair_banks):
+            c, half = divmod(index, 2)
             z_pairs = z_turned[c][:].rearrange("p s u r e -> p (s u r e)").bitcast(F32)
+            for i in range(TILES):
+                nc.tensor.transpose(
+                    pair_bank[:, P * i : P * (i + 1)],
+                    z_pairs[:, BANK * half + P * i : BANK * half + P * (i + 1)],
+                    ident[:],
+                )
+        for c in range(CHUNKS):
+            if c < CHUNKS - 1:
+                z_grouped = alloc([P, BANK, PACK], BF16, "z_grouped_%d" % c, grouped_after[c])
+            else:
+                z_grouped = placed_by_hand.tile(
+                    [P, BANK, PACK], BF16, name="z_grouped_last", offset=row_bytes - BANK * PACK, align_bytes=64
+                )
             for half in range(2):
-                pair_bank = bank(LOW + 2 * c + half, "pair_bank")
-                for i in range(TILES):
-                    nc.tensor.transpose(
-                        pair_bank[:, P * i : P * (i + 1)],
-                        z_pairs[:, BANK * half + P * i : BANK * half + P * (i + 1)],
-                        ident[:],
-                    )
                 dst = z_grouped[:, half_chunk * half : half_chunk * (half + 1), :]
                 dst = dst.rearrange("p c j -> p (c j)").bitcast(F32).rearrange("p (s c u) -> p s c u", s=2, u=2)
-                src = pair_bank[:].rearrange("p (s u c) -> p s c u", s=2, u=2)
+                src = pair_banks[2 * c + half][:].rearrange("p (s u c) -> p s c u", s=2, u=2)
                 if half == 0 or c == scalar_chunk:
                     nc.scalar.copy(dst, src)
                 else:
@@ -345,22 +356,26 @@ def tile_list_pass_arbitration_scores_kernel(
                 )
                 score(0, c, LOW + c if i == 0 else LOW, count * i, count)
 
+        last_result = zeroed(placed_by_hand.tile([P, T], F32, name="result_2", offset=0, align_bytes=64))
+        first_result = zeroed(placed_by_hand.tile([P, T], F32, name="result_0", offset=row_bytes, align_bytes=64))
+        results = (first_result, second_result, last_result)
+
         gates.append(alloc([P, T], F32, "gates_1", "z_turned_3"))
-        gates.append(alloc([P, T], F32, "gates_2", "tab_words_0"))
-        for n in range(1, OUT_BLOCKS):
-            for c in range(CHUNKS):
-                score(n, c, (HIGH if n == 1 else LOW) + c)
+        for c in range(CHUNKS):
+            score(1, c, HIGH + c)
 
         picked_gates = []
 
         def pick(n):
-            after = ("b_sq_3_0", "b_sq_3_1", "picked_gates_0")[n]
+            after = ("b_sq_3_0", "b_sq_3_1", "a_sq_3_0")[n]
             picked_gate = alloc([P, S], F32, "picked_gates_%d" % n, after)
             nc.vector.tensor_tensor(picked_gate[:], gates[n][:].indirect(idx3[:]), prios[n][:], ALU.mult)
             picked_gates.append(picked_gate)
 
         pick(0)
-        results.append(zeroed_window("result_2", "gates_0"))
+        gates.append(alloc([P, T], F32, "gates_2", "prio_0"))
+        for c in range(CHUNKS):
+            score(2, c, HIGH + c)
         for n in range(OUT_BLOCKS):
             if n + 1 < OUT_BLOCKS:
                 pick(n + 1)

@@ -1,3 +1,4 @@
+import math
 from contextlib import ExitStack
 
 import concourse.mybir as mybir
@@ -29,11 +30,11 @@ ROW_BLOCKS = H // P
 OUT_BLOCKS = N // P
 CHUNKS = T // BANK
 TILES = BANK // P
-SCALE_ROW0 = P - PASSES * K_PASS // 32
 LOW, HIGH = 0, 4
 PIECES = ((256, 256, 512), (512, 512), (512, 512), (512, 512))
-FUSED_PIECES = 2
 PAGES = 3
+ALIGN = 64
+ITEM_BYTES = {F32: 4, I32: 4, U32: 4, BF16: 2, U8: 1}
 
 
 def tile_list_pass_arbitration_scores_kernel(
@@ -42,25 +43,32 @@ def tile_list_pass_arbitration_scores_kernel(
 ):
     nc = tc.nc
     with ExitStack() as ctx:
+        lists = ctx.enter_context(tc.tile_pool(name="lists", bufs=1))
         sbuf = ctx.enter_context(tc.tile_pool(name="sbuf", bufs=1))
-        placed_by_hand = ctx.enter_context(tc.tile_pool(name="placed_by_hand", bufs=1))
         psum = ctx.enter_context(tc.psum_pool(name="psum", bufs=1))
-        place = {}
+        place = {"free": 0}
 
-        def alloc(shape, dtype, name, after=None):
-            place[name] = place[after] if after else name
-            return sbuf.tile(shape, dtype, name=name, tag=place[name], align_bytes=64)
+        def reserve(name, size):
+            place[name] = place["free"]
+            place["free"] = place[name] + -(-size // ALIGN) * ALIGN
+
+        def alloc(shape, dtype, name, after=None, at=0):
+            if after:
+                place[name] = place[after] + at
+            else:
+                reserve(name, math.prod(shape[1:]) * ITEM_BYTES[dtype])
+            return sbuf.tile(shape, dtype, name=name, offset=place[name], align_bytes=ALIGN)
 
         def bank(index, name):
             return psum.tile([P, BANK], F32, name=name, tag="bank%d" % index)
 
         def load_list(src, name):
-            dst = alloc([P, S // GROUP], U16, name)
+            dst = lists.tile([P, S // GROUP], U16, name=name)
             nc.sync.dma_start(dst[:], src)
             return dst
 
-        def load(src, shape, name, after):
-            dst = alloc(shape, F32, name, after)
+        def load(src, shape, name, after, at=0):
+            dst = alloc(shape, F32, name, after, at)
             nc.sync.dma_start(dst[:], src)
             return dst
 
@@ -69,12 +77,10 @@ def tile_list_pass_arbitration_scores_kernel(
             engine.memset(plane[:].bitcast(I32), 0)
             return plane
 
-        def zeroed(window):
+        def zeroed_window(name, after=None, at=0):
+            window = alloc([P, T], F32, name, after, at)
             nc.gpsimd.memset(window[:], 0.0)
             return window
-
-        def zeroed_window(name, after=None):
-            return zeroed(alloc([P, T], F32, name, after))
 
         def live_rows(plane, q):
             return plane[QUADRANT * q : QUADRANT * q + PACK, :]
@@ -84,15 +90,14 @@ def tile_list_pass_arbitration_scores_kernel(
             nc.sync.dma_start(words[:].bitcast(I32), tab_words[a].rearrange("p t i -> p (t i)").bitcast(I32))
             return words
 
-        def load_w1(dst, first, last):
-            views = []
+        def load_w1(name, first, last, after, at, pitch):
+            tiles = []
             for a in range(PASSES):
+                dst = alloc([P, PACK, last - first], F32, "%s_%d" % (name, a), after, at + pitch * a)
                 src = w1[K_PASS * a : K_PASS * (a + 1), first:last].rearrange("(p j) c -> p j c", j=PACK)
-                size = PACK * (last - first)
-                view = dst[:, size * a : size * (a + 1)].rearrange("p (j c) -> p j c", j=PACK)
-                nc.sync.dma_start(view, src)
-                views.append(view)
-            return views
+                nc.sync.dma_start(dst[:], src)
+                tiles.append(dst)
+            return tiles
 
         w2_plane = zeroed_plane(nc.gpsimd, PASSES * H, "w2_plane")
         for q in range(QUADRANTS):
@@ -106,165 +111,140 @@ def tile_list_pass_arbitration_scores_kernel(
         nc.scalar.activation(table_warmup[:], warmup_in[:], ACT.Sigmoid)
 
         idx = load_list(offs, "idx")
-        tab_plane = alloc([P, T], U8, "tab_plane")
-        nc.sync.dma_start(
-            tab_plane[SCALE_ROW0:P, :].bitcast(I32), tab_scales.rearrange("a q c -> q a c").bitcast(I32)
-        )
-        nc.vector.memset(tab_plane[0:SCALE_ROW0, :].bitcast(I32), 0)
-        tab_tiles = [load_table_pass(a) for a in range(PASSES)]
-        w1_first = alloc([P, PASSES * PACK * P], F32, "w1_first")
-        w1_loads = [load_w1(w1_first, 0, P)]
+        reserve("w1_room", 4 * PASSES * PACK * 2 * P)
+        w1_raw = [load_w1("w1_raw_0", 0, P, "w1_room", 0, 4 * S)]
+        reserve("second_room", 16 * S)
+        reserve("board_room", 4 * T)
+        tab_plane = alloc([P, T], U8, "tab_plane", "board_room")
+        nc.vector.memset(tab_plane[:].bitcast(I32), 0)
+        for q in range(QUADRANTS):
+            nc.sync.dma_start(
+                tab_plane[QUADRANT * q : QUADRANT * q + PASSES * PACK, :].bitcast(I32),
+                tab_scales[:, PACK * q : PACK * (q + 1), :].bitcast(I32),
+            )
+        tab_tiles = [load_table_pass(0)]
         w2_codes = alloc([P, PASSES, 2 * H], U8, "w2_codes")
         nc.sync.dma_start(w2_codes[:].bitcast(I32), w2_words.rearrange("a p c -> p a c").bitcast(I32))
-        idx2 = load_list(offs2, "idx2")
+        tab_tiles.append(load_table_pass(1))
+        idx2, idx3, idx4 = load_list(offs2, "idx2"), load_list(offs3, "idx3"), load_list(offs4, "idx4")
 
-        pages = [zeroed_window("page_0")]
         ident = alloc([P, P], F32, "ident")
         make_identity(nc, ident[:])
+        pages = [zeroed_window("page_%d" % b) for b in range(2)]
 
-        v_plane = zeroed_plane(nc.vector, PASSES * S, "v_plane")
+        moved_scales = zeroed_plane(nc.vector, S, "moved_scales")
         picked_scales = alloc([P, S], U8, "picked_scales")
         nc.vector.tensor_copy(picked_scales[:], tab_plane[:].indirect(idx[:]))
-        quadrant_rows = PASSES * PACK
-        for q in range(QUADRANTS):
-            nc.scalar.dma_start(
-                live_rows(v_plane, q).bitcast(I32),
-                picked_scales[SCALE_ROW0 + quadrant_rows * q : SCALE_ROW0 + quadrant_rows * (q + 1), :].bitcast(I32),
-            )
+        span = QUADRANT * (QUADRANTS - 1) + PACK
+        nc.sync.dma_start(moved_scales[0:span, :].bitcast(I32), picked_scales[PACK : PACK + span, :].bitcast(I32))
 
-        v_words = {}
-        half_columns = BANK // GROUP
+        v_words = [alloc([P, S], U32, "v_words_%d" % a) for a in range(PASSES)]
 
-        def pick_words(a, h, after=None):
-            picked = alloc([P, BANK], U32, "v_words_%d_%d" % (a, h), after)
-            entries = idx[:, half_columns * h : half_columns * (h + 1)]
-            nc.vector.tensor_copy(picked[:], tab_tiles[a][:].indirect(entries))
-            v_words[(a, h)] = picked
+        def pick_words(a, first, last):
+            entries = idx[:, first // GROUP : last // GROUP]
+            nc.vector.tensor_copy(v_words[a][:, first:last], tab_tiles[a][:].indirect(entries))
 
-        def cast_w1(views, name, after=None):
-            grouped = alloc([P, len(views), views[0].shape[2], PACK], BF16, name, after)
-            for i, view in enumerate(views):
+        def cast_w1(b, raw, column0, grouped=None):
+            if grouped is None:
+                grouped = alloc([P, PASSES, P, PACK], BF16, "w1_grouped_%d" % b)
+            for a in range(PASSES):
                 nc.scalar.copy(
-                    grouped[:, i, :, :].rearrange("p (c i) j -> p c j i", i=4),
-                    view.rearrange("p j (c i) -> p c j i", i=4),
+                    grouped[:, a, :, :].rearrange("p (c i) j -> p c j i", i=4),
+                    raw[a][:, :, column0 : column0 + P].rearrange("p j (c i) -> p c j i", i=4),
                 )
             return grouped
 
-        def quantise_w1(codes, plane, grouped):
+        def quantise_w1(b, grouped, after=None, plane_after=None):
+            codes = alloc([P, PASSES * P], U32, "w1_codes_%d" % b, after)
+            plane = alloc([P, PASSES * P], U8, "w1_plane_%d" % b, plane_after)
             nc.vector.quantize_mx(
-                out=codes.bitcast(FP8X4), scales=plane, in_=grouped[:].rearrange("p a c j -> p (a c j)")
+                out=codes[:].bitcast(FP8X4), scales=plane[:], in_=grouped[:].rearrange("p a c j -> p (a c j)")
             )
-
-        first_codes = alloc([P, PASSES * P], U32, "w1_codes_0")
-        first_plane = alloc([P, PASSES * P], U8, "w1_plane_0")
-        pick_words(0, 0)
-        pick_words(0, 1)
-        pick_words(1, 0)
-        for a, name in enumerate(("w1_grouped_0a", "w1_grouped_0")):
-            columns = slice(P * a, P * (a + 1))
-            quantise_w1(first_codes[:, columns], first_plane[:, columns], cast_w1(w1_loads[0][a : a + 1], name))
-        pick_words(1, 1, "w1_grouped_0")
-
-        w1_block = PASSES * PACK * P
-        second_loads = alloc([P, S + 3 * w1_block], F32, "second_loads", "tab_plane")
-        wgs_sb = second_loads[:, 0:S]
-        nc.sync.dma_start(wgs_sb, wgs)
-        w1_loads.append(load_w1(second_loads[:, S : S + w1_block], P, 2 * P))
-        w1_loads.append(load_w1(second_loads[:, S + w1_block :], 2 * P, H))
-        idx3 = load_list(offs3, "idx3")
-        idx4 = load_list(offs4, "idx4")
-
-        pages.append(zeroed_window("page_1", "tab_words_1"))
-
-        squares = []
-
-        def project(b, codes, plane, stride, column0):
-            squares.append([])
-            for i, width in enumerate(PIECES[b]):
-                start = sum(PIECES[b][:i])
-                h, first = divmod(start, BANK)
-                bank0 = HIGH + 2 * (sum(len(block) for block in squares) % 2)
-                a_bank, b_bank = bank(bank0, "a_bank"), bank(bank0 + 1, "b_bank")
-                for a in range(PASSES):
-                    nc.tensor.matmul_mx(
-                        out=a_bank[:, 0:width],
-                        lhsT=codes[:, stride * a + column0 : stride * a + column0 + P].bitcast(FP8X4),
-                        lhsT_scale=plane[:, stride * a + column0 : stride * a + column0 + P],
-                        rhs=v_words[(a, h)][:, first : first + width].bitcast(FP8X4),
-                        rhs_scale=v_plane[:, S * a + start : S * a + start + width],
-                        start=(a == 0),
-                        stop=(a == PASSES - 1),
-                    )
-                step = BANK if width == BANK else P
-                for offset in range(0, width, step):
-                    for a in range(PASSES):
-                        nc.tensor.matmul_mx(
-                            out=b_bank[:, offset : offset + step],
-                            lhsT=w2_codes[:, a, 2 * P * b : 2 * P * (b + 1)].bitcast(FP4X4),
-                            lhsT_scale=w2_plane[:, H * a + P * b : H * a + P * (b + 1)],
-                            rhs=v_words[(a, h)][:, first + offset : first + offset + step].bitcast(FP8X4),
-                            rhs_scale=v_plane[:, S * a + start + offset : S * a + start + offset + step],
-                            start=(a == 0),
-                            stop=(a == PASSES - 1),
-                        )
-                piece_squares = tuple(alloc([P, width], F32, "%s_sq_%d_%d" % (x, b, i)) for x in "ab")
-                for square, source in zip(piece_squares, (a_bank, b_bank)):
-                    nc.scalar.activation(square[:], source[:, 0:width], ACT.Square)
-                squares[b].append(piece_squares)
-
-        def place_piece(b, i, contest_after=None, placed_after=None):
-            width, start = PIECES[b][i], sum(PIECES[b][:i])
-            engine = nc.vector if b == 0 else nc.gpsimd
-            a_sq, b_sq = squares[b][i]
-            contest = alloc([P, width], F32, "contest_%d_%d" % (b, i), contest_after)
-            engine.tensor_tensor(contest[:], a_sq[:], b_sq[:], ALU.subtract)
-            entries = idx2[:, start // GROUP : (start + width) // GROUP]
-            window, weight = pages[b % PAGES][:].indirect(entries), wgs_sb[:, start : start + width]
-            if b == 0 and i < FUSED_PIECES:
-                nc.vector.tensor_tensor(window, contest[:], weight, ALU.mult)
-            else:
-                placed = alloc([P, width], F32, "placed_%d_%d" % (b, i), placed_after)
-                engine.tensor_tensor(placed[:], contest[:], weight, ALU.mult)
-                nc.vector.tensor_copy(window, placed[:])
-
-        def quantised_w1(grouped, b, codes_after=None):
-            columns = PASSES * grouped.shape[2]
-            codes = alloc([P, columns], U32, "w1_codes_%d" % b, codes_after)
-            plane = alloc([P, columns], U8, "w1_plane_%d" % b)
-            quantise_w1(codes[:], plane[:], grouped)
             return codes, plane
 
-        project(0, first_codes, first_plane, P, 0)
-        place_piece(0, 0)
-        pages.append(zeroed_window("page_2", "b_sq_0_0"))
-        place_piece(0, 1)
-        second_grouped = cast_w1(w1_loads[1], "w1_grouped_1", "a_sq_0_0")
-        last_grouped = cast_w1(w1_loads[2], "w1_grouped_2")
-        project(1, *quantised_w1(second_grouped, 1), P, 0)
-        place_piece(0, 2, "w1_grouped_1")
-        last_codes, last_plane = quantised_w1(last_grouped, 2, "placed_0_2")
-        project(2, last_codes, last_plane, 2 * P, 0)
-        project(3, last_codes, last_plane, 2 * P, P)
+        w1_mx = [quantise_w1(0, cast_w1(0, w1_raw[0], 0), "board_room")]
+        pick_words(0, 0, S // 2)
+        pick_words(0, S // 2, S)
+        for first, last in ((0, 256), (256, 512), (512, S)):
+            pick_words(1, first, last)
 
-        w3_plane = zeroed_plane(nc.gpsimd, N, "w3_plane", "a_sq_0_1")
-        for q in range(QUADRANTS):
-            nc.sync.dma_start(
-                live_rows(w3_plane, q).bitcast(I32), w3_scales[0, PACK * q : PACK * (q + 1), :].bitcast(I32)
+        half = S // 2
+        w1_raw.append(load_w1("w1_raw_1", P, 2 * P, "second_room", 4 * S, 2 * S))
+        wgs_halves = [load(wgs[:, 0:half], [P, half], "wgs_0", "second_room")]
+        wgs_halves.append(load(wgs[:, half:S], [P, half], "wgs_1", "second_room", 4 * half))
+        w1_raw.append(load_w1("w1_raw_2", 2 * P, H, "second_room", 8 * S, 4 * S))
+
+        pieces = [(b, sum(widths[:i]), width) for b, widths in enumerate(PIECES) for i, width in enumerate(widths)]
+        squares = {}
+
+        def project(k, after=None):
+            b, start, width = pieces[k]
+            codes, plane = w1_mx[b]
+            bank0 = HIGH + 2 * (k % 2)
+            a_bank, b_bank = bank(bank0, "a_bank"), bank(bank0 + 1, "b_bank")
+            step = BANK if width == BANK else P
+            for a in range(PASSES):
+                nc.tensor.matmul_mx(
+                    out=a_bank[:, 0:width],
+                    lhsT=codes[:, P * a : P * (a + 1)].bitcast(FP8X4),
+                    lhsT_scale=plane[:, P * a : P * (a + 1)],
+                    rhs=v_words[a][:, start : start + width].bitcast(FP8X4),
+                    rhs_scale=picked_scales[PACK * a : P, start : start + width],
+                    start=(a == 0),
+                    stop=(a == PASSES - 1),
+                )
+                for offset in range(0, width, step):
+                    entries = slice(start + offset, start + offset + step)
+                    nc.tensor.matmul_mx(
+                        out=b_bank[:, offset : offset + step],
+                        lhsT=w2_codes[:, a, 2 * P * b : 2 * P * (b + 1)].bitcast(FP4X4),
+                        lhsT_scale=w2_plane[:, H * a + P * b : H * a + P * (b + 1)],
+                        rhs=v_words[a][:, entries].bitcast(FP8X4),
+                        rhs_scale=(picked_scales, moved_scales)[a][:, entries],
+                        start=(a == 0 and offset == 0),
+                        stop=(a == PASSES - 1 and offset + step == width),
+                    )
+            squares[k] = tuple(
+                alloc([P, width], F32, "%s_sq_%d" % (x, k), after, 4 * width * i) for i, x in enumerate("ba")
             )
+            for square, source in reversed(list(zip(squares[k], (b_bank, a_bank)))):
+                nc.scalar.activation(square[:], source[:, 0:width], ACT.Square)
 
-        contest_chain = ["contest_0_2", "w1_grouped_2"]
-        placed_chain = [None, None, None]
-        board_after = ("w1_codes_0", "w1_plane_1", "v_words_0_1", "v_words_1_1")
-        z_turned = [alloc([P, TILES, 2, P, 2], BF16, "z_turned_%d" % c) for c in range(CHUNKS)]
-        for b in range(ROW_BLOCKS):
+        contests, placeds = {}, {}
+
+        def subtract(k, after=None):
+            engine = nc.vector if k < 2 else nc.gpsimd
+            b_sq, a_sq = squares[k]
+            contests[k] = alloc([P, pieces[k][2]], F32, "contest_%d" % k, after)
+            engine.tensor_tensor(contests[k][:], a_sq[:], b_sq[:], ALU.subtract)
+
+        def weigh(k, after=None):
+            engine = nc.vector if k < 2 else nc.gpsimd
+            b, start, width = pieces[k]
+            placeds[k] = alloc([P, width], F32, "placed_%d" % k, after)
+            weight = wgs_halves[start // half][:, start % half : start % half + width]
+            engine.tensor_tensor(placeds[k][:], contests[k][:], weight, ALU.mult)
+
+        def scatter(k):
+            b, start, width = pieces[k]
+            window = pages[b % PAGES][:].indirect(idx2[:, start // GROUP : (start + width) // GROUP])
+            nc.vector.tensor_copy(window, placeds[k][:])
+
+        def place_piece(k, contest_after=None, placed_after=None):
+            subtract(k, contest_after)
+            weigh(k, placed_after)
+            scatter(k)
+
+        reserve("gates_room", 4 * T)
+        z_turned = [
+            alloc([P, TILES, 2, P, 2], BF16, "z_turned_%d" % c, "gates_room" if c == CHUNKS - 1 else None)
+            for c in range(CHUNKS)
+        ]
+
+        def add_board(b, board_after):
             page = pages[b % PAGES]
             last_block = b == ROW_BLOCKS - 1
-            if b > 0:
-                for i in range(len(PIECES[b])):
-                    place_piece(b, i, contest_chain[-2], placed_chain[-3])
-                    contest_chain.append("contest_%d_%d" % (b, i))
-                    placed_chain.append("placed_%d_%d" % (b, i))
-            board_sb = load(board[P * b : P * (b + 1), :], [P, T], "board_%d" % b, board_after[b])
+            board_sb = load(board[P * b : P * (b + 1), :], [P, T], "board_%d" % b, board_after)
             banks = HIGH if last_block else LOW
             sums = [bank(banks + c, "z_bank") for c in range(CHUNKS)]
             for c in range(CHUNKS):
@@ -287,10 +267,57 @@ def tile_list_pass_arbitration_scores_kernel(
                     sums[c][:].rearrange("p (s i u e) -> p s u i e", s=TILES, u=2, e=2),
                 )
 
-        second_result = zeroed_window("result_1", "contest_3_1")
-        wgo_sb = load(wgo, [P, S], "wgo_sb", "w1_plane_2")
-        prios = [load(prio[P * n : P * (n + 1), :], [P, S], "prio_%d" % n, "board_%d" % n) for n in range(OUT_BLOCKS)]
-        w3_codes = alloc([P, N], U32, "w3_codes", "w1_codes_2")
+        reserve("contest_room", 4 * BANK)
+        reserve("second_contest_room", 4 * BANK)
+        project(0)
+        project(1)
+        subtract(0, "contest_room")
+        subtract(1, "second_contest_room")
+        weigh(0)
+        scatter(0)
+        grouped = cast_w1(1, w1_raw[1], 0)
+        project(2, "w1_raw_1_0")
+        w1_mx.append(quantise_w1(1, grouped, None, "w1_room"))
+        weigh(1, "w1_grouped_1")
+        scatter(1)
+        pages.append(zeroed_window("page_2", "tab_words_0"))
+        last_grouped = alloc([P, 2, PASSES, P, PACK], BF16, "w1_grouped_2")
+        for i in range(2):
+            cast_w1(2 + i, w1_raw[2], P * i, last_grouped[:, i])
+        project(3)
+        project(4, "w1_raw_2_0")
+        place_piece(2, "contest_room", "contest_1")
+        codes = alloc([P, 2 * PASSES * P], U32, "w1_codes_2")
+        plane = alloc([P, 2 * PASSES * P], U8, "w1_plane_2")
+        nc.vector.quantize_mx(
+            out=codes[:].bitcast(FP8X4), scales=plane[:], in_=last_grouped[:].rearrange("p b a c j -> p (b a c j)")
+        )
+        for i in range(2):
+            columns = slice(PASSES * P * i, PASSES * P * (i + 1))
+            w1_mx.append((codes[:, columns], plane[:, columns]))
+        for k in range(5, 9):
+            project(k)
+        contest_chain = ["contest_2", "w1_grouped_2"]
+        placed_chain = ["w1_raw_2_1", None, None]
+        board_after = ("tab_words_1", "board_room", "w1_room", "board_0")
+        for b in range(ROW_BLOCKS):
+            if b > 0:
+                for k in (2 * b + 1, 2 * b + 2):
+                    place_piece(k, contest_chain[-2], placed_chain[-3])
+                    contest_chain.append("contest_%d" % k)
+                    placed_chain.append("placed_%d" % k)
+            add_board(b, board_after[b])
+
+        second_result = zeroed_window("result_1", "second_room")
+        wgo_sb = load(wgo, [P, S], "wgo_sb", "v_words_0")
+        prio_places = (("board_1", 0), ("board_2", 0), ("board_2", 4 * S))
+        prios = [load(prio[P * n : P * (n + 1), :], [P, S], "prio_%d" % n, *prio_places[n]) for n in range(OUT_BLOCKS)]
+        w3_plane = zeroed_plane(nc.gpsimd, N, "w3_plane", "b_sq_3")
+        for q in range(QUADRANTS):
+            nc.sync.dma_start(
+                live_rows(w3_plane, q).bitcast(I32), w3_scales[0, PACK * q : PACK * (q + 1), :].bitcast(I32)
+            )
+        w3_codes = alloc([P, N], U32, "w3_codes", "v_words_1")
         nc.sync.dma_start(w3_codes[:].bitcast(I32), w3_words[0].rearrange("p c i -> p (c i)").bitcast(I32))
 
         z_codes, z_planes = [], []
@@ -313,7 +340,7 @@ def tile_list_pass_arbitration_scores_kernel(
             )
 
         half_chunk = BANK // 2
-        grouped_after = ("a_sq_2_0", "a_sq_2_1", "v_words_1_0")
+        grouped_after = ("b_sq_4", "b_sq_5", "b_sq_6")
         row_bytes = 4 * T
         scalar_chunk = 1
         pair_banks = [bank(index, "pair_bank") for index in range(2 * CHUNKS)]
@@ -330,9 +357,8 @@ def tile_list_pass_arbitration_scores_kernel(
             if c < CHUNKS - 1:
                 z_grouped = alloc([P, BANK, PACK], BF16, "z_grouped_%d" % c, grouped_after[c])
             else:
-                z_grouped = placed_by_hand.tile(
-                    [P, BANK, PACK], BF16, name="z_grouped_last", offset=row_bytes - BANK * PACK, align_bytes=64
-                )
+                reserve("result_room", 2 * row_bytes)
+                z_grouped = alloc([P, BANK, PACK], BF16, "z_grouped_last", "result_room", row_bytes - BANK * PACK)
             for half in range(2):
                 dst = z_grouped[:, half_chunk * half : half_chunk * (half + 1), :]
                 dst = dst.rearrange("p c j -> p (c j)").bitcast(F32).rearrange("p (s c u) -> p s c u", s=2, u=2)
@@ -356,8 +382,8 @@ def tile_list_pass_arbitration_scores_kernel(
                 )
                 score(0, c, LOW + c if i == 0 else LOW, count * i, count)
 
-        last_result = zeroed(placed_by_hand.tile([P, T], F32, name="result_2", offset=0, align_bytes=64))
-        first_result = zeroed(placed_by_hand.tile([P, T], F32, name="result_0", offset=row_bytes, align_bytes=64))
+        last_result = zeroed_window("result_2", "result_room")
+        first_result = zeroed_window("result_0", "result_room", row_bytes)
         results = (first_result, second_result, last_result)
 
         gates.append(alloc([P, T], F32, "gates_1", "z_turned_3"))
@@ -367,7 +393,7 @@ def tile_list_pass_arbitration_scores_kernel(
         picked_gates = []
 
         def pick(n):
-            after = ("b_sq_3_0", "b_sq_3_1", "a_sq_3_0")[n]
+            after = ("b_sq_7", "b_sq_8", "z_turned_0")[n]
             picked_gate = alloc([P, S], F32, "picked_gates_%d" % n, after)
             nc.vector.tensor_tensor(picked_gate[:], gates[n][:].indirect(idx3[:]), prios[n][:], ALU.mult)
             picked_gates.append(picked_gate)

@@ -30,9 +30,10 @@ ROW_BLOCKS = H // P
 OUT_BLOCKS = N // P
 CHUNKS = T // BANK
 TILES = BANK // P
+SCALE_ROW0 = P - PASSES * K_PASS // 32
 LOW, HIGH = 0, 4
 PIECES = ((256, 256, 512), (512, 512), (512, 512), (512, 512))
-PAGES = 3
+PAGES = 2
 ALIGN = 64
 ITEM_BYTES = {F32: 4, I32: 4, U32: 4, BF16: 2, U8: 1}
 
@@ -111,32 +112,33 @@ def tile_list_pass_arbitration_scores_kernel(
         nc.scalar.activation(table_warmup[:], warmup_in[:], ACT.Sigmoid)
 
         idx = load_list(offs, "idx")
-        reserve("w1_room", 4 * PASSES * PACK * 2 * P)
-        w1_raw = [load_w1("w1_raw_0", 0, P, "w1_room", 0, 4 * S)]
         reserve("second_room", 16 * S)
         reserve("board_room", 4 * T)
-        tab_plane = alloc([P, T], U8, "tab_plane", "board_room")
-        nc.vector.memset(tab_plane[:].bitcast(I32), 0)
-        for q in range(QUADRANTS):
-            nc.sync.dma_start(
-                tab_plane[QUADRANT * q : QUADRANT * q + PASSES * PACK, :].bitcast(I32),
-                tab_scales[:, PACK * q : PACK * (q + 1), :].bitcast(I32),
-            )
+        tab_plane = alloc([P, T], U8, "tab_plane")
+        nc.sync.dma_start(
+            tab_plane[SCALE_ROW0:P, :].bitcast(I32), tab_scales.rearrange("a q c -> q a c").bitcast(I32)
+        )
+        nc.vector.memset(tab_plane[0:SCALE_ROW0, :].bitcast(I32), 0)
         tab_tiles = [load_table_pass(0)]
+        reserve("w1_room", 4 * PASSES * PACK * 2 * P)
+        w1_raw = [load_w1("w1_raw_0", 0, P, "w1_room", 0, 4 * S)]
         w2_codes = alloc([P, PASSES, 2 * H], U8, "w2_codes")
         nc.sync.dma_start(w2_codes[:].bitcast(I32), w2_words.rearrange("a p c -> p a c").bitcast(I32))
         tab_tiles.append(load_table_pass(1))
-        idx2, idx3, idx4 = load_list(offs2, "idx2"), load_list(offs3, "idx3"), load_list(offs4, "idx4")
 
         ident = alloc([P, P], F32, "ident")
         make_identity(nc, ident[:])
-        pages = [zeroed_window("page_%d" % b) for b in range(2)]
+        pages = [zeroed_window("page_%d" % b) for b in range(1)]
 
-        moved_scales = zeroed_plane(nc.vector, S, "moved_scales")
+        v_plane = zeroed_plane(nc.vector, PASSES * S, "v_plane")
         picked_scales = alloc([P, S], U8, "picked_scales")
         nc.vector.tensor_copy(picked_scales[:], tab_plane[:].indirect(idx[:]))
-        span = QUADRANT * (QUADRANTS - 1) + PACK
-        nc.sync.dma_start(moved_scales[0:span, :].bitcast(I32), picked_scales[PACK : PACK + span, :].bitcast(I32))
+        quadrant_rows = PASSES * PACK
+        for q in range(QUADRANTS):
+            nc.scalar.dma_start(
+                live_rows(v_plane, q).bitcast(I32),
+                picked_scales[SCALE_ROW0 + quadrant_rows * q : SCALE_ROW0 + quadrant_rows * (q + 1), :].bitcast(I32),
+            )
 
         v_words = [alloc([P, S], U32, "v_words_%d" % a) for a in range(PASSES)]
 
@@ -162,17 +164,19 @@ def tile_list_pass_arbitration_scores_kernel(
             )
             return codes, plane
 
+        pick_words(0, 0, S)
         w1_mx = [quantise_w1(0, cast_w1(0, w1_raw[0], 0), "board_room")]
-        pick_words(0, 0, S // 2)
-        pick_words(0, S // 2, S)
         for first, last in ((0, 256), (256, 512), (512, S)):
             pick_words(1, first, last)
 
+        pages.append(zeroed_window("page_1", "tab_words_1"))
         half = S // 2
         w1_raw.append(load_w1("w1_raw_1", P, 2 * P, "second_room", 4 * S, 2 * S))
         wgs_halves = [load(wgs[:, 0:half], [P, half], "wgs_0", "second_room")]
+        idx2 = load_list(offs2, "idx2")
         wgs_halves.append(load(wgs[:, half:S], [P, half], "wgs_1", "second_room", 4 * half))
         w1_raw.append(load_w1("w1_raw_2", 2 * P, H, "second_room", 8 * S, 4 * S))
+        idx3, idx4 = load_list(offs3, "idx3"), load_list(offs4, "idx4")
 
         pieces = [(b, sum(widths[:i]), width) for b, widths in enumerate(PIECES) for i, width in enumerate(widths)]
         squares = {}
@@ -189,7 +193,7 @@ def tile_list_pass_arbitration_scores_kernel(
                     lhsT=codes[:, P * a : P * (a + 1)].bitcast(FP8X4),
                     lhsT_scale=plane[:, P * a : P * (a + 1)],
                     rhs=v_words[a][:, start : start + width].bitcast(FP8X4),
-                    rhs_scale=picked_scales[PACK * a : P, start : start + width],
+                    rhs_scale=v_plane[:, S * a + start : S * a + start + width],
                     start=(a == 0),
                     stop=(a == PASSES - 1),
                 )
@@ -200,7 +204,7 @@ def tile_list_pass_arbitration_scores_kernel(
                         lhsT=w2_codes[:, a, 2 * P * b : 2 * P * (b + 1)].bitcast(FP4X4),
                         lhsT_scale=w2_plane[:, H * a + P * b : H * a + P * (b + 1)],
                         rhs=v_words[a][:, entries].bitcast(FP8X4),
-                        rhs_scale=(picked_scales, moved_scales)[a][:, entries],
+                        rhs_scale=v_plane[:, S * a + entries.start : S * a + entries.stop],
                         start=(a == 0 and offset == 0),
                         stop=(a == PASSES - 1 and offset + step == width),
                     )
@@ -271,7 +275,7 @@ def tile_list_pass_arbitration_scores_kernel(
         reserve("second_contest_room", 4 * BANK)
         project(0)
         project(1)
-        subtract(0, "contest_room")
+        subtract(0)
         subtract(1, "second_contest_room")
         weigh(0)
         scatter(0)
@@ -280,15 +284,14 @@ def tile_list_pass_arbitration_scores_kernel(
         w1_mx.append(quantise_w1(1, grouped, None, "w1_room"))
         weigh(1, "w1_grouped_1")
         scatter(1)
-        pages.append(zeroed_window("page_2", "tab_words_0"))
         last_grouped = alloc([P, 2, PASSES, P, PACK], BF16, "w1_grouped_2")
         for i in range(2):
             cast_w1(2 + i, w1_raw[2], P * i, last_grouped[:, i])
         project(3)
         project(4, "w1_raw_2_0")
-        place_piece(2, "contest_room", "contest_1")
+        place_piece(2, "contest_1", "contest_room")
         codes = alloc([P, 2 * PASSES * P], U32, "w1_codes_2")
-        plane = alloc([P, 2 * PASSES * P], U8, "w1_plane_2")
+        plane = alloc([P, 2 * PASSES * P], U8, "w1_plane_2", "tab_words_0")
         nc.vector.quantize_mx(
             out=codes[:].bitcast(FP8X4), scales=plane[:], in_=last_grouped[:].rearrange("p b a c j -> p (b a c j)")
         )
@@ -299,7 +302,7 @@ def tile_list_pass_arbitration_scores_kernel(
             project(k)
         contest_chain = ["contest_2", "w1_grouped_2"]
         placed_chain = ["w1_raw_2_1", None, None]
-        board_after = ("tab_words_1", "board_room", "w1_room", "board_0")
+        board_after = ("board_room", "w1_room", "tab_words_0", "board_0")
         for b in range(ROW_BLOCKS):
             if b > 0:
                 for k in (2 * b + 1, 2 * b + 2):

@@ -32,7 +32,7 @@ CHUNKS = T // BANK
 TILES = BANK // P
 SCALE_ROW0 = P - PASSES * K_PASS // 32
 LOW, HIGH = 0, 4
-PIECES = ((256, 256, 512), (512, 512), (512, 512), (512, 512))
+PIECES = ((256, 256, 256, 256), (288, 320, 416), (512, 512), (1024,))
 PAGES = 2
 ALIGN = 64
 ITEM_BYTES = {F32: 4, I32: 4, U32: 4, BF16: 2, U8: 1}
@@ -169,22 +169,23 @@ def tile_list_pass_arbitration_scores_kernel(
         for first, last in ((0, 256), (256, 512), (512, S)):
             pick_words(1, first, last)
 
-        pages.append(zeroed_window("page_1", "tab_words_1"))
+        pages.append(zeroed_window("page_1", "tab_words_0"))
         half = S // 2
         w1_raw.append(load_w1("w1_raw_1", P, 2 * P, "second_room", 4 * S, 2 * S))
-        wgs_halves = [load(wgs[:, 0:half], [P, half], "wgs_0", "second_room")]
+        wgs_sb = alloc([P, S], F32, "wgs_sb", "second_room")
+        nc.sync.dma_start(wgs_sb[:, 0:half], wgs[:, 0:half])
         idx2 = load_list(offs2, "idx2")
-        wgs_halves.append(load(wgs[:, half:S], [P, half], "wgs_1", "second_room", 4 * half))
+        nc.sync.dma_start(wgs_sb[:, half:S], wgs[:, half:S])
         w1_raw.append(load_w1("w1_raw_2", 2 * P, H, "second_room", 8 * S, 4 * S))
         idx3, idx4 = load_list(offs3, "idx3"), load_list(offs4, "idx4")
 
         pieces = [(b, sum(widths[:i]), width) for b, widths in enumerate(PIECES) for i, width in enumerate(widths)]
-        squares = {}
+        runs = []
 
-        def project(k, after=None):
-            b, start, width = pieces[k]
+        def project(b, start, width, a_sq, b_sq):
             codes, plane = w1_mx[b]
-            bank0 = HIGH + 2 * (k % 2)
+            bank0 = HIGH + 2 * (len(runs) % 2)
+            runs.append((b, start, width))
             a_bank, b_bank = bank(bank0, "a_bank"), bank(bank0 + 1, "b_bank")
             step = BANK if width == BANK else P
             for a in range(PASSES):
@@ -208,25 +209,39 @@ def tile_list_pass_arbitration_scores_kernel(
                         start=(a == 0 and offset == 0),
                         stop=(a == PASSES - 1 and offset + step == width),
                     )
-            squares[k] = tuple(
-                alloc([P, width], F32, "%s_sq_%d" % (x, k), after, 4 * width * i) for i, x in enumerate("ba")
+            for square, source in ((a_sq, a_bank), (b_sq, b_bank)):
+                nc.scalar.activation(square, source[:, 0:width], ACT.Square)
+
+        squares = {}
+
+        def project_piece(k, a_place=(), b_place=()):
+            b, start, width = pieces[k]
+            squares[k] = (
+                alloc([P, width], F32, "a_sq_%d" % k, *a_place)[:], alloc([P, width], F32, "b_sq_%d" % k, *b_place)[:]
             )
-            for square, source in reversed(list(zip(squares[k], (b_bank, a_bank)))):
-                nc.scalar.activation(square[:], source[:, 0:width], ACT.Square)
+            project(b, start, width, *squares[k])
+
+        def project_block(b, places=((), ())):
+            tiles = [alloc([P, S], F32, "%s_sq_block_%d" % (x, b), *at) for x, at in zip("ab", places)]
+            for start in range(0, S, BANK):
+                project(b, start, BANK, *[tile[:, start : start + BANK] for tile in tiles])
+            for k, (block, start, width) in enumerate(pieces):
+                if block == b:
+                    squares[k] = [tile[:, start : start + width] for tile in tiles]
 
         contests, placeds = {}, {}
 
         def subtract(k, after=None):
-            engine = nc.vector if k < 2 else nc.gpsimd
-            b_sq, a_sq = squares[k]
+            engine = nc.vector if k == 0 else nc.gpsimd
+            a_sq, b_sq = squares[k]
             contests[k] = alloc([P, pieces[k][2]], F32, "contest_%d" % k, after)
-            engine.tensor_tensor(contests[k][:], a_sq[:], b_sq[:], ALU.subtract)
+            engine.tensor_tensor(contests[k][:], a_sq, b_sq, ALU.subtract)
 
         def weigh(k, after=None):
-            engine = nc.vector if k < 2 else nc.gpsimd
+            engine = nc.vector if k == 0 else nc.gpsimd
             b, start, width = pieces[k]
             placeds[k] = alloc([P, width], F32, "placed_%d" % k, after)
-            weight = wgs_halves[start // half][:, start % half : start % half + width]
+            weight = wgs_sb[:, start : start + width]
             engine.tensor_tensor(placeds[k][:], contests[k][:], weight, ALU.mult)
 
         def scatter(k):
@@ -271,41 +286,38 @@ def tile_list_pass_arbitration_scores_kernel(
                     sums[c][:].rearrange("p (s i u e) -> p s u i e", s=TILES, u=2, e=2),
                 )
 
-        reserve("contest_room", 4 * BANK)
-        reserve("second_contest_room", 4 * BANK)
-        project(0)
-        project(1)
-        subtract(0)
-        subtract(1, "second_contest_room")
-        weigh(0)
-        scatter(0)
+        for name in ("contest_room_0", "contest_room_1", "placed_room_0", "placed_room_1", "placed_room_2"):
+            reserve(name, 4 * S)
+        project_piece(0)
+        project_piece(1)
+        place_piece(0, "contest_room_0")
         grouped = cast_w1(1, w1_raw[1], 0)
-        project(2, "w1_raw_1_0")
         w1_mx.append(quantise_w1(1, grouped, None, "w1_room"))
-        weigh(1, "w1_grouped_1")
-        scatter(1)
+        place_piece(1, "contest_0", "w1_raw_1_1")
+        project_piece(2, ("w1_raw_1_0",), ("w1_raw_1_0", 4 * 256))
+        project_piece(3, ("w1_raw_1_1", 4 * 256))
+        place_piece(2, "w1_grouped_1", "placed_room_0")
         last_grouped = alloc([P, 2, PASSES, P, PACK], BF16, "w1_grouped_2")
         for i in range(2):
             cast_w1(2 + i, w1_raw[2], P * i, last_grouped[:, i])
-        project(3)
-        project(4, "w1_raw_2_0")
-        place_piece(2, "contest_1", "contest_room")
+        project_block(1)
+        place_piece(3, "contest_2", "placed_room_1")
         codes = alloc([P, 2 * PASSES * P], U32, "w1_codes_2")
-        plane = alloc([P, 2 * PASSES * P], U8, "w1_plane_2", "tab_words_0")
+        plane = alloc([P, 2 * PASSES * P], U8, "w1_plane_2", "tab_words_1")
         nc.vector.quantize_mx(
             out=codes[:].bitcast(FP8X4), scales=plane[:], in_=last_grouped[:].rearrange("p b a c j -> p (b a c j)")
         )
         for i in range(2):
             columns = slice(PASSES * P * i, PASSES * P * (i + 1))
             w1_mx.append((codes[:, columns], plane[:, columns]))
-        for k in range(5, 9):
-            project(k)
-        contest_chain = ["contest_2", "w1_grouped_2"]
-        placed_chain = ["w1_raw_2_1", None, None]
-        board_after = ("board_room", "w1_room", "tab_words_0", "board_0")
+        project_block(2)
+        project_block(3)
+        contest_chain = ["contest_room_0", "w1_grouped_2"]
+        placed_chain = ["w1_raw_2_1", "placed_room_0", "placed_room_1"]
+        board_after = ("board_room", "w1_room", "tab_words_1", "board_0")
         for b in range(ROW_BLOCKS):
-            if b > 0:
-                for k in (2 * b + 1, 2 * b + 2):
+            for k in range(len(PIECES[0]), len(pieces)):
+                if pieces[k][0] == b:
                     place_piece(k, contest_chain[-2], placed_chain[-3])
                     contest_chain.append("contest_%d" % k)
                     placed_chain.append("placed_%d" % k)
@@ -315,7 +327,7 @@ def tile_list_pass_arbitration_scores_kernel(
         wgo_sb = load(wgo, [P, S], "wgo_sb", "v_words_0")
         prio_places = (("board_1", 0), ("board_2", 0), ("board_2", 4 * S))
         prios = [load(prio[P * n : P * (n + 1), :], [P, S], "prio_%d" % n, *prio_places[n]) for n in range(OUT_BLOCKS)]
-        w3_plane = zeroed_plane(nc.gpsimd, N, "w3_plane", "b_sq_3")
+        w3_plane = zeroed_plane(nc.gpsimd, N, "w3_plane", "b_sq_block_1")
         for q in range(QUADRANTS):
             nc.sync.dma_start(
                 live_rows(w3_plane, q).bitcast(I32), w3_scales[0, PACK * q : PACK * (q + 1), :].bitcast(I32)
@@ -343,7 +355,7 @@ def tile_list_pass_arbitration_scores_kernel(
             )
 
         half_chunk = BANK // 2
-        grouped_after = ("b_sq_4", "b_sq_5", "b_sq_6")
+        grouped_after = ("a_sq_block_1", "a_sq_block_2", "b_sq_block_2")
         row_bytes = 4 * T
         scalar_chunk = 1
         pair_banks = [bank(index, "pair_bank") for index in range(2 * CHUNKS)]
@@ -396,7 +408,7 @@ def tile_list_pass_arbitration_scores_kernel(
         picked_gates = []
 
         def pick(n):
-            after = ("b_sq_7", "b_sq_8", "z_turned_0")[n]
+            after = ("a_sq_block_3", "b_sq_block_3", "z_turned_0")[n]
             picked_gate = alloc([P, S], F32, "picked_gates_%d" % n, after)
             nc.vector.tensor_tensor(picked_gate[:], gates[n][:].indirect(idx3[:]), prios[n][:], ALU.mult)
             picked_gates.append(picked_gate)

@@ -31,6 +31,7 @@ OUT_BLOCKS = N // P
 CHUNKS = T // BANK
 TILES = BANK // P
 SCALE_ROW0 = P - PASSES * K_PASS // 32
+HALF = P // 2
 LOW, HIGH = 0, 4
 PIECES = ((256, 256, 256, 256), (288, 320, 416), (512, 512), (1024,))
 PAGES = 2
@@ -73,8 +74,8 @@ def tile_list_pass_arbitration_scores_kernel(
             nc.sync.dma_start(dst[:], src)
             return dst
 
-        def zeroed_plane(engine, width, name, after=None):
-            plane = alloc([P, width], U8, name, after)
+        def zeroed_plane(engine, width, name, after=None, at=0):
+            plane = alloc([P, width], U8, name, after, at)
             engine.memset(plane[:].bitcast(I32), 0)
             return plane
 
@@ -128,7 +129,7 @@ def tile_list_pass_arbitration_scores_kernel(
 
         ident = alloc([P, P], F32, "ident")
         make_identity(nc, ident[:])
-        pages = [zeroed_window("page_%d" % b) for b in range(1)]
+        pages = [zeroed_window("page_0")]
 
         v_plane = zeroed_plane(nc.vector, PASSES * S, "v_plane")
         picked_scales = alloc([P, S], U8, "picked_scales")
@@ -181,8 +182,15 @@ def tile_list_pass_arbitration_scores_kernel(
 
         pieces = [(b, sum(widths[:i]), width) for b, widths in enumerate(PIECES) for i, width in enumerate(widths)]
         runs = []
+        squares = {}
+        places = {
+            2: (("w1_raw_1_0",), ("w1_raw_1_0", 4 * 256)),
+            3: (("w1_raw_1_1", 4 * 256), ()),
+            5: (("w1_raw_2_0",), ("w1_raw_2_0", 4 * 320)),
+            6: (("w1_raw_2_0", 4 * 640), ("w1_raw_2_1", 192)),
+        }
 
-        def project(b, start, width, a_sq, b_sq):
+        def project(b, start, width):
             codes, plane = w1_mx[b]
             bank0 = HIGH + 2 * (len(runs) % 2)
             runs.append((b, start, width))
@@ -209,25 +217,24 @@ def tile_list_pass_arbitration_scores_kernel(
                         start=(a == 0 and offset == 0),
                         stop=(a == PASSES - 1 and offset + step == width),
                     )
-            for square, source in ((a_sq, a_bank), (b_sq, b_bank)):
-                nc.scalar.activation(square, source[:, 0:width], ACT.Square)
+            for k, (block, first, count) in enumerate(pieces):
+                low, high = max(first, start), min(first + count, start + width)
+                if block == b and low < high:
+                    if k not in squares:
+                        squares[k] = [
+                            alloc([P, count], F32, "%s_sq_%d" % (x, k), *at) for x, at in zip("ab", places.get(k, ((), ())))
+                        ]
+                    for square, source in zip(squares[k], (a_bank, b_bank)):
+                        nc.scalar.activation(
+                            square[:, low - first : high - first], source[:, low - start : high - start], ACT.Square
+                        )
 
-        squares = {}
+        def project_piece(k):
+            project(*pieces[k])
 
-        def project_piece(k, a_place=(), b_place=()):
-            b, start, width = pieces[k]
-            squares[k] = (
-                alloc([P, width], F32, "a_sq_%d" % k, *a_place)[:], alloc([P, width], F32, "b_sq_%d" % k, *b_place)[:]
-            )
-            project(b, start, width, *squares[k])
-
-        def project_block(b, places=((), ())):
-            tiles = [alloc([P, S], F32, "%s_sq_block_%d" % (x, b), *at) for x, at in zip("ab", places)]
+        def project_block(b):
             for start in range(0, S, BANK):
-                project(b, start, BANK, *[tile[:, start : start + BANK] for tile in tiles])
-            for k, (block, start, width) in enumerate(pieces):
-                if block == b:
-                    squares[k] = [tile[:, start : start + width] for tile in tiles]
+                project(b, start, BANK)
 
         contests, placeds = {}, {}
 
@@ -235,7 +242,7 @@ def tile_list_pass_arbitration_scores_kernel(
             engine = nc.vector if k == 0 else nc.gpsimd
             a_sq, b_sq = squares[k]
             contests[k] = alloc([P, pieces[k][2]], F32, "contest_%d" % k, after)
-            engine.tensor_tensor(contests[k][:], a_sq, b_sq, ALU.subtract)
+            engine.tensor_tensor(contests[k][:], a_sq[:], b_sq[:], ALU.subtract)
 
         def weigh(k, after=None):
             engine = nc.vector if k == 0 else nc.gpsimd
@@ -254,37 +261,35 @@ def tile_list_pass_arbitration_scores_kernel(
             weigh(k, placed_after)
             scatter(k)
 
-        reserve("gates_room", 4 * T)
         z_turned = [
-            alloc([P, TILES, 2, P, 2], BF16, "z_turned_%d" % c, "gates_room" if c == CHUNKS - 1 else None)
-            for c in range(CHUNKS)
+            [alloc([P, 2, 2, P, 2], BF16, "z_turned_%d_%d" % (g, quarter)) for quarter in range(CHUNKS)] for g in range(2)
         ]
 
         def add_board(b, board_after):
             page = pages[b % PAGES]
             last_block = b == ROW_BLOCKS - 1
             board_sb = load(board[P * b : P * (b + 1), :], [P, T], "board_%d" % b, board_after)
-            banks = HIGH if last_block else LOW
+            banks = LOW if b < 2 else HIGH
             sums = [bank(banks + c, "z_bank") for c in range(CHUNKS)]
-            for c in range(CHUNKS):
-                for s in range(TILES):
-                    slots = slice(BANK * c + P * s, BANK * c + P * (s + 1))
+
+            def turn(source, quarter, first):
+                h, a = divmod(quarter, 2)
+                for index in range(TILES):
+                    s, j = divmod(index, 2)
+                    slot0 = BANK * (2 * h + j) + BANK // 2 * a + P * s
                     nc.tensor.matmul(
-                        sums[c][:, P * s : P * (s + 1)], board_sb[:, slots], ident[:],
-                        start=(s == 0), stop=False, is_transpose=True,
+                        sums[quarter][:, P * index : P * (index + 1)], source[:, slot0 : slot0 + P], ident[:],
+                        start=(first and index == 0), stop=(not first and index == TILES - 1), is_transpose=True,
                     )
-            for c in range(CHUNKS):
-                for s in range(TILES):
-                    slots = slice(BANK * c + P * s, BANK * c + P * (s + 1))
-                    nc.tensor.matmul(
-                        sums[c][:, P * s : P * (s + 1)], page[:, slots], ident[:],
-                        start=False, stop=(s == TILES - 1), is_transpose=True,
-                    )
-                copy_out = nc.vector.tensor_copy if last_block and c % 2 else nc.scalar.copy
-                copy_out(
-                    z_turned[c][:, :, :, P // PACK * b : P // PACK * (b + 1), :],
-                    sums[c][:].rearrange("p (s i u e) -> p s u i e", s=TILES, u=2, e=2),
-                )
+
+            for quarter in range(CHUNKS):
+                turn(board_sb, quarter, True)
+            for quarter in range(CHUNKS):
+                turn(page, quarter, False)
+                dst = z_turned[b // 2][quarter][:].rearrange("p u s (j b i) e -> p b (s j) u i e", j=2, b=2)[:, b % 2]
+                src = sums[quarter][:].rearrange("p (n i u e) -> p n u i e", n=TILES, u=2, e=2)
+                copy_out = nc.vector.tensor_copy if last_block and quarter % 2 else nc.scalar.copy
+                copy_out(dst, src)
 
         for name in ("contest_room_0", "contest_room_1", "placed_room_0", "placed_room_1", "placed_room_2"):
             reserve(name, 4 * S)
@@ -294,8 +299,8 @@ def tile_list_pass_arbitration_scores_kernel(
         grouped = cast_w1(1, w1_raw[1], 0)
         w1_mx.append(quantise_w1(1, grouped, None, "w1_room"))
         place_piece(1, "contest_0", "w1_raw_1_1")
-        project_piece(2, ("w1_raw_1_0",), ("w1_raw_1_0", 4 * 256))
-        project_piece(3, ("w1_raw_1_1", 4 * 256))
+        project_piece(2)
+        project_piece(3)
         place_piece(2, "w1_grouped_1", "placed_room_0")
         last_grouped = alloc([P, 2, PASSES, P, PACK], BF16, "w1_grouped_2")
         for i in range(2):
@@ -312,10 +317,12 @@ def tile_list_pass_arbitration_scores_kernel(
             w1_mx.append((codes[:, columns], plane[:, columns]))
         project_block(2)
         project_block(3)
-        contest_chain = ["contest_room_0", "w1_grouped_2"]
-        placed_chain = ["w1_raw_2_1", "placed_room_0", "placed_room_1"]
+        contest_chain = ["contest_3", "w1_grouped_2"]
+        place["late_room"] = place["w1_raw_2_1"] + 4 * BANK
+        placed_chain = ["late_room", "placed_room_0", "placed_room_1"]
         board_after = ("board_room", "w1_room", "tab_words_1", "board_0")
-        for b in range(ROW_BLOCKS):
+
+        def place_block(b):
             for k in range(len(PIECES[0]), len(pieces)):
                 if pieces[k][0] == b:
                     place_piece(k, contest_chain[-2], placed_chain[-3])
@@ -323,92 +330,143 @@ def tile_list_pass_arbitration_scores_kernel(
                     placed_chain.append("placed_%d" % k)
             add_board(b, board_after[b])
 
-        second_result = zeroed_window("result_1", "second_room")
-        wgo_sb = load(wgo, [P, S], "wgo_sb", "v_words_0")
-        prio_places = (("board_1", 0), ("board_2", 0), ("board_2", 4 * S))
-        prios = [load(prio[P * n : P * (n + 1), :], [P, S], "prio_%d" % n, *prio_places[n]) for n in range(OUT_BLOCKS)]
-        w3_plane = zeroed_plane(nc.gpsimd, N, "w3_plane", "b_sq_block_1")
+        def turn_back(g, grouped, vector_banks):
+            pair_banks = [bank((LOW, HIGH)[g] + index, "pair_bank") for index in range(CHUNKS)]
+            for index, pair_bank in enumerate(pair_banks):
+                z_pairs = z_turned[g][index][:].rearrange("p u s r e -> p (u s r e)").bitcast(F32)
+                for i in range(TILES):
+                    nc.tensor.transpose(
+                        pair_bank[:, P * i : P * (i + 1)],
+                        z_pairs[:, P * i : P * (i + 1)],
+                        ident[:],
+                    )
+            for index, pair_bank in enumerate(pair_banks):
+                dst = grouped[:, BANK // 2 * index : BANK // 2 * (index + 1), :]
+                dst = dst.rearrange("p c j -> p (c j)").bitcast(F32).rearrange("p (s c u) -> p s c u", s=2, u=2)
+                src = pair_bank[:].rearrange("p (u s c) -> p s c u", s=2, u=2)
+                if index in vector_banks:
+                    nc.vector.tensor_copy(dst, src)
+                else:
+                    nc.scalar.copy(dst, src)
+
+        def quantise_z(codes, plane, grouped, slots):
+            nc.vector.quantize_mx(
+                out=codes[:, slots].bitcast(FP8X4),
+                scales=plane[:, slots],
+                in_=grouped[:, slots, :].rearrange("p c j -> p (c j)"),
+            )
+
+        def first_block_passes(g, quarter, y_bank):
+            slots = slice(BANK // 2 * quarter, BANK // 2 * (quarter + 1))
+            for j in range(2):
+                nc.tensor.matmul_mx(
+                    out=y_bank[:, BANK // 2 * j : BANK // 2 * (j + 1)],
+                    lhsT=w3_halves[:, g, j, :].bitcast(FP8X4),
+                    lhsT_scale=w3_halves_plane[:, P * g : P * (g + 1)],
+                    rhs=z_codes[g][:, slots].bitcast(FP8X4),
+                    rhs_scale=z_planes[g][:, slots],
+                    start=(g == 0 and j == 0),
+                    stop=(g == 1 and j == 1),
+                )
+
+        def move_half(dst, dst_half, src, src_half):
+            nc.sync.dma_start(
+                dst[HALF * dst_half : HALF * (dst_half + 1), :].bitcast(I32),
+                src[HALF * src_half : HALF * (src_half + 1), :].bitcast(I32),
+            )
+
+        place_block(0)
+        place_block(1)
+        grouped_0 = alloc([P, 2 * BANK, PACK], BF16, "z_grouped_0")
+        turn_back(0, grouped_0, ())
+        place_block(2)
+        last = len(pieces) - 1
+        subtract(last, contest_chain[-2])
+        z_planes = [zeroed_plane(nc.gpsimd, 2 * BANK, "z_plane_%d" % g, "b_sq_9", 2 * BANK * g) for g in range(2)]
+        w3_halves = alloc([P, 2, 2, P], U32, "w3_halves", "a_sq_9")
+        nc.gpsimd.memset(w3_halves[:].bitcast(I32), 0)
+        w3_first = w3_words[0][:, 0:P, :].rearrange("p c i -> p (c i)").bitcast(I32)
+        for g in range(2):
+            for j in range(2):
+                nc.sync.dma_start(
+                    w3_halves[HALF * j : HALF * (j + 1), g, j, :].bitcast(I32), w3_first[HALF * g : HALF * (g + 1), :]
+                )
+        w3_halves_plane = zeroed_plane(nc.gpsimd, 2 * P, "w3_halves_plane", "b_sq_9", 4 * BANK)
+        w3_plane = zeroed_plane(nc.gpsimd, N, "w3_plane", "b_sq_9", 5 * BANK)
+        by_group = w3_scales[0, :, 0:P].rearrange("(g b r) c -> b r g c", g=2, b=2)
         for q in range(QUADRANTS):
+            nc.sync.dma_start(
+                live_rows(w3_halves_plane, q).rearrange("p (g c) -> p g c", g=2).bitcast(I32), by_group[q % 2].bitcast(I32)
+            )
             nc.sync.dma_start(
                 live_rows(w3_plane, q).bitcast(I32), w3_scales[0, PACK * q : PACK * (q + 1), :].bitcast(I32)
             )
+
+        z_codes = [alloc([P, 2 * BANK], U32, "z_codes_0", "placed_room_0")]
+        quantise_z(z_codes[0], z_planes[0], grouped_0, slice(0, 2 * BANK))
+        y_banks = [bank(LOW + c, "y_bank") for c in range(CHUNKS)]
+        for c in range(CHUNKS):
+            first_block_passes(0, c, y_banks[c])
+        odd_codes = alloc([P, 2 * BANK], U32, "odd_codes")
+        odd_plane = alloc([P, 2 * BANK], U8, "odd_plane")
+        move_half(odd_codes, 0, z_codes[0], 1)
+        move_half(odd_plane, 0, z_planes[0], 1)
+        weigh(last, "z_turned_0_2")
+        scatter(last)
+        add_board(3, board_after[3])
+
+        second_result = zeroed_window("result_1", "z_grouped_0")
+        wgo_sb = load(wgo, [P, S], "wgo_sb", "v_words_0")
+        prio_places = (("board_1", 0), ("board_2", 0), ("board_2", 4 * S))
+        prios = [load(prio[P * n : P * (n + 1), :], [P, S], "prio_%d" % n, *prio_places[n]) for n in range(OUT_BLOCKS)]
         w3_codes = alloc([P, N], U32, "w3_codes", "v_words_1")
         nc.sync.dma_start(w3_codes[:].bitcast(I32), w3_words[0].rearrange("p c i -> p (c i)").bitcast(I32))
 
-        z_codes, z_planes = [], []
+        row_bytes = 4 * T
+        reserve("result_room", 2 * row_bytes)
+        grouped_1 = alloc([P, 2 * BANK, PACK], BF16, "z_grouped_1", "result_room", row_bytes // 2)
+        turn_back(1, grouped_1, (1,))
+        z_codes.append(alloc([P, 2 * BANK], U32, "z_codes_1"))
         gates = [alloc([P, T], F32, "gates_0")]
+        by_quarter = gates[0][:].rearrange("p (h j a c) -> p h a j c", h=2, j=2, a=2)
+        for quarter in range(CHUNKS):
+            quantise_z(z_codes[1], z_planes[1], grouped_1, slice(BANK // 2 * quarter, BANK // 2 * (quarter + 1)))
+            first_block_passes(1, quarter, y_banks[quarter])
+            nc.scalar.activation(
+                by_quarter[:, quarter // 2, quarter % 2], y_banks[quarter][:].rearrange("p (j c) -> p j c", j=2), ACT.Sigmoid
+            )
+        for dst, src in ((z_codes[0], z_codes[1]), (z_planes[0], z_planes[1])):
+            move_half(dst, 1, src, 0)
+        for dst, src in ((odd_codes, z_codes[1]), (odd_plane, z_planes[1])):
+            move_half(dst, 1, src, 1)
 
-        def score(n, c, index, first=0, count=BANK):
+        def score(n, c, index):
+            h, j = divmod(c, 2)
+            codes, plane = ((z_codes[0], z_planes[0]), (odd_codes, odd_plane))[j]
+            slots = slice(BANK * h, BANK * (h + 1))
             y_bank = bank(index, "y_bank")
-            slots = slice(first, first + count)
             nc.tensor.matmul_mx(
-                out=y_bank[:, 0:count],
+                out=y_bank[:],
                 lhsT=w3_codes[:, P * n : P * (n + 1)].bitcast(FP8X4),
                 lhsT_scale=w3_plane[:, P * n : P * (n + 1)],
-                rhs=z_codes[c][:, slots].bitcast(FP8X4),
-                rhs_scale=z_planes[c][:, slots],
+                rhs=codes[:, slots].bitcast(FP8X4),
+                rhs_scale=plane[:, slots],
                 start=True,
                 stop=True,
             )
-            nc.scalar.activation(
-                gates[n][:, BANK * c + first : BANK * c + first + count], y_bank[:, 0:count], ACT.Sigmoid
-            )
+            nc.scalar.activation(gates[n][:, BANK * c : BANK * (c + 1)], y_bank[:], ACT.Sigmoid)
 
-        half_chunk = BANK // 2
-        grouped_after = ("a_sq_block_1", "a_sq_block_2", "b_sq_block_2")
-        row_bytes = 4 * T
-        scalar_chunk = 1
-        pair_banks = [bank(index, "pair_bank") for index in range(2 * CHUNKS)]
-        for index, pair_bank in enumerate(pair_banks):
-            c, half = divmod(index, 2)
-            z_pairs = z_turned[c][:].rearrange("p s u r e -> p (s u r e)").bitcast(F32)
-            for i in range(TILES):
-                nc.tensor.transpose(
-                    pair_bank[:, P * i : P * (i + 1)],
-                    z_pairs[:, BANK * half + P * i : BANK * half + P * (i + 1)],
-                    ident[:],
-                )
-        for c in range(CHUNKS):
-            if c < CHUNKS - 1:
-                z_grouped = alloc([P, BANK, PACK], BF16, "z_grouped_%d" % c, grouped_after[c])
-            else:
-                reserve("result_room", 2 * row_bytes)
-                z_grouped = alloc([P, BANK, PACK], BF16, "z_grouped_last", "result_room", row_bytes - BANK * PACK)
-            for half in range(2):
-                dst = z_grouped[:, half_chunk * half : half_chunk * (half + 1), :]
-                dst = dst.rearrange("p c j -> p (c j)").bitcast(F32).rearrange("p (s c u) -> p s c u", s=2, u=2)
-                src = pair_banks[2 * c + half][:].rearrange("p (s u c) -> p s c u", s=2, u=2)
-                if half == 0 or c == scalar_chunk:
-                    nc.scalar.copy(dst, src)
-                else:
-                    nc.vector.tensor_copy(dst, src)
-            codes = alloc([P, BANK], U32, "z_codes_%d" % c)
-            plane = alloc([P, BANK], U8, "z_plane_%d" % c)
-            z_codes.append(codes)
-            z_planes.append(plane)
-            parts = 2 if c == CHUNKS - 1 else 1
-            count = BANK // parts
-            for i in range(parts):
-                slots = slice(count * i, count * (i + 1))
-                nc.vector.quantize_mx(
-                    out=codes[:, slots].bitcast(FP8X4),
-                    scales=plane[:, slots],
-                    in_=z_grouped[:, slots, :].rearrange("p c j -> p (c j)"),
-                )
-                score(0, c, LOW + c if i == 0 else LOW, count * i, count)
-
-        last_result = zeroed_window("result_2", "result_room")
         first_result = zeroed_window("result_0", "result_room", row_bytes)
+        last_result = zeroed_window("result_2", "result_room")
         results = (first_result, second_result, last_result)
-
-        gates.append(alloc([P, T], F32, "gates_1", "z_turned_3"))
-        for c in range(CHUNKS):
+        gates.append(alloc([P, T], F32, "gates_1", "z_turned_1_0"))
+        for c in (0, 2, 1, 3):
             score(1, c, HIGH + c)
 
         picked_gates = []
 
         def pick(n):
-            after = ("a_sq_block_3", "b_sq_block_3", "z_turned_0")[n]
+            after = ("a_sq_7", "a_sq_8", "page_0")[n]
             picked_gate = alloc([P, S], F32, "picked_gates_%d" % n, after)
             nc.vector.tensor_tensor(picked_gate[:], gates[n][:].indirect(idx3[:]), prios[n][:], ALU.mult)
             picked_gates.append(picked_gate)
@@ -417,8 +475,13 @@ def tile_list_pass_arbitration_scores_kernel(
         gates.append(alloc([P, T], F32, "gates_2", "prio_0"))
         for c in range(CHUNKS):
             score(2, c, HIGH + c)
-        for n in range(OUT_BLOCKS):
-            if n + 1 < OUT_BLOCKS:
-                pick(n + 1)
+
+        def put(n):
             nc.vector.tensor_tensor(results[n][:].indirect(idx4[:]), picked_gates[n][:], wgo_sb[:], ALU.mult)
             nc.sync.dma_start(out[P * n : P * (n + 1), :], results[n][:])
+
+        put(0)
+        pick(1)
+        pick(2)
+        put(1)
+        put(2)

@@ -180,6 +180,8 @@ def tile_list_pass_arbitration_scores_kernel(
         w1_raw.append(load_w1("w1_raw_2", 2 * P, H, "second_room", 8 * S, 4 * S))
         idx3, idx4 = load_list(offs3, "idx3"), load_list(offs4, "idx4")
 
+        z_planes = [zeroed_plane(nc.gpsimd, 2 * BANK, "z_plane_%d" % g) for g in range(2)]
+
         pieces = [(b, sum(widths[:i]), width) for b, widths in enumerate(PIECES) for i, width in enumerate(widths)]
         runs = []
         squares = {}
@@ -362,7 +364,7 @@ def tile_list_pass_arbitration_scores_kernel(
                 nc.tensor.matmul_mx(
                     out=y_bank[:, BANK // 2 * j : BANK // 2 * (j + 1)],
                     lhsT=w3_halves[:, g, j, :].bitcast(FP8X4),
-                    lhsT_scale=w3_halves_plane[:, P * g : P * (g + 1)],
+                    lhsT_scale=(w3_plane if j == g else swapped_plane)[:, 0:P],
                     rhs=z_codes[g][:, slots].bitcast(FP8X4),
                     rhs_scale=z_planes[g][:, slots],
                     start=(g == 0 and j == 0),
@@ -377,33 +379,29 @@ def tile_list_pass_arbitration_scores_kernel(
 
         place_block(0)
         place_block(1)
-        grouped_0 = alloc([P, 2 * BANK, PACK], BF16, "z_grouped_0")
+        reserve("group_room", 4 * (T + S))
+        grouped_0 = alloc([P, 2 * BANK, PACK], BF16, "z_grouped_0", "group_room", 4 * S)
         turn_back(0, grouped_0, ())
         place_block(2)
-        last = len(pieces) - 1
-        subtract(last, contest_chain[-2])
-        z_planes = [zeroed_plane(nc.gpsimd, 2 * BANK, "z_plane_%d" % g, "b_sq_9", 2 * BANK * g) for g in range(2)]
-        w3_halves = alloc([P, 2, 2, P], U32, "w3_halves", "a_sq_9")
-        nc.gpsimd.memset(w3_halves[:].bitcast(I32), 0)
-        w3_first = w3_words[0][:, 0:P, :].rearrange("p c i -> p (c i)").bitcast(I32)
-        for g in range(2):
-            for j in range(2):
-                nc.sync.dma_start(
-                    w3_halves[HALF * j : HALF * (j + 1), g, j, :].bitcast(I32), w3_first[HALF * g : HALF * (g + 1), :]
-                )
-        w3_halves_plane = zeroed_plane(nc.gpsimd, 2 * P, "w3_halves_plane", "b_sq_9", 4 * BANK)
-        w3_plane = zeroed_plane(nc.gpsimd, N, "w3_plane", "b_sq_9", 5 * BANK)
-        by_group = w3_scales[0, :, 0:P].rearrange("(g b r) c -> b r g c", g=2, b=2)
+        w3_codes = alloc([P, N], U32, "w3_codes", "v_words_1")
+        nc.sync.dma_start(w3_codes[:].bitcast(I32), w3_words[0].rearrange("p c i -> p (c i)").bitcast(I32))
+        w3_plane = zeroed_plane(nc.gpsimd, N, "w3_plane", "w1_codes_2")
         for q in range(QUADRANTS):
-            nc.sync.dma_start(
-                live_rows(w3_halves_plane, q).rearrange("p (g c) -> p g c", g=2).bitcast(I32), by_group[q % 2].bitcast(I32)
-            )
             nc.sync.dma_start(
                 live_rows(w3_plane, q).bitcast(I32), w3_scales[0, PACK * q : PACK * (q + 1), :].bitcast(I32)
             )
-
+        swapped_plane = alloc([P, P], U8, "swapped_plane")
+        for g in range(2):
+            move_half(swapped_plane, 1 - g, w3_plane[:, 0:P], g)
+        last = len(pieces) - 1
+        subtract(last, contest_chain[-2])
         z_codes = [alloc([P, 2 * BANK], U32, "z_codes_0", "placed_room_0")]
         quantise_z(z_codes[0], z_planes[0], grouped_0, slice(0, 2 * BANK))
+        w3_halves = alloc([P, 2, 2, P], U32, "w3_halves", "group_room", 4 * T)
+        nc.gpsimd.memset(w3_halves[:].bitcast(I32), 0)
+        for g in range(2):
+            for j in range(2):
+                move_half(w3_halves[:, g, j, :], j, w3_codes[:, 0:P], g)
         y_banks = [bank(LOW + c, "y_bank") for c in range(CHUNKS)]
         for c in range(CHUNKS):
             first_block_passes(0, c, y_banks[c])
@@ -415,12 +413,10 @@ def tile_list_pass_arbitration_scores_kernel(
         scatter(last)
         add_board(3, board_after[3])
 
-        second_result = zeroed_window("result_1", "z_grouped_0")
+        second_result = zeroed_window("result_1", "group_room")
         wgo_sb = load(wgo, [P, S], "wgo_sb", "v_words_0")
         prio_places = (("board_1", 0), ("board_2", 0), ("board_2", 4 * S))
         prios = [load(prio[P * n : P * (n + 1), :], [P, S], "prio_%d" % n, *prio_places[n]) for n in range(OUT_BLOCKS)]
-        w3_codes = alloc([P, N], U32, "w3_codes", "v_words_1")
-        nc.sync.dma_start(w3_codes[:].bitcast(I32), w3_words[0].rearrange("p c i -> p (c i)").bitcast(I32))
 
         row_bytes = 4 * T
         reserve("result_room", 2 * row_bytes)

@@ -33,7 +33,7 @@ TILES = BANK // P
 SCALE_ROW0 = P - PASSES * K_PASS // 32
 HALF = P // 2
 LOW, HIGH = 0, 4
-PIECES = ((256, 256, 256, 256), (288, 320, 416), (512, 512), (1024,))
+PIECES = ((256, 256, 256, 256), (288, 320, 416), (512, 512), (512, 512))
 PAGES = 2
 ALIGN = 64
 ITEM_BYTES = {F32: 4, I32: 4, U32: 4, BF16: 2, U8: 1}
@@ -115,17 +115,17 @@ def tile_list_pass_arbitration_scores_kernel(
         idx = load_list(offs, "idx")
         reserve("second_room", 16 * S)
         reserve("board_room", 4 * T)
-        tab_plane = alloc([P, T], U8, "tab_plane")
+        tab_plane = alloc([P, 16 * S], U8, "tab_room", "second_room")[:, 0:T]
         nc.sync.dma_start(
             tab_plane[SCALE_ROW0:P, :].bitcast(I32), tab_scales.rearrange("a q c -> q a c").bitcast(I32)
         )
         nc.vector.memset(tab_plane[0:SCALE_ROW0, :].bitcast(I32), 0)
-        tab_tiles = [load_table_pass(0)]
+        tab_tiles = [load_table_pass(a) for a in range(PASSES)]
         reserve("w1_room", 4 * PASSES * PACK * 2 * P)
         w1_raw = [load_w1("w1_raw_0", 0, P, "w1_room", 0, 4 * S)]
         w2_codes = alloc([P, PASSES, 2 * H], U8, "w2_codes")
         nc.sync.dma_start(w2_codes[:].bitcast(I32), w2_words.rearrange("a p c -> p a c").bitcast(I32))
-        tab_tiles.append(load_table_pass(1))
+        idx2 = load_list(offs2, "idx2")
 
         ident = alloc([P, P], F32, "ident")
         make_identity(nc, ident[:])
@@ -133,7 +133,7 @@ def tile_list_pass_arbitration_scores_kernel(
 
         v_plane = zeroed_plane(nc.vector, PASSES * S, "v_plane")
         picked_scales = alloc([P, S], U8, "picked_scales")
-        nc.vector.tensor_copy(picked_scales[:], tab_plane[:].indirect(idx[:]))
+        nc.vector.tensor_copy(picked_scales[:], tab_plane.indirect(idx[:]))
         quadrant_rows = PASSES * PACK
         for q in range(QUADRANTS):
             nc.scalar.dma_start(
@@ -141,11 +141,19 @@ def tile_list_pass_arbitration_scores_kernel(
                 picked_scales[SCALE_ROW0 + quadrant_rows * q : SCALE_ROW0 + quadrant_rows * (q + 1), :].bitcast(I32),
             )
 
-        v_words = [alloc([P, S], U32, "v_words_%d" % a) for a in range(PASSES)]
+        reserve("v_words_0", 4 * S)
+        reserve("v_words_1", 4 * BANK)
+        reserve("cast_room", 4 * T + 4 * BANK)
+        v_words = {(0, h): alloc([P, BANK], U32, "v_0_%d" % h, "v_words_0", 4 * BANK * h) for h in range(2)}
+        v_words[(1, 0)] = alloc([P, BANK], U32, "v_1_0", "v_words_1")
 
         def pick_words(a, first, last):
             entries = idx[:, first // GROUP : last // GROUP]
-            nc.vector.tensor_copy(v_words[a][:, first:last], tab_tiles[a][:].indirect(entries))
+            picked = v_words[(a, first // BANK)][:, first % BANK : first % BANK + last - first]
+            nc.vector.tensor_copy(picked, tab_tiles[a][:].indirect(entries))
+
+        def v_run(a, first, last):
+            return v_words[(a, first // BANK)][:, first % BANK : first % BANK + last - first].bitcast(FP8X4)
 
         def cast_w1(b, raw, column0, grouped=None):
             if grouped is None:
@@ -165,17 +173,28 @@ def tile_list_pass_arbitration_scores_kernel(
             )
             return codes, plane
 
-        pick_words(0, 0, S)
-        w1_mx = [quantise_w1(0, cast_w1(0, w1_raw[0], 0), "board_room")]
-        for first, last in ((0, 256), (256, 512), (512, S)):
-            pick_words(1, first, last)
+        pick_words(0, 0, BANK)
+        pick_words(0, BANK, S)
+        pick_words(1, 0, BANK)
+        first_grouped = alloc([P, PASSES, P, PACK], BF16, "w1_grouped_0", "cast_room", 4 * T - S)
+        cast_w1(0, w1_raw[0], 0, first_grouped)
+        first_codes = alloc([P, PASSES * P], U32, "w1_codes_0", "board_room")
+        first_plane = alloc([P, PASSES * P], U8, "w1_plane_0")
+        for a in range(PASSES):
+            nc.vector.quantize_mx(
+                out=first_codes[:, P * a : P * (a + 1)].bitcast(FP8X4),
+                scales=first_plane[:, P * a : P * (a + 1)],
+                in_=first_grouped[:, a, :, :].rearrange("p c j -> p (c j)"),
+            )
+        w1_mx = [(first_codes, first_plane)]
+        v_words[(1, 1)] = alloc([P, BANK], U32, "v_1_1", "cast_room", 4 * T)
+        pick_words(1, BANK, S)
 
-        pages.append(zeroed_window("page_1", "tab_words_0"))
+        pages.append(zeroed_window("page_1", "cast_room"))
         half = S // 2
         w1_raw.append(load_w1("w1_raw_1", P, 2 * P, "second_room", 4 * S, 2 * S))
         wgs_sb = alloc([P, S], F32, "wgs_sb", "second_room")
         nc.sync.dma_start(wgs_sb[:, 0:half], wgs[:, 0:half])
-        idx2 = load_list(offs2, "idx2")
         nc.sync.dma_start(wgs_sb[:, half:S], wgs[:, half:S])
         w1_raw.append(load_w1("w1_raw_2", 2 * P, H, "second_room", 8 * S, 4 * S))
         idx3, idx4 = load_list(offs3, "idx3"), load_list(offs4, "idx4")
@@ -203,7 +222,7 @@ def tile_list_pass_arbitration_scores_kernel(
                     out=a_bank[:, 0:width],
                     lhsT=codes[:, P * a : P * (a + 1)].bitcast(FP8X4),
                     lhsT_scale=plane[:, P * a : P * (a + 1)],
-                    rhs=v_words[a][:, start : start + width].bitcast(FP8X4),
+                    rhs=v_run(a, start, start + width),
                     rhs_scale=v_plane[:, S * a + start : S * a + start + width],
                     start=(a == 0),
                     stop=(a == PASSES - 1),
@@ -214,7 +233,7 @@ def tile_list_pass_arbitration_scores_kernel(
                         out=b_bank[:, offset : offset + step],
                         lhsT=w2_codes[:, a, 2 * P * b : 2 * P * (b + 1)].bitcast(FP4X4),
                         lhsT_scale=w2_plane[:, H * a + P * b : H * a + P * (b + 1)],
-                        rhs=v_words[a][:, entries].bitcast(FP8X4),
+                        rhs=v_run(a, entries.start, entries.stop),
                         rhs_scale=v_plane[:, S * a + entries.start : S * a + entries.stop],
                         start=(a == 0 and offset == 0),
                         stop=(a == PASSES - 1 and offset + step == width),
@@ -299,7 +318,7 @@ def tile_list_pass_arbitration_scores_kernel(
         project_piece(1)
         place_piece(0, "contest_room_0")
         grouped = cast_w1(1, w1_raw[1], 0)
-        w1_mx.append(quantise_w1(1, grouped, None, "w1_room"))
+        w1_mx.append(quantise_w1(1, grouped, "tab_words_1", "w1_room"))
         place_piece(1, "contest_0", "w1_raw_1_1")
         project_piece(2)
         project_piece(3)
@@ -308,9 +327,9 @@ def tile_list_pass_arbitration_scores_kernel(
         for i in range(2):
             cast_w1(2 + i, w1_raw[2], P * i, last_grouped[:, i])
         project_block(1)
-        place_piece(3, "contest_2", "placed_room_1")
+        place_piece(4, "contest_2", "placed_room_1")
         codes = alloc([P, 2 * PASSES * P], U32, "w1_codes_2")
-        plane = alloc([P, 2 * PASSES * P], U8, "w1_plane_2", "tab_words_1")
+        plane = alloc([P, 2 * PASSES * P], U8, "w1_plane_2")
         nc.vector.quantize_mx(
             out=codes[:].bitcast(FP8X4), scales=plane[:], in_=last_grouped[:].rearrange("p b a c j -> p (b a c j)")
         )
@@ -319,13 +338,14 @@ def tile_list_pass_arbitration_scores_kernel(
             w1_mx.append((codes[:, columns], plane[:, columns]))
         project_block(2)
         project_block(3)
-        contest_chain = ["contest_3", "w1_grouped_2"]
         place["late_room"] = place["w1_raw_2_1"] + 4 * BANK
-        placed_chain = ["late_room", "placed_room_0", "placed_room_1"]
+        place_piece(3, "contest_4", "late_room")
+        contest_chain = ["w1_grouped_2", "contest_3"]
+        placed_chain = ["placed_room_0", "placed_room_1", "late_room"]
         board_after = ("board_room", "w1_room", "tab_words_1", "board_0")
 
         def place_block(b):
-            for k in range(len(PIECES[0]), len(pieces)):
+            for k in range(len(PIECES[0]) + 1, len(pieces)):
                 if pieces[k][0] == b:
                     place_piece(k, contest_chain[-2], placed_chain[-3])
                     contest_chain.append("contest_%d" % k)
@@ -333,7 +353,7 @@ def tile_list_pass_arbitration_scores_kernel(
             add_board(b, board_after[b])
 
         def turn_back(g, grouped, vector_banks):
-            pair_banks = [bank((LOW, HIGH)[g] + index, "pair_bank") for index in range(CHUNKS)]
+            pair_banks = [bank(HIGH + index, "pair_bank") for index in range(CHUNKS)]
             for index, pair_bank in enumerate(pair_banks):
                 z_pairs = z_turned[g][index][:].rearrange("p u s r e -> p (u s r e)").bitcast(F32)
                 for i in range(TILES):
@@ -383,7 +403,7 @@ def tile_list_pass_arbitration_scores_kernel(
         grouped_0 = alloc([P, 2 * BANK, PACK], BF16, "z_grouped_0", "group_room", 4 * S)
         turn_back(0, grouped_0, ())
         place_block(2)
-        w3_codes = alloc([P, N], U32, "w3_codes", "v_words_1")
+        w3_codes = alloc([P, N], U32, "w3_codes", "v_1_1")
         nc.sync.dma_start(w3_codes[:].bitcast(I32), w3_words[0].rearrange("p c i -> p (c i)").bitcast(I32))
         w3_plane = zeroed_plane(nc.gpsimd, N, "w3_plane", "w1_codes_2")
         for q in range(QUADRANTS):
@@ -394,10 +414,12 @@ def tile_list_pass_arbitration_scores_kernel(
         for g in range(2):
             move_half(swapped_plane, 1 - g, w3_plane[:, 0:P], g)
         last = len(pieces) - 1
-        subtract(last, contest_chain[-2])
-        z_codes = [alloc([P, 2 * BANK], U32, "z_codes_0", "placed_room_0")]
+        place_piece(last - 1, contest_chain[-2], placed_chain[-3])
+        subtract(last, "z_turned_0_3")
+        weigh(last, placed_chain[-2])
+        z_codes = [alloc([P, 2 * BANK], U32, "z_codes_0", "placed_room_1")]
         quantise_z(z_codes[0], z_planes[0], grouped_0, slice(0, 2 * BANK))
-        w3_halves = alloc([P, 2, 2, P], U32, "w3_halves", "group_room", 4 * T)
+        w3_halves = alloc([P, 2, 2, P], U32, "w3_halves", "contest_%d" % last)
         nc.gpsimd.memset(w3_halves[:].bitcast(I32), 0)
         for g in range(2):
             for j in range(2):
@@ -409,7 +431,6 @@ def tile_list_pass_arbitration_scores_kernel(
         odd_plane = alloc([P, 2 * BANK], U8, "odd_plane")
         move_half(odd_codes, 0, z_codes[0], 1)
         move_half(odd_plane, 0, z_planes[0], 1)
-        weigh(last, "z_turned_0_2")
         scatter(last)
         add_board(3, board_after[3])
 

@@ -33,7 +33,7 @@ TILES = BANK // P
 SCALE_ROW0 = P - PASSES * K_PASS // 32
 HALF = P // 2
 LOW, HIGH = 0, 4
-PIECES = ((256, 256, 256, 256), (288, 320, 416), (512, 512), (512, 512))
+PIECES = ((256, 256, 512), (512, 512), (512, 512), (512, 512))
 PAGES = 2
 ALIGN = 64
 ITEM_BYTES = {F32: 4, I32: 4, U32: 4, BF16: 2, U8: 1}
@@ -125,6 +125,8 @@ def tile_list_pass_arbitration_scores_kernel(
         w1_raw = [load_w1("w1_raw_0", 0, P, "w1_room", 0, 4 * S)]
         w2_codes = alloc([P, PASSES, 2 * H], U8, "w2_codes")
         nc.sync.dma_start(w2_codes[:].bitcast(I32), w2_words.rearrange("a p c -> p a c").bitcast(I32))
+        reserve("raw_room", 4 * S)
+        w1_raw.append(load_w1("w1_raw_1", P, 2 * P, "raw_room", 0, 2 * S))
         idx2 = load_list(offs2, "idx2")
 
         ident = alloc([P, P], F32, "ident")
@@ -192,7 +194,6 @@ def tile_list_pass_arbitration_scores_kernel(
 
         pages.append(zeroed_window("page_1", "cast_room"))
         half = S // 2
-        w1_raw.append(load_w1("w1_raw_1", P, 2 * P, "second_room", 4 * S, 2 * S))
         wgs_sb = alloc([P, S], F32, "wgs_sb", "second_room")
         nc.sync.dma_start(wgs_sb[:, 0:half], wgs[:, 0:half])
         nc.sync.dma_start(wgs_sb[:, half:S], wgs[:, half:S])
@@ -204,12 +205,7 @@ def tile_list_pass_arbitration_scores_kernel(
         pieces = [(b, sum(widths[:i]), width) for b, widths in enumerate(PIECES) for i, width in enumerate(widths)]
         runs = []
         squares = {}
-        places = {
-            2: (("w1_raw_1_0",), ("w1_raw_1_0", 4 * 256)),
-            3: (("w1_raw_1_1", 4 * 256), ()),
-            5: (("w1_raw_2_0",), ("w1_raw_2_0", 4 * 320)),
-            6: (("w1_raw_2_0", 4 * 640), ("w1_raw_2_1", 192)),
-        }
+        places = {4: (("w1_raw_2_0",), ("w1_raw_2_0", 4 * BANK))}
 
         def project(b, start, width):
             codes, plane = w1_mx[b]
@@ -260,13 +256,13 @@ def tile_list_pass_arbitration_scores_kernel(
         contests, placeds = {}, {}
 
         def subtract(k, after=None):
-            engine = nc.vector if k == 0 else nc.gpsimd
+            engine = nc.vector if k < 2 else nc.gpsimd
             a_sq, b_sq = squares[k]
             contests[k] = alloc([P, pieces[k][2]], F32, "contest_%d" % k, after)
             engine.tensor_tensor(contests[k][:], a_sq[:], b_sq[:], ALU.subtract)
 
         def weigh(k, after=None):
-            engine = nc.vector if k == 0 else nc.gpsimd
+            engine = nc.vector if k < 2 else nc.gpsimd
             b, start, width = pieces[k]
             placeds[k] = alloc([P, width], F32, "placed_%d" % k, after)
             weight = wgs_sb[:, start : start + width]
@@ -314,20 +310,21 @@ def tile_list_pass_arbitration_scores_kernel(
 
         for name in ("contest_room_0", "contest_room_1", "placed_room_0", "placed_room_1", "placed_room_2"):
             reserve(name, 4 * S)
-        project_piece(0)
-        project_piece(1)
-        place_piece(0, "contest_room_0")
-        grouped = cast_w1(1, w1_raw[1], 0)
-        w1_mx.append(quantise_w1(1, grouped, "tab_words_1", "w1_room"))
-        place_piece(1, "contest_0", "w1_raw_1_1")
-        project_piece(2)
-        project_piece(3)
-        place_piece(2, "w1_grouped_1", "placed_room_0")
+        w1_mx.append(quantise_w1(1, cast_w1(1, w1_raw[1], 0), "tab_words_1", "w1_room"))
+        for k in range(len(PIECES[0])):
+            project_piece(k)
+        subtract(0)
+        reserve("contest_1_room", 4 * BANK)
+        subtract(1, "contest_1_room")
+        weigh(0)
+        weigh(1, "contest_room_1")
+        scatter(0)
+        scatter(1)
+        place_piece(2, "contest_1_room")
         last_grouped = alloc([P, 2, PASSES, P, PACK], BF16, "w1_grouped_2")
         for i in range(2):
             cast_w1(2 + i, w1_raw[2], P * i, last_grouped[:, i])
         project_block(1)
-        place_piece(4, "contest_2", "placed_room_1")
         codes = alloc([P, 2 * PASSES * P], U32, "w1_codes_2")
         plane = alloc([P, 2 * PASSES * P], U8, "w1_plane_2")
         nc.vector.quantize_mx(
@@ -339,15 +336,15 @@ def tile_list_pass_arbitration_scores_kernel(
         project_block(2)
         project_block(3)
         place["late_room"] = place["w1_raw_2_1"] + 4 * BANK
-        place_piece(3, "contest_4", "late_room")
-        contest_chain = ["w1_grouped_2", "contest_3"]
-        placed_chain = ["placed_room_0", "placed_room_1", "late_room"]
+        contest_chain = ["contest_2", "w1_grouped_2"]
+        placed_chain = ["late_room", "placed_room_1", "placed_room_0"]
+        place["late_codes_room"] = place["placed_room_2"]
         board_after = ("board_room", "w1_room", "tab_words_1", "board_0")
 
         def place_block(b):
-            for k in range(len(PIECES[0]) + 1, len(pieces)):
+            for k in range(len(PIECES[0]), len(pieces)):
                 if pieces[k][0] == b:
-                    place_piece(k, contest_chain[-2], placed_chain[-3])
+                    place_piece(k, contest_chain[-2], "placed_room_2" if k == len(pieces) - 3 else placed_chain[-3])
                     contest_chain.append("contest_%d" % k)
                     placed_chain.append("placed_%d" % k)
             add_board(b, board_after[b])
@@ -417,7 +414,7 @@ def tile_list_pass_arbitration_scores_kernel(
         place_piece(last - 1, contest_chain[-2], placed_chain[-3])
         subtract(last, "z_turned_0_3")
         weigh(last, placed_chain[-2])
-        z_codes = [alloc([P, 2 * BANK], U32, "z_codes_0", "placed_room_1")]
+        z_codes = [alloc([P, 2 * BANK], U32, "z_codes_0", "late_codes_room")]
         quantise_z(z_codes[0], z_planes[0], grouped_0, slice(0, 2 * BANK))
         w3_halves = alloc([P, 2, 2, P], U32, "w3_halves", "contest_%d" % last)
         nc.gpsimd.memset(w3_halves[:].bitcast(I32), 0)
@@ -434,10 +431,13 @@ def tile_list_pass_arbitration_scores_kernel(
         scatter(last)
         add_board(3, board_after[3])
 
-        second_result = zeroed_window("result_1", "group_room")
         wgo_sb = load(wgo, [P, S], "wgo_sb", "v_words_0")
         prio_places = (("board_1", 0), ("board_2", 0), ("board_2", 4 * S))
         prios = [load(prio[P * n : P * (n + 1), :], [P, S], "prio_%d" % n, *prio_places[n]) for n in range(OUT_BLOCKS)]
+
+        first_weight = alloc([P, S], F32, "first_weight", "group_room", 4 * T)
+        nc.gpsimd.tensor_tensor(first_weight[:], prios[0][:], wgo_sb[:], ALU.mult)
+        second_result = zeroed_window("result_1", "group_room")
 
         row_bytes = 4 * T
         reserve("result_room", 2 * row_bytes)
@@ -449,9 +449,8 @@ def tile_list_pass_arbitration_scores_kernel(
         for quarter in range(CHUNKS):
             quantise_z(z_codes[1], z_planes[1], grouped_1, slice(BANK // 2 * quarter, BANK // 2 * (quarter + 1)))
             first_block_passes(1, quarter, y_banks[quarter])
-            nc.scalar.activation(
-                by_quarter[:, quarter // 2, quarter % 2], y_banks[quarter][:].rearrange("p (j c) -> p j c", j=2), ACT.Sigmoid
-            )
+            copy_out = nc.vector.tensor_copy if quarter == CHUNKS - 1 else nc.scalar.copy
+            copy_out(by_quarter[:, quarter // 2, quarter % 2], y_banks[quarter][:].rearrange("p (j c) -> p j c", j=2))
         for dst, src in ((z_codes[0], z_codes[1]), (z_planes[0], z_planes[1])):
             move_half(dst, 1, src, 0)
         for dst, src in ((odd_codes, z_codes[1]), (odd_plane, z_planes[1])):
@@ -480,15 +479,20 @@ def tile_list_pass_arbitration_scores_kernel(
         for c in (0, 2, 1, 3):
             score(1, c, HIGH + c)
 
-        picked_gates = []
+        picked_gates = [None]
 
         def pick(n):
-            after = ("a_sq_7", "a_sq_8", "page_0")[n]
+            after = ("a_sq_5", "a_sq_6", "page_0")[n]
             picked_gate = alloc([P, S], F32, "picked_gates_%d" % n, after)
             nc.vector.tensor_tensor(picked_gate[:], gates[n][:].indirect(idx3[:]), prios[n][:], ALU.mult)
             picked_gates.append(picked_gate)
 
-        pick(0)
+        first_gates = []
+        for i in range(2):
+            picked = alloc([P, BANK], F32, "picked_scores_%d" % i, "a_sq_5", 4 * BANK * i)
+            nc.vector.tensor_copy(picked[:], gates[0][:].indirect(idx3[:, 32 * i : 32 * (i + 1)]))
+            first_gates.append(alloc([P, BANK], F32, "first_gates_%d" % i, "page_1", 4 * BANK * i))
+            nc.scalar.activation(first_gates[i][:], picked[:], ACT.Sigmoid)
         gates.append(alloc([P, T], F32, "gates_2", "prio_0"))
         for c in range(CHUNKS):
             score(2, c, HIGH + c)
@@ -497,7 +501,10 @@ def tile_list_pass_arbitration_scores_kernel(
             nc.vector.tensor_tensor(results[n][:].indirect(idx4[:]), picked_gates[n][:], wgo_sb[:], ALU.mult)
             nc.sync.dma_start(out[P * n : P * (n + 1), :], results[n][:])
 
-        put(0)
+        for i in range(2):
+            window = results[0][:].indirect(idx4[:, 32 * i : 32 * (i + 1)])
+            nc.vector.tensor_tensor(window, first_gates[i][:], first_weight[:, BANK * i : BANK * (i + 1)], ALU.mult)
+        nc.sync.dma_start(out[0:P, :], results[0][:])
         pick(1)
         pick(2)
         put(1)

@@ -132,6 +132,7 @@ def tile_list_pass_arbitration_scores_kernel(
         ident = alloc([P, P], F32, "ident")
         make_identity(nc, ident[:])
         pages = [zeroed_window("page_0")]
+        z_planes = [zeroed_plane(nc.gpsimd, 2 * BANK, "z_plane_%d" % g) for g in range(2)]
 
         v_plane = zeroed_plane(nc.vector, PASSES * S, "v_plane")
         picked_scales = alloc([P, S], U8, "picked_scales")
@@ -157,11 +158,11 @@ def tile_list_pass_arbitration_scores_kernel(
         def v_run(a, first, last):
             return v_words[(a, first // BANK)][:, first % BANK : first % BANK + last - first].bitcast(FP8X4)
 
-        def cast_w1(b, raw, column0, grouped=None):
+        def cast_w1(b, raw, column0, grouped=None, copy=nc.scalar.copy):
             if grouped is None:
                 grouped = alloc([P, PASSES, P, PACK], BF16, "w1_grouped_%d" % b)
             for a in range(PASSES):
-                nc.scalar.copy(
+                copy(
                     grouped[:, a, :, :].rearrange("p (c i) j -> p c j i", i=4),
                     raw[a][:, :, column0 : column0 + P].rearrange("p j (c i) -> p c j i", i=4),
                 )
@@ -200,7 +201,6 @@ def tile_list_pass_arbitration_scores_kernel(
         w1_raw.append(load_w1("w1_raw_2", 2 * P, H, "second_room", 8 * S, 4 * S))
         idx3, idx4 = load_list(offs3, "idx3"), load_list(offs4, "idx4")
 
-        z_planes = [zeroed_plane(nc.gpsimd, 2 * BANK, "z_plane_%d" % g) for g in range(2)]
 
         pieces = [(b, sum(widths[:i]), width) for b, widths in enumerate(PIECES) for i, width in enumerate(widths)]
         runs = []
@@ -209,7 +209,7 @@ def tile_list_pass_arbitration_scores_kernel(
 
         def project(b, start, width):
             codes, plane = w1_mx[b]
-            bank0 = HIGH + 2 * (len(runs) % 2)
+            bank0 = LOW if len(runs) == 2 else HIGH + 2 * (len(runs) % 2)
             runs.append((b, start, width))
             a_bank, b_bank = bank(bank0, "a_bank"), bank(bank0 + 1, "b_bank")
             step = BANK if width == BANK else P
@@ -310,7 +310,9 @@ def tile_list_pass_arbitration_scores_kernel(
 
         for name in ("contest_room_0", "contest_room_1", "placed_room_0", "placed_room_1", "placed_room_2"):
             reserve(name, 4 * S)
-        w1_mx.append(quantise_w1(1, cast_w1(1, w1_raw[1], 0), "tab_words_1", "w1_room"))
+        second_grouped = alloc([P, PASSES, P, PACK], BF16, "w1_grouped_1", "tab_words_1")
+        cast_w1(1, w1_raw[1], 0, second_grouped, lambda dst, src: nc.vector.tensor_tensor(dst, src, src, ALU.max))
+        w1_mx.append(quantise_w1(1, second_grouped, "tab_words_0", "w1_room"))
         for k in range(len(PIECES[0])):
             project_piece(k)
         subtract(0)
@@ -339,7 +341,7 @@ def tile_list_pass_arbitration_scores_kernel(
         contest_chain = ["contest_2", "w1_grouped_2"]
         placed_chain = ["late_room", "placed_room_1", "placed_room_0"]
         place["late_codes_room"] = place["placed_room_2"]
-        board_after = ("board_room", "w1_room", "tab_words_1", "board_0")
+        board_after = ("board_room", "w1_room", "tab_words_0", "board_0")
 
         def place_block(b):
             for k in range(len(PIECES[0]), len(pieces)):
@@ -350,7 +352,7 @@ def tile_list_pass_arbitration_scores_kernel(
             add_board(b, board_after[b])
 
         def turn_back(g, grouped, vector_banks):
-            pair_banks = [bank(HIGH + index, "pair_bank") for index in range(CHUNKS)]
+            pair_banks = [bank((LOW, HIGH)[g] + index, "pair_bank") for index in range(CHUNKS)]
             for index, pair_bank in enumerate(pair_banks):
                 z_pairs = z_turned[g][index][:].rearrange("p u s r e -> p (u s r e)").bitcast(F32)
                 for i in range(TILES):

@@ -19,24 +19,30 @@ ACT = mybir.ActivationFunctionType
 ALU = mybir.AluOpType
 
 P = 128
+HALF = P // 2
 PACK = 4
 K_PASS = P * PACK
 PASSES = K // K_PASS
 QUADRANT = 32
 QUADRANTS = P // QUADRANT
-GROUP = 16
+SCALE_ROW0 = P - PASSES * K_PASS // 32
+LIST_ROWS = 16
 BANK = 512
+TILES = BANK // P
+LOW, HIGH = 0, 4
 ROW_BLOCKS = H // P
 OUT_BLOCKS = N // P
 CHUNKS = T // BANK
-TILES = BANK // P
-SCALE_ROW0 = P - PASSES * K_PASS // 32
-HALF = P // 2
-LOW, HIGH = 0, 4
+GROUPS = 2
+PACKED = T // 2
+QUARTERS = 4
+QUARTER = PACKED // QUARTERS
 PIECES = ((256, 256, 512), (512, 512), (512, 512), (512, 512))
+VECTOR_PIECES = 2
 PAGES = 2
+KB = 1024
 ALIGN = 64
-ITEM_BYTES = {F32: 4, I32: 4, U32: 4, BF16: 2, U8: 1}
+ITEM_BYTES = {F32: 4, U32: 4, BF16: 2, U8: 1}
 
 
 def tile_list_pass_arbitration_scores_kernel(
@@ -65,17 +71,20 @@ def tile_list_pass_arbitration_scores_kernel(
             return psum.tile([P, BANK], F32, name=name, tag="bank%d" % index)
 
         def load_list(src, name):
-            dst = lists.tile([P, S // GROUP], U16, name=name)
+            dst = lists.tile([P, S // LIST_ROWS], U16, name=name)
             nc.sync.dma_start(dst[:], src)
             return dst
+
+        def entries_of(list_tile, first, last):
+            return list_tile[:, first // LIST_ROWS : last // LIST_ROWS]
 
         def load(src, shape, name, after, at=0):
             dst = alloc(shape, F32, name, after, at)
             nc.sync.dma_start(dst[:], src)
             return dst
 
-        def zeroed_plane(engine, width, name, after=None, at=0):
-            plane = alloc([P, width], U8, name, after, at)
+        def zeroed_plane(engine, width, name, after=None):
+            plane = alloc([P, width], U8, name, after)
             engine.memset(plane[:].bitcast(I32), 0)
             return plane
 
@@ -92,14 +101,25 @@ def tile_list_pass_arbitration_scores_kernel(
             nc.sync.dma_start(words[:].bitcast(I32), tab_words[a].rearrange("p t i -> p (t i)").bitcast(I32))
             return words
 
-        def load_w1(name, first, last, after, at, pitch):
+        def load_w1(name, first, last, after=None, at=0):
             tiles = []
             for a in range(PASSES):
-                dst = alloc([P, PACK, last - first], F32, "%s_%d" % (name, a), after, at + pitch * a)
+                pass_bytes = 4 * PACK * (last - first)
+                dst = alloc([P, PACK, last - first], F32, "%s_%d" % (name, a), after, at + pass_bytes * a)
                 src = w1[K_PASS * a : K_PASS * (a + 1), first:last].rearrange("(p j) c -> p j c", j=PACK)
                 nc.sync.dma_start(dst[:], src)
                 tiles.append(dst)
             return tiles
+
+        def cast_w1(grouped, raw, column0, copy):
+            for a in range(PASSES):
+                copy(
+                    grouped[:, a, :, :].rearrange("p (c i) j -> p c j i", i=4),
+                    raw[a][:, :, column0 : column0 + P].rearrange("p j (c i) -> p c j i", i=4),
+                )
+
+        def quantise(codes, plane, grouped):
+            nc.vector.quantize_mx(out=codes.bitcast(FP8X4), scales=plane, in_=grouped)
 
         w2_plane = zeroed_plane(nc.gpsimd, PASSES * H, "w2_plane")
         for q in range(QUADRANTS):
@@ -113,26 +133,23 @@ def tile_list_pass_arbitration_scores_kernel(
         nc.scalar.activation(table_warmup[:], warmup_in[:], ACT.Sigmoid)
 
         idx = load_list(offs, "idx")
-        reserve("second_room", 16 * S)
-        reserve("board_room", 4 * T)
-        tab_plane = alloc([P, 16 * S], U8, "tab_room", "second_room")[:, 0:T]
+        tab_plane = alloc([P, 12 * KB], U8, "second_room")[:, 0:T]
         nc.sync.dma_start(
             tab_plane[SCALE_ROW0:P, :].bitcast(I32), tab_scales.rearrange("a q c -> q a c").bitcast(I32)
         )
         nc.vector.memset(tab_plane[0:SCALE_ROW0, :].bitcast(I32), 0)
         tab_tiles = [load_table_pass(a) for a in range(PASSES)]
-        reserve("w1_room", 4 * PASSES * PACK * 2 * P)
-        w1_raw = [load_w1("w1_raw_0", 0, P, "w1_room", 0, 4 * S)]
+        reserve("board_1_room", 4 * T)
+        w1_raw = [load_w1("w1_raw_0", 0, P, "board_1_room")]
         w2_codes = alloc([P, PASSES, 2 * H], U8, "w2_codes")
         nc.sync.dma_start(w2_codes[:].bitcast(I32), w2_words.rearrange("a p c -> p a c").bitcast(I32))
-        reserve("raw_room", 4 * S)
-        w1_raw.append(load_w1("w1_raw_1", P, 2 * P, "raw_room", 0, 2 * S))
+        w1_raw.append(load_w1("w1_raw_1", P, 2 * P))
         idx2 = load_list(offs2, "idx2")
 
         ident = alloc([P, P], F32, "ident")
         make_identity(nc, ident[:])
         pages = [zeroed_window("page_0")]
-        z_planes = [zeroed_plane(nc.gpsimd, 2 * BANK, "z_plane_%d" % g) for g in range(2)]
+        z_planes = [zeroed_plane(nc.gpsimd, PACKED, "z_plane_%d" % g) for g in range(GROUPS)]
 
         v_plane = zeroed_plane(nc.vector, PASSES * S, "v_plane")
         picked_scales = alloc([P, S], U8, "picked_scales")
@@ -144,251 +161,138 @@ def tile_list_pass_arbitration_scores_kernel(
                 picked_scales[SCALE_ROW0 + quadrant_rows * q : SCALE_ROW0 + quadrant_rows * (q + 1), :].bitcast(I32),
             )
 
-        reserve("v_words_0", 4 * S)
-        reserve("v_words_1", 4 * BANK)
-        reserve("cast_room", 4 * T + 4 * BANK)
-        v_words = {(0, h): alloc([P, BANK], U32, "v_0_%d" % h, "v_words_0", 4 * BANK * h) for h in range(2)}
-        v_words[(1, 0)] = alloc([P, BANK], U32, "v_1_0", "v_words_1")
+        v_words = {}
 
-        def pick_words(a, first, last):
-            entries = idx[:, first // GROUP : last // GROUP]
-            picked = v_words[(a, first // BANK)][:, first % BANK : first % BANK + last - first]
-            nc.vector.tensor_copy(picked, tab_tiles[a][:].indirect(entries))
+        def pick_words(a, h, after=None, at=0):
+            v_words[(a, h)] = alloc([P, BANK], U32, "v_words_%d_%d" % (a, h), after, at)
+            nc.vector.tensor_copy(v_words[(a, h)][:], tab_tiles[a][:].indirect(entries_of(idx, BANK * h, BANK * (h + 1))))
 
         def v_run(a, first, last):
             return v_words[(a, first // BANK)][:, first % BANK : first % BANK + last - first].bitcast(FP8X4)
 
-        def cast_w1(b, raw, column0, grouped=None, copy=nc.scalar.copy):
-            if grouped is None:
-                grouped = alloc([P, PASSES, P, PACK], BF16, "w1_grouped_%d" % b)
-            for a in range(PASSES):
-                copy(
-                    grouped[:, a, :, :].rearrange("p (c i) j -> p c j i", i=4),
-                    raw[a][:, :, column0 : column0 + P].rearrange("p j (c i) -> p c j i", i=4),
-                )
-            return grouped
-
-        def quantise_w1(b, grouped, after=None, plane_after=None):
-            codes = alloc([P, PASSES * P], U32, "w1_codes_%d" % b, after)
-            plane = alloc([P, PASSES * P], U8, "w1_plane_%d" % b, plane_after)
-            nc.vector.quantize_mx(
-                out=codes[:].bitcast(FP8X4), scales=plane[:], in_=grouped[:].rearrange("p a c j -> p (a c j)")
-            )
-            return codes, plane
-
-        pick_words(0, 0, BANK)
-        pick_words(0, BANK, S)
-        pick_words(1, 0, BANK)
-        first_grouped = alloc([P, PASSES, P, PACK], BF16, "w1_grouped_0", "cast_room", 4 * T - S)
-        cast_w1(0, w1_raw[0], 0, first_grouped)
-        first_codes = alloc([P, PASSES * P], U32, "w1_codes_0", "board_room")
-        first_plane = alloc([P, PASSES * P], U8, "w1_plane_0")
+        pick_words(0, 0)
+        pick_words(0, 1)
+        pick_words(1, 0)
+        reserve("page_1_room", 4 * T + 4 * BANK)
+        reserve("board_0_room", 4 * T)
+        grouped = alloc([P, PASSES, P, PACK], BF16, "w1_grouped_0", "page_1_room", 4 * T - KB)
+        cast_w1(grouped, w1_raw[0], 0, nc.scalar.copy)
+        codes = alloc([P, PASSES * P], U32, "w1_codes_0", "board_0_room")
+        plane = alloc([P, PASSES * P], U8, "w1_plane_0")
         for a in range(PASSES):
-            nc.vector.quantize_mx(
-                out=first_codes[:, P * a : P * (a + 1)].bitcast(FP8X4),
-                scales=first_plane[:, P * a : P * (a + 1)],
-                in_=first_grouped[:, a, :, :].rearrange("p c j -> p (c j)"),
-            )
-        w1_mx = [(first_codes, first_plane)]
-        v_words[(1, 1)] = alloc([P, BANK], U32, "v_1_1", "cast_room", 4 * T)
-        pick_words(1, BANK, S)
+            columns = slice(P * a, P * (a + 1))
+            quantise(codes[:, columns], plane[:, columns], grouped[:, a, :, :].rearrange("p c j -> p (c j)"))
+        w1_mx = [(codes, plane)]
+        pick_words(1, 1, "page_1_room", 4 * T)
+        pages.append(zeroed_window("page_1", "page_1_room"))
 
-        pages.append(zeroed_window("page_1", "cast_room"))
-        half = S // 2
         wgs_sb = alloc([P, S], F32, "wgs_sb", "second_room")
-        nc.sync.dma_start(wgs_sb[:, 0:half], wgs[:, 0:half])
-        nc.sync.dma_start(wgs_sb[:, half:S], wgs[:, half:S])
-        w1_raw.append(load_w1("w1_raw_2", 2 * P, H, "second_room", 8 * S, 4 * S))
-        idx3, idx4 = load_list(offs3, "idx3"), load_list(offs4, "idx4")
-
+        for h in range(2):
+            nc.sync.dma_start(wgs_sb[:, BANK * h : BANK * (h + 1)], wgs[:, BANK * h : BANK * (h + 1)])
+        w1_raw.append(load_w1("w1_raw_2", 2 * P, H, "second_room", 4 * S))
+        idx3 = load_list(offs3, "idx3")
+        idx4 = load_list(offs4, "idx4")
 
         pieces = [(b, sum(widths[:i]), width) for b, widths in enumerate(PIECES) for i, width in enumerate(widths)]
-        runs = []
-        squares = {}
-        places = {4: (("w1_raw_2_0",), ("w1_raw_2_0", 4 * BANK))}
+        last = len(pieces) - 1
+        squares, contests, weighted = {}, {}, {}
 
-        def project(b, start, width):
-            codes, plane = w1_mx[b]
-            bank0 = LOW if len(runs) == 2 else HIGH + 2 * (len(runs) % 2)
-            runs.append((b, start, width))
+        def project(k, bank0, after=None):
+            b, start, width = pieces[k]
+            w1_codes, w1_plane = w1_mx[b]
             a_bank, b_bank = bank(bank0, "a_bank"), bank(bank0 + 1, "b_bank")
             step = BANK if width == BANK else P
             for a in range(PASSES):
                 nc.tensor.matmul_mx(
                     out=a_bank[:, 0:width],
-                    lhsT=codes[:, P * a : P * (a + 1)].bitcast(FP8X4),
-                    lhsT_scale=plane[:, P * a : P * (a + 1)],
+                    lhsT=w1_codes[:, P * a : P * (a + 1)].bitcast(FP8X4),
+                    lhsT_scale=w1_plane[:, P * a : P * (a + 1)],
                     rhs=v_run(a, start, start + width),
                     rhs_scale=v_plane[:, S * a + start : S * a + start + width],
                     start=(a == 0),
                     stop=(a == PASSES - 1),
                 )
                 for offset in range(0, width, step):
-                    entries = slice(start + offset, start + offset + step)
+                    first = start + offset
                     nc.tensor.matmul_mx(
                         out=b_bank[:, offset : offset + step],
                         lhsT=w2_codes[:, a, 2 * P * b : 2 * P * (b + 1)].bitcast(FP4X4),
                         lhsT_scale=w2_plane[:, H * a + P * b : H * a + P * (b + 1)],
-                        rhs=v_run(a, entries.start, entries.stop),
-                        rhs_scale=v_plane[:, S * a + entries.start : S * a + entries.stop],
+                        rhs=v_run(a, first, first + step),
+                        rhs_scale=v_plane[:, S * a + first : S * a + first + step],
                         start=(a == 0 and offset == 0),
                         stop=(a == PASSES - 1 and offset + step == width),
                     )
-            for k, (block, first, count) in enumerate(pieces):
-                low, high = max(first, start), min(first + count, start + width)
-                if block == b and low < high:
-                    if k not in squares:
-                        squares[k] = [
-                            alloc([P, count], F32, "%s_sq_%d" % (x, k), *at) for x, at in zip("ab", places.get(k, ((), ())))
-                        ]
-                    for square, source in zip(squares[k], (a_bank, b_bank)):
-                        nc.scalar.activation(
-                            square[:, low - first : high - first], source[:, low - start : high - start], ACT.Square
-                        )
+            squares[k] = [alloc([P, width], F32, "%s_sq_%d" % (x, k), after, 4 * width * i) for i, x in enumerate("ab")]
+            for square, source in zip(squares[k], (a_bank, b_bank)):
+                nc.scalar.activation(square[:], source[:, 0:width], ACT.Square)
 
-        def project_piece(k):
-            project(*pieces[k])
+        def pair_of_banks(k):
+            return HIGH + 2 * (k % 2)
 
-        def project_block(b):
-            for start in range(0, S, BANK):
-                project(b, start, BANK)
-
-        contests, placeds = {}, {}
+        def forms(k):
+            return nc.vector if k < VECTOR_PIECES else nc.gpsimd
 
         def subtract(k, after=None):
-            engine = nc.vector if k < 2 else nc.gpsimd
-            a_sq, b_sq = squares[k]
             contests[k] = alloc([P, pieces[k][2]], F32, "contest_%d" % k, after)
-            engine.tensor_tensor(contests[k][:], a_sq[:], b_sq[:], ALU.subtract)
+            forms(k).tensor_tensor(contests[k][:], squares[k][0][:], squares[k][1][:], ALU.subtract)
 
-        def weigh(k, after=None):
-            engine = nc.vector if k < 2 else nc.gpsimd
+        def weigh(k, after=None, at=0):
             b, start, width = pieces[k]
-            placeds[k] = alloc([P, width], F32, "placed_%d" % k, after)
-            weight = wgs_sb[:, start : start + width]
-            engine.tensor_tensor(placeds[k][:], contests[k][:], weight, ALU.mult)
+            weighted[k] = alloc([P, width], F32, "weighted_%d" % k, after, at)
+            forms(k).tensor_tensor(weighted[k][:], contests[k][:], wgs_sb[:, start : start + width], ALU.mult)
 
         def scatter(k):
             b, start, width = pieces[k]
-            window = pages[b % PAGES][:].indirect(idx2[:, start // GROUP : (start + width) // GROUP])
-            nc.vector.tensor_copy(window, placeds[k][:])
+            window = pages[b % PAGES][:].indirect(entries_of(idx2, start, start + width))
+            nc.vector.tensor_copy(window, weighted[k][:])
 
-        def place_piece(k, contest_after=None, placed_after=None):
+        def place_piece(k, contest_after, weighted_after, weighted_at=0):
             subtract(k, contest_after)
-            weigh(k, placed_after)
+            weigh(k, weighted_after, weighted_at)
             scatter(k)
 
         z_turned = [
-            [alloc([P, 2, 2, P, 2], BF16, "z_turned_%d_%d" % (g, quarter)) for quarter in range(CHUNKS)] for g in range(2)
+            [alloc([P, 2, 2, P, 2], BF16, "z_turned_%d_%d" % (g, quarter)) for quarter in range(QUARTERS)]
+            for g in range(GROUPS)
         ]
 
         def add_board(b, board_after):
-            page = pages[b % PAGES]
-            last_block = b == ROW_BLOCKS - 1
+            g, c = divmod(b, 2)
             board_sb = load(board[P * b : P * (b + 1), :], [P, T], "board_%d" % b, board_after)
-            banks = LOW if b < 2 else HIGH
-            sums = [bank(banks + c, "z_bank") for c in range(CHUNKS)]
+            sums = [bank((LOW, HIGH)[g] + quarter, "z_bank") for quarter in range(QUARTERS)]
 
-            def turn(source, quarter, first):
+            def turn(source, quarter, opens):
                 h, a = divmod(quarter, 2)
                 for index in range(TILES):
                     s, j = divmod(index, 2)
-                    slot0 = BANK * (2 * h + j) + BANK // 2 * a + P * s
+                    slot0 = BANK * (2 * h + j) + QUARTER * a + P * s
                     nc.tensor.matmul(
                         sums[quarter][:, P * index : P * (index + 1)], source[:, slot0 : slot0 + P], ident[:],
-                        start=(first and index == 0), stop=(not first and index == TILES - 1), is_transpose=True,
+                        start=(opens and index == 0), stop=(not opens and index == TILES - 1), is_transpose=True,
                     )
 
-            for quarter in range(CHUNKS):
+            for quarter in range(QUARTERS):
                 turn(board_sb, quarter, True)
-            for quarter in range(CHUNKS):
-                turn(page, quarter, False)
-                dst = z_turned[b // 2][quarter][:].rearrange("p u s (j b i) e -> p b (s j) u i e", j=2, b=2)[:, b % 2]
+            for quarter in range(QUARTERS):
+                turn(pages[b % PAGES], quarter, False)
+                dst = z_turned[g][quarter][:].rearrange("p u s (j c i) e -> p c (s j) u i e", j=2, c=2)[:, c]
                 src = sums[quarter][:].rearrange("p (n i u e) -> p n u i e", n=TILES, u=2, e=2)
-                copy_out = nc.vector.tensor_copy if last_block and quarter % 2 else nc.scalar.copy
+                copy_out = nc.vector.tensor_copy if b == ROW_BLOCKS - 1 and quarter % 2 else nc.scalar.copy
                 copy_out(dst, src)
 
-        for name in ("contest_room_0", "contest_room_1", "placed_room_0", "placed_room_1", "placed_room_2"):
-            reserve(name, 4 * S)
-        second_grouped = alloc([P, PASSES, P, PACK], BF16, "w1_grouped_1", "tab_words_1")
-        cast_w1(1, w1_raw[1], 0, second_grouped, lambda dst, src: nc.vector.tensor_tensor(dst, src, src, ALU.max))
-        w1_mx.append(quantise_w1(1, second_grouped, "tab_words_0", "w1_room"))
-        for k in range(len(PIECES[0])):
-            project_piece(k)
-        subtract(0)
-        reserve("contest_1_room", 4 * BANK)
-        subtract(1, "contest_1_room")
-        weigh(0)
-        weigh(1, "contest_room_1")
-        scatter(0)
-        scatter(1)
-        place_piece(2, "contest_1_room")
-        last_grouped = alloc([P, 2, PASSES, P, PACK], BF16, "w1_grouped_2")
-        for i in range(2):
-            cast_w1(2 + i, w1_raw[2], P * i, last_grouped[:, i])
-        project_block(1)
-        codes = alloc([P, 2 * PASSES * P], U32, "w1_codes_2")
-        plane = alloc([P, 2 * PASSES * P], U8, "w1_plane_2")
-        nc.vector.quantize_mx(
-            out=codes[:].bitcast(FP8X4), scales=plane[:], in_=last_grouped[:].rearrange("p b a c j -> p (b a c j)")
-        )
-        for i in range(2):
-            columns = slice(PASSES * P * i, PASSES * P * (i + 1))
-            w1_mx.append((codes[:, columns], plane[:, columns]))
-        project_block(2)
-        project_block(3)
-        place["late_room"] = place["w1_raw_2_1"] + 4 * BANK
-        contest_chain = ["contest_2", "w1_grouped_2"]
-        placed_chain = ["late_room", "placed_room_1", "placed_room_0"]
-        place["late_codes_room"] = place["placed_room_2"]
-        board_after = ("board_room", "w1_room", "tab_words_0", "board_0")
-
-        def place_block(b):
-            for k in range(len(PIECES[0]), len(pieces)):
-                if pieces[k][0] == b:
-                    place_piece(k, contest_chain[-2], "placed_room_2" if k == len(pieces) - 3 else placed_chain[-3])
-                    contest_chain.append("contest_%d" % k)
-                    placed_chain.append("placed_%d" % k)
-            add_board(b, board_after[b])
-
-        def turn_back(g, grouped, vector_banks):
-            pair_banks = [bank((LOW, HIGH)[g] + index, "pair_bank") for index in range(CHUNKS)]
-            for index, pair_bank in enumerate(pair_banks):
-                z_pairs = z_turned[g][index][:].rearrange("p u s r e -> p (u s r e)").bitcast(F32)
+        def turn_back(g, z_grouped, vector_quarters):
+            pair_banks = [bank((LOW, HIGH)[g] + quarter, "pair_bank") for quarter in range(QUARTERS)]
+            for quarter, pair_bank in enumerate(pair_banks):
+                z_pairs = z_turned[g][quarter][:].rearrange("p u s r e -> p (u s r e)").bitcast(F32)
                 for i in range(TILES):
-                    nc.tensor.transpose(
-                        pair_bank[:, P * i : P * (i + 1)],
-                        z_pairs[:, P * i : P * (i + 1)],
-                        ident[:],
-                    )
-            for index, pair_bank in enumerate(pair_banks):
-                dst = grouped[:, BANK // 2 * index : BANK // 2 * (index + 1), :]
+                    nc.tensor.transpose(pair_bank[:, P * i : P * (i + 1)], z_pairs[:, P * i : P * (i + 1)], ident[:])
+            for quarter, pair_bank in enumerate(pair_banks):
+                dst = z_grouped[:, QUARTER * quarter : QUARTER * (quarter + 1), :]
                 dst = dst.rearrange("p c j -> p (c j)").bitcast(F32).rearrange("p (s c u) -> p s c u", s=2, u=2)
                 src = pair_bank[:].rearrange("p (u s c) -> p s c u", s=2, u=2)
-                if index in vector_banks:
-                    nc.vector.tensor_copy(dst, src)
-                else:
-                    nc.scalar.copy(dst, src)
-
-        def quantise_z(codes, plane, grouped, slots):
-            nc.vector.quantize_mx(
-                out=codes[:, slots].bitcast(FP8X4),
-                scales=plane[:, slots],
-                in_=grouped[:, slots, :].rearrange("p c j -> p (c j)"),
-            )
-
-        def first_block_passes(g, quarter, y_bank):
-            slots = slice(BANK // 2 * quarter, BANK // 2 * (quarter + 1))
-            for j in range(2):
-                nc.tensor.matmul_mx(
-                    out=y_bank[:, BANK // 2 * j : BANK // 2 * (j + 1)],
-                    lhsT=w3_halves[:, g, j, :].bitcast(FP8X4),
-                    lhsT_scale=(w3_plane if j == g else swapped_plane)[:, 0:P],
-                    rhs=z_codes[g][:, slots].bitcast(FP8X4),
-                    rhs_scale=z_planes[g][:, slots],
-                    start=(g == 0 and j == 0),
-                    stop=(g == 1 and j == 1),
-                )
+                copy_out = nc.vector.tensor_copy if quarter in vector_quarters else nc.scalar.copy
+                copy_out(dst, src)
 
         def move_half(dst, dst_half, src, src_half):
             nc.sync.dma_start(
@@ -396,13 +300,50 @@ def tile_list_pass_arbitration_scores_kernel(
                 src[HALF * src_half : HALF * (src_half + 1), :].bitcast(I32),
             )
 
-        place_block(0)
-        place_block(1)
-        reserve("group_room", 4 * (T + S))
-        grouped_0 = alloc([P, 2 * BANK, PACK], BF16, "z_grouped_0", "group_room", 4 * S)
-        turn_back(0, grouped_0, ())
-        place_block(2)
-        w3_codes = alloc([P, N], U32, "w3_codes", "v_1_1")
+        grouped = alloc([P, PASSES, P, PACK], BF16, "w1_grouped_1", "tab_words_1")
+        cast_w1(grouped, w1_raw[1], 0, lambda dst, src: nc.vector.tensor_tensor(dst, src, src, ALU.max))
+        project(0, pair_of_banks(0))
+        project(1, pair_of_banks(1))
+        project(2, LOW)
+        subtract(0, "tab_words_0")
+        reserve("contest_room", 4 * BANK)
+        subtract(1, "contest_room")
+        weigh(0)
+        weigh(1)
+        scatter(0)
+        codes = alloc([P, PASSES * P], U32, "w1_codes_1", "contest_0")
+        plane = alloc([P, PASSES * P], U8, "w1_plane_1", "board_1_room")
+        quantise(codes[:], plane[:], grouped[:].rearrange("p a c j -> p (a c j)"))
+        w1_mx.append((codes, plane))
+        scatter(1)
+        place_piece(2, "contest_room", "w1_grouped_1")
+        grouped = alloc([P, 2, PASSES, P, PACK], BF16, "w1_grouped_2")
+        for i in range(2):
+            cast_w1(grouped[:, i], w1_raw[2], P * i, nc.scalar.copy)
+        project(3, pair_of_banks(3))
+        project(4, pair_of_banks(4), "w1_raw_2_0")
+        codes = alloc([P, 2 * PASSES * P], U32, "w1_codes_2")
+        plane = alloc([P, 2 * PASSES * P], U8, "w1_plane_2")
+        quantise(codes[:], plane[:], grouped[:].rearrange("p b a c j -> p (b a c j)"))
+        for i in range(2):
+            columns = slice(PASSES * P * i, PASSES * P * (i + 1))
+            w1_mx.append((codes[:, columns], plane[:, columns]))
+        for k in range(5, last + 1):
+            project(k, pair_of_banks(k))
+
+        add_board(0, "board_0_room")
+        place_piece(3, "contest_2", "w1_raw_2_1", 4 * BANK)
+        place_piece(4, "w1_grouped_2", None)
+        add_board(1, "board_1_room")
+        reserve("group_0_room", 4 * S + 2 * PACK * PACKED)
+        z_grouped_0 = alloc([P, PACKED, PACK], BF16, "z_grouped_0", "group_0_room", 4 * S)
+        turn_back(0, z_grouped_0, ())
+        place_piece(5, "contest_3", None)
+        reserve("z_codes_0_room", 4 * PACKED)
+        place_piece(6, "contest_4", "z_codes_0_room")
+        add_board(2, "tab_words_0")
+
+        w3_codes = alloc([P, N], U32, "w3_codes", "v_words_1_1")
         nc.sync.dma_start(w3_codes[:].bitcast(I32), w3_words[0].rearrange("p c i -> p (c i)").bitcast(I32))
         w3_plane = zeroed_plane(nc.gpsimd, N, "w3_plane", "w1_codes_2")
         for q in range(QUADRANTS):
@@ -410,104 +351,109 @@ def tile_list_pass_arbitration_scores_kernel(
                 live_rows(w3_plane, q).bitcast(I32), w3_scales[0, PACK * q : PACK * (q + 1), :].bitcast(I32)
             )
         swapped_plane = alloc([P, P], U8, "swapped_plane")
-        for g in range(2):
+        for g in range(GROUPS):
             move_half(swapped_plane, 1 - g, w3_plane[:, 0:P], g)
-        last = len(pieces) - 1
-        place_piece(last - 1, contest_chain[-2], placed_chain[-3])
+
+        place_piece(last - 1, "contest_5", "weighted_4")
         subtract(last, "z_turned_0_3")
-        weigh(last, placed_chain[-2])
-        z_codes = [alloc([P, 2 * BANK], U32, "z_codes_0", "late_codes_room")]
-        quantise_z(z_codes[0], z_planes[0], grouped_0, slice(0, 2 * BANK))
-        w3_halves = alloc([P, 2, 2, P], U32, "w3_halves", "contest_%d" % last)
+        weigh(last, "weighted_5")
+        z_codes = [alloc([P, PACKED], U32, "z_codes_0", "z_codes_0_room")]
+        quantise(z_codes[0][:], z_planes[0][:], z_grouped_0[:].rearrange("p c j -> p (c j)"))
+
+        w3_halves = alloc([P, GROUPS, 2, P], U32, "w3_halves", "contest_%d" % last)
         nc.gpsimd.memset(w3_halves[:].bitcast(I32), 0)
-        for g in range(2):
+        for g in range(GROUPS):
             for j in range(2):
                 move_half(w3_halves[:, g, j, :], j, w3_codes[:, 0:P], g)
-        y_banks = [bank(LOW + c, "y_bank") for c in range(CHUNKS)]
-        for c in range(CHUNKS):
-            first_block_passes(0, c, y_banks[c])
-        odd_codes = alloc([P, 2 * BANK], U32, "odd_codes")
-        odd_plane = alloc([P, 2 * BANK], U8, "odd_plane")
+
+        y_banks = [bank(LOW + quarter, "y_bank") for quarter in range(QUARTERS)]
+
+        def first_rows_passes(g, quarter):
+            columns = slice(QUARTER * quarter, QUARTER * (quarter + 1))
+            for j in range(2):
+                nc.tensor.matmul_mx(
+                    out=y_banks[quarter][:, QUARTER * j : QUARTER * (j + 1)],
+                    lhsT=w3_halves[:, g, j, :].bitcast(FP8X4),
+                    lhsT_scale=(w3_plane if j == g else swapped_plane)[:, 0:P],
+                    rhs=z_codes[g][:, columns].bitcast(FP8X4),
+                    rhs_scale=z_planes[g][:, columns],
+                    start=(g == 0 and j == 0),
+                    stop=(g == GROUPS - 1 and j == 1),
+                )
+
+        for quarter in range(QUARTERS):
+            first_rows_passes(0, quarter)
+        odd_codes = alloc([P, PACKED], U32, "odd_codes")
+        odd_plane = alloc([P, PACKED], U8, "odd_plane")
         move_half(odd_codes, 0, z_codes[0], 1)
         move_half(odd_plane, 0, z_planes[0], 1)
         scatter(last)
-        add_board(3, board_after[3])
+        add_board(3, "board_0")
 
-        wgo_sb = load(wgo, [P, S], "wgo_sb", "v_words_0")
         prio_places = (("board_1", 0), ("board_2", 0), ("board_2", 4 * S))
+        wgo_sb = load(wgo, [P, S], "wgo_sb", "v_words_0_0")
         prios = [load(prio[P * n : P * (n + 1), :], [P, S], "prio_%d" % n, *prio_places[n]) for n in range(OUT_BLOCKS)]
-
-        first_weight = alloc([P, S], F32, "first_weight", "group_room", 4 * T)
+        first_weight = alloc([P, S], F32, "first_weight", "group_0_room", 4 * T)
         nc.gpsimd.tensor_tensor(first_weight[:], prios[0][:], wgo_sb[:], ALU.mult)
-        second_result = zeroed_window("result_1", "group_room")
+        second_result = zeroed_window("result_1", "group_0_room")
 
-        row_bytes = 4 * T
-        reserve("result_room", 2 * row_bytes)
-        grouped_1 = alloc([P, 2 * BANK, PACK], BF16, "z_grouped_1", "result_room", row_bytes // 2)
-        turn_back(1, grouped_1, (1,))
-        z_codes.append(alloc([P, 2 * BANK], U32, "z_codes_1"))
-        gates = [alloc([P, T], F32, "gates_0")]
-        by_quarter = gates[0][:].rearrange("p (h j a c) -> p h a j c", h=2, j=2, a=2)
-        for quarter in range(CHUNKS):
-            quantise_z(z_codes[1], z_planes[1], grouped_1, slice(BANK // 2 * quarter, BANK // 2 * (quarter + 1)))
-            first_block_passes(1, quarter, y_banks[quarter])
-            copy_out = nc.vector.tensor_copy if quarter == CHUNKS - 1 else nc.scalar.copy
+        reserve("result_room", 2 * 4 * T)
+        z_grouped_1 = alloc([P, PACKED, PACK], BF16, "z_grouped_1", "result_room", 2 * T)
+        turn_back(1, z_grouped_1, (1,))
+        z_codes.append(alloc([P, PACKED], U32, "z_codes_1"))
+        first_scores = alloc([P, T], F32, "first_scores")
+        by_quarter = first_scores[:].rearrange("p (h j a c) -> p h a j c", h=2, j=2, a=2)
+        for quarter in range(QUARTERS):
+            columns = slice(QUARTER * quarter, QUARTER * (quarter + 1))
+            quantise(
+                z_codes[1][:, columns], z_planes[1][:, columns], z_grouped_1[:, columns, :].rearrange("p c j -> p (c j)")
+            )
+            first_rows_passes(1, quarter)
+            copy_out = nc.vector.tensor_copy if quarter == QUARTERS - 1 else nc.scalar.copy
             copy_out(by_quarter[:, quarter // 2, quarter % 2], y_banks[quarter][:].rearrange("p (j c) -> p j c", j=2))
-        for dst, src in ((z_codes[0], z_codes[1]), (z_planes[0], z_planes[1])):
-            move_half(dst, 1, src, 0)
-        for dst, src in ((odd_codes, z_codes[1]), (odd_plane, z_planes[1])):
-            move_half(dst, 1, src, 1)
+        for j, joined in enumerate(((z_codes[0], z_planes[0]), (odd_codes, odd_plane))):
+            for dst, src in zip(joined, (z_codes[1], z_planes[1])):
+                move_half(dst, 1, src, j)
 
-        def score(n, c, index):
+        def score(gates, n, c):
             h, j = divmod(c, 2)
-            codes, plane = ((z_codes[0], z_planes[0]), (odd_codes, odd_plane))[j]
-            slots = slice(BANK * h, BANK * (h + 1))
-            y_bank = bank(index, "y_bank")
+            joined_codes, joined_plane = ((z_codes[0], z_planes[0]), (odd_codes, odd_plane))[j]
+            columns = slice(BANK * h, BANK * (h + 1))
+            y_bank = bank(HIGH + c, "y_bank")
             nc.tensor.matmul_mx(
                 out=y_bank[:],
                 lhsT=w3_codes[:, P * n : P * (n + 1)].bitcast(FP8X4),
                 lhsT_scale=w3_plane[:, P * n : P * (n + 1)],
-                rhs=codes[:, slots].bitcast(FP8X4),
-                rhs_scale=plane[:, slots],
+                rhs=joined_codes[:, columns].bitcast(FP8X4),
+                rhs_scale=joined_plane[:, columns],
                 start=True,
                 stop=True,
             )
-            nc.scalar.activation(gates[n][:, BANK * c : BANK * (c + 1)], y_bank[:], ACT.Sigmoid)
+            nc.scalar.activation(gates[:, BANK * c : BANK * (c + 1)], y_bank[:], ACT.Sigmoid)
 
-        first_result = zeroed_window("result_0", "result_room", row_bytes)
+        first_result = zeroed_window("result_0", "result_room", 4 * T)
         last_result = zeroed_window("result_2", "result_room")
-        results = (first_result, second_result, last_result)
-        gates.append(alloc([P, T], F32, "gates_1", "z_turned_1_0"))
+        second_gates = alloc([P, T], F32, "second_gates", "z_turned_1_0")
         for c in (0, 2, 1, 3):
-            score(1, c, HIGH + c)
-
-        picked_gates = [None]
-
-        def pick(n):
-            after = ("a_sq_5", "a_sq_6", "page_0")[n]
-            picked_gate = alloc([P, S], F32, "picked_gates_%d" % n, after)
-            nc.vector.tensor_tensor(picked_gate[:], gates[n][:].indirect(idx3[:]), prios[n][:], ALU.mult)
-            picked_gates.append(picked_gate)
+            score(second_gates, 1, c)
 
         first_gates = []
-        for i in range(2):
-            picked = alloc([P, BANK], F32, "picked_scores_%d" % i, "a_sq_5", 4 * BANK * i)
-            nc.vector.tensor_copy(picked[:], gates[0][:].indirect(idx3[:, 32 * i : 32 * (i + 1)]))
-            first_gates.append(alloc([P, BANK], F32, "first_gates_%d" % i, "page_1", 4 * BANK * i))
-            nc.scalar.activation(first_gates[i][:], picked[:], ACT.Sigmoid)
-        gates.append(alloc([P, T], F32, "gates_2", "prio_0"))
+        for h in range(2):
+            picked = alloc([P, BANK], F32, "picked_scores_%d" % h, "a_sq_5", 4 * BANK * h)
+            nc.vector.tensor_copy(picked[:], first_scores[:].indirect(entries_of(idx3, BANK * h, BANK * (h + 1))))
+            first_gates.append(alloc([P, BANK], F32, "first_gates_%d" % h, "page_1", 4 * BANK * h))
+            nc.scalar.activation(first_gates[h][:], picked[:], ACT.Sigmoid)
+        last_gates = alloc([P, T], F32, "last_gates", "prio_0")
         for c in range(CHUNKS):
-            score(2, c, HIGH + c)
-
-        def put(n):
-            nc.vector.tensor_tensor(results[n][:].indirect(idx4[:]), picked_gates[n][:], wgo_sb[:], ALU.mult)
-            nc.sync.dma_start(out[P * n : P * (n + 1), :], results[n][:])
-
-        for i in range(2):
-            window = results[0][:].indirect(idx4[:, 32 * i : 32 * (i + 1)])
-            nc.vector.tensor_tensor(window, first_gates[i][:], first_weight[:, BANK * i : BANK * (i + 1)], ALU.mult)
-        nc.sync.dma_start(out[0:P, :], results[0][:])
-        pick(1)
-        pick(2)
-        put(1)
-        put(2)
+            score(last_gates, 2, c)
+        for h in range(2):
+            window = first_result[:].indirect(entries_of(idx4, BANK * h, BANK * (h + 1)))
+            nc.vector.tensor_tensor(window, first_gates[h][:], first_weight[:, BANK * h : BANK * (h + 1)], ALU.mult)
+        nc.sync.dma_start(out[0:P, :], first_result[:])
+        picked_gates = []
+        for n, gates, after in ((1, second_gates, "a_sq_6"), (2, last_gates, "page_0")):
+            picked_gates.append(alloc([P, S], F32, "picked_gates_%d" % n, after))
+            nc.vector.tensor_tensor(picked_gates[-1][:], gates[:].indirect(idx3[:]), prios[n][:], ALU.mult)
+        for n, result, picked_gate in zip((1, 2), (second_result, last_result), picked_gates):
+            nc.vector.tensor_tensor(result[:].indirect(idx4[:]), picked_gate[:], wgo_sb[:], ALU.mult)
+            nc.sync.dma_start(out[P * n : P * (n + 1), :], result[:])

@@ -395,13 +395,13 @@ def tile_list_pass_arbitration_scores_kernel(
         prios = [load(prio[P * n : P * (n + 1), :], [P, S], "prio_%d" % n, *prio_places[n]) for n in range(OUT_BLOCKS)]
         first_weight = alloc([P, S], F32, "first_weight", "group_0_room", 4 * T)
         nc.gpsimd.tensor_tensor(first_weight[:], prios[0][:], wgo_sb[:], ALU.mult)
-        second_result = zeroed_window("result_1", "group_0_room")
+        first_result = zeroed_window("result_0", "group_0_room")
 
-        reserve("result_room", 2 * 4 * T)
-        z_grouped_1 = alloc([P, PACKED, PACK], BF16, "z_grouped_1", "result_room", 2 * T)
+        z_grouped_1 = alloc([P, PACKED, PACK], BF16, "z_grouped_1")
         turn_back(1, z_grouped_1, (1,))
         z_codes.append(alloc([P, PACKED], U32, "z_codes_1"))
-        first_scores = alloc([P, T], F32, "first_scores")
+        reserve("result_room", 2 * 4 * T)
+        first_scores = alloc([P, T], F32, "first_scores", "result_room", 2 * T)
         by_quarter = first_scores[:].rearrange("p (h j a c) -> p h a j c", h=2, j=2, a=2)
         for quarter in range(QUARTERS):
             columns = slice(QUARTER * quarter, QUARTER * (quarter + 1))
@@ -431,8 +431,6 @@ def tile_list_pass_arbitration_scores_kernel(
             )
             nc.scalar.activation(gates[:, BANK * c : BANK * (c + 1)], y_bank[:], ACT.Sigmoid)
 
-        first_result = zeroed_window("result_0", "result_room", 4 * T)
-        last_result = zeroed_window("result_2", "result_room")
         second_gates = alloc([P, T], F32, "second_gates", "z_turned_1_0")
         for c in (0, 2, 1, 3):
             score(second_gates, 1, c)
@@ -443,6 +441,8 @@ def tile_list_pass_arbitration_scores_kernel(
             nc.vector.tensor_copy(picked[:], first_scores[:].indirect(entries_of(idx3, BANK * h, BANK * (h + 1))))
             first_gates.append(alloc([P, BANK], F32, "first_gates_%d" % h, "page_1", 4 * BANK * h))
             nc.scalar.activation(first_gates[h][:], picked[:], ACT.Sigmoid)
+        second_result = zeroed_window("result_1", "result_room")
+        last_result = zeroed_window("result_2", "result_room", 4 * T)
         last_gates = alloc([P, T], F32, "last_gates", "prio_0")
         for c in range(CHUNKS):
             score(last_gates, 2, c)

@@ -143,7 +143,8 @@ def tile_list_pass_arbitration_scores_kernel(
         w1_raw = [load_w1("w1_raw_0", 0, P, "board_1_room")]
         w2_codes = alloc([P, PASSES, 2 * H], U8, "w2_codes")
         nc.sync.dma_start(w2_codes[:].bitcast(I32), w2_words.rearrange("a p c -> p a c").bitcast(I32))
-        w1_raw.append(load_w1("w1_raw_1", P, 2 * P))
+        wgs_sb = alloc([P, S], F32, "wgs_sb")
+        nc.sync.dma_start(wgs_sb[:, 0:BANK], wgs[:, 0:BANK])
         idx2 = load_list(offs2, "idx2")
 
         ident = alloc([P, P], F32, "ident")
@@ -178,7 +179,8 @@ def tile_list_pass_arbitration_scores_kernel(
         grouped = alloc([P, PASSES, P, PACK], BF16, "w1_grouped_0", "page_1_room", 4 * T - KB)
         cast_w1(grouped, w1_raw[0], 0, nc.scalar.copy)
         codes = alloc([P, PASSES * P], U32, "w1_codes_0", "board_0_room")
-        plane = alloc([P, PASSES * P], U8, "w1_plane_0")
+        reserve("grouped_1_room", 2 * KB)
+        plane = alloc([P, PASSES * P], U8, "w1_plane_0", "grouped_1_room")
         for a in range(PASSES):
             columns = slice(P * a, P * (a + 1))
             quantise(codes[:, columns], plane[:, columns], grouped[:, a, :, :].rearrange("p c j -> p (c j)"))
@@ -186,9 +188,8 @@ def tile_list_pass_arbitration_scores_kernel(
         pick_words(1, 1, "page_1_room", 4 * T)
         pages.append(zeroed_window("page_1", "page_1_room"))
 
-        wgs_sb = alloc([P, S], F32, "wgs_sb", "second_room")
-        for h in range(2):
-            nc.sync.dma_start(wgs_sb[:, BANK * h : BANK * (h + 1)], wgs[:, BANK * h : BANK * (h + 1)])
+        w1_raw.append(load_w1("w1_raw_1", P, 2 * P, "second_room"))
+        nc.sync.dma_start(wgs_sb[:, BANK:S], wgs[:, BANK:S])
         w1_raw.append(load_w1("w1_raw_2", 2 * P, H, "second_room", 4 * S))
         idx3 = load_list(offs3, "idx3")
         idx4 = load_list(offs4, "idx4")
@@ -201,7 +202,7 @@ def tile_list_pass_arbitration_scores_kernel(
             b, start, width = pieces[k]
             w1_codes, w1_plane = w1_mx[b]
             a_bank, b_bank = bank(bank0, "a_bank"), bank(bank0 + 1, "b_bank")
-            step = BANK if width == BANK else P
+            step = width
             for a in range(PASSES):
                 nc.tensor.matmul_mx(
                     out=a_bank[:, 0:width],
@@ -300,18 +301,18 @@ def tile_list_pass_arbitration_scores_kernel(
                 src[HALF * src_half : HALF * (src_half + 1), :].bitcast(I32),
             )
 
-        grouped = alloc([P, PASSES, P, PACK], BF16, "w1_grouped_1", "tab_words_1")
-        cast_w1(grouped, w1_raw[1], 0, lambda dst, src: nc.vector.tensor_tensor(dst, src, src, ALU.max))
         project(0, pair_of_banks(0))
         project(1, pair_of_banks(1))
         project(2, LOW)
-        subtract(0, "tab_words_0")
+        grouped = alloc([P, PASSES, P, PACK], BF16, "w1_grouped_1", "grouped_1_room")
+        cast_w1(grouped, w1_raw[1], 0, nc.scalar.copy)
         reserve("contest_room", 4 * BANK)
-        subtract(1, "contest_room")
+        subtract(0, "contest_room")
+        subtract(1)
         weigh(0)
-        weigh(1)
         scatter(0)
-        codes = alloc([P, PASSES * P], U32, "w1_codes_1", "contest_0")
+        weigh(1, "w1_raw_1_1")
+        codes = alloc([P, PASSES * P], U32, "w1_codes_1", "tab_words_0")
         plane = alloc([P, PASSES * P], U8, "w1_plane_1", "board_1_room")
         quantise(codes[:], plane[:], grouped[:].rearrange("p a c j -> p (a c j)"))
         w1_mx.append((codes, plane))

@@ -101,9 +101,9 @@ def tile_list_pass_arbitration_scores_kernel(
             nc.sync.dma_start(words[:].bitcast(I32), tab_words[a].rearrange("p t i -> p (t i)").bitcast(I32))
             return words
 
-        def load_w1(name, first, last, after=None, at=0):
+        def load_w1(name, first, last, after=None, at=0, passes=range(PASSES)):
             tiles = []
-            for a in range(PASSES):
+            for a in passes:
                 pass_bytes = 4 * PACK * (last - first)
                 dst = alloc([P, PACK, last - first], F32, "%s_%d" % (name, a), after, at + pass_bytes * a)
                 src = w1[K_PASS * a : K_PASS * (a + 1), first:last].rearrange("(p j) c -> p j c", j=PACK)
@@ -111,11 +111,11 @@ def tile_list_pass_arbitration_scores_kernel(
                 tiles.append(dst)
             return tiles
 
-        def cast_w1(grouped, raw, column0, copy):
+        def cast_w1(grouped, raw):
             for a in range(PASSES):
-                copy(
+                nc.scalar.copy(
                     grouped[:, a, :, :].rearrange("p (c i) j -> p c j i", i=4),
-                    raw[a][:, :, column0 : column0 + P].rearrange("p j (c i) -> p c j i", i=4),
+                    raw[a][:].rearrange("p j (c i) -> p c j i", i=4),
                 )
 
         def quantise(codes, plane, grouped):
@@ -143,6 +143,7 @@ def tile_list_pass_arbitration_scores_kernel(
         w1_raw = [load_w1("w1_raw_0", 0, P, "board_1_room")]
         w2_codes = alloc([P, PASSES, 2 * H], U8, "w2_codes")
         nc.sync.dma_start(w2_codes[:].bitcast(I32), w2_words.rearrange("a p c -> p a c").bitcast(I32))
+        w1_raw.append(load_w1("w1_raw_1", P, 2 * P, passes=(0,)))
         wgs_sb = alloc([P, S], F32, "wgs_sb")
         nc.sync.dma_start(wgs_sb[:, 0:BANK], wgs[:, 0:BANK])
         idx2 = load_list(offs2, "idx2")
@@ -177,18 +178,18 @@ def tile_list_pass_arbitration_scores_kernel(
         reserve("page_1_room", 4 * T + 4 * BANK)
         reserve("board_0_room", 4 * T)
         grouped = alloc([P, PASSES, P, PACK], BF16, "w1_grouped_0", "page_1_room", 4 * T - KB)
-        cast_w1(grouped, w1_raw[0], 0, nc.scalar.copy)
+        cast_w1(grouped, w1_raw[0])
         codes = alloc([P, PASSES * P], U32, "w1_codes_0", "board_0_room")
         reserve("grouped_1_room", 2 * KB)
         plane = alloc([P, PASSES * P], U8, "w1_plane_0", "grouped_1_room")
         for a in range(PASSES):
             columns = slice(P * a, P * (a + 1))
             quantise(codes[:, columns], plane[:, columns], grouped[:, a, :, :].rearrange("p c j -> p (c j)"))
-        w1_mx = [(codes, plane)]
+        w1_mx = [(codes, plane, 0, P)]
         pick_words(1, 1, "page_1_room", 4 * T)
         pages.append(zeroed_window("page_1", "page_1_room"))
 
-        w1_raw.append(load_w1("w1_raw_1", P, 2 * P, "second_room"))
+        w1_raw[1].extend(load_w1("w1_raw_1", P, 2 * P, "second_room", passes=(1,)))
         nc.sync.dma_start(wgs_sb[:, BANK:S], wgs[:, BANK:S])
         w1_raw.append(load_w1("w1_raw_2", 2 * P, H, "second_room", 4 * S))
         idx3 = load_list(offs3, "idx3")
@@ -200,14 +201,15 @@ def tile_list_pass_arbitration_scores_kernel(
 
         def project(k, bank0, after=None):
             b, start, width = pieces[k]
-            w1_codes, w1_plane = w1_mx[b]
+            w1_codes, w1_plane, column0, pass_columns = w1_mx[b]
             a_bank, b_bank = bank(bank0, "a_bank"), bank(bank0 + 1, "b_bank")
             step = width
             for a in range(PASSES):
+                columns = slice(column0 + pass_columns * a, column0 + pass_columns * a + P)
                 nc.tensor.matmul_mx(
                     out=a_bank[:, 0:width],
-                    lhsT=w1_codes[:, P * a : P * (a + 1)].bitcast(FP8X4),
-                    lhsT_scale=w1_plane[:, P * a : P * (a + 1)],
+                    lhsT=w1_codes[:, columns].bitcast(FP8X4),
+                    lhsT_scale=w1_plane[:, columns],
                     rhs=v_run(a, start, start + width),
                     rhs_scale=v_plane[:, S * a + start : S * a + start + width],
                     start=(a == 0),
@@ -305,7 +307,7 @@ def tile_list_pass_arbitration_scores_kernel(
         project(1, pair_of_banks(1))
         project(2, LOW)
         grouped = alloc([P, PASSES, P, PACK], BF16, "w1_grouped_1", "grouped_1_room")
-        cast_w1(grouped, w1_raw[1], 0, nc.scalar.copy)
+        cast_w1(grouped, w1_raw[1])
         reserve("contest_room", 4 * BANK)
         subtract(0, "contest_room")
         subtract(1)
@@ -315,20 +317,17 @@ def tile_list_pass_arbitration_scores_kernel(
         codes = alloc([P, PASSES * P], U32, "w1_codes_1", "tab_words_0")
         plane = alloc([P, PASSES * P], U8, "w1_plane_1", "board_1_room")
         quantise(codes[:], plane[:], grouped[:].rearrange("p a c j -> p (a c j)"))
-        w1_mx.append((codes, plane))
+        w1_mx.append((codes, plane, 0, P))
         scatter(1)
         place_piece(2, "contest_room", "w1_grouped_1")
-        grouped = alloc([P, 2, PASSES, P, PACK], BF16, "w1_grouped_2")
-        for i in range(2):
-            cast_w1(grouped[:, i], w1_raw[2], P * i, nc.scalar.copy)
+        grouped = alloc([P, PASSES, 2 * P, PACK], BF16, "w1_grouped_2")
+        cast_w1(grouped, w1_raw[2])
         project(3, pair_of_banks(3))
         project(4, pair_of_banks(4), "w1_raw_2_0")
         codes = alloc([P, 2 * PASSES * P], U32, "w1_codes_2")
         plane = alloc([P, 2 * PASSES * P], U8, "w1_plane_2")
-        quantise(codes[:], plane[:], grouped[:].rearrange("p b a c j -> p (b a c j)"))
-        for i in range(2):
-            columns = slice(PASSES * P * i, PASSES * P * (i + 1))
-            w1_mx.append((codes[:, columns], plane[:, columns]))
+        quantise(codes[:], plane[:], grouped[:].rearrange("p a c j -> p (a c j)"))
+        w1_mx.extend((codes, plane, P * i, 2 * P) for i in range(2))
         for k in range(5, last + 1):
             project(k, pair_of_banks(k))
 

@@ -360,7 +360,7 @@ def tile_list_pass_arbitration_scores_kernel(
         z_codes = [alloc([P, PACKED], U32, "z_codes_0", "z_codes_0_room")]
         quantise(z_codes[0][:], z_planes[0][:], z_grouped_0[:].rearrange("p c j -> p (c j)"))
 
-        w3_halves = alloc([P, GROUPS, 2, P], U32, "w3_halves", "contest_%d" % last)
+        w3_halves = alloc([P, GROUPS, 2, P], U32, "w3_halves", "contest_6")
         nc.gpsimd.memset(w3_halves[:].bitcast(I32), 0)
         for g in range(GROUPS):
             for j in range(2):

@@ -255,8 +255,16 @@ def tile_list_pass_arbitration_scores_kernel(
             weigh(k, weighted_after, weighted_at)
             scatter(k)
 
+        reserve("group_0_room", 4 * T + 4 * KB + 4 * S)
+        held = {(1, 2): 4 * T, (1, 3): 4 * T + 2 * KB}
         z_turned = [
-            [alloc([P, 2, 2, P, 2], BF16, "z_turned_%d_%d" % (g, quarter)) for quarter in range(QUARTERS)]
+            [
+                alloc(
+                    [P, 2, 2, P, 2], BF16, "z_turned_%d_%d" % (g, quarter),
+                    "group_0_room" if (g, quarter) in held else None, held.get((g, quarter), 0),
+                )
+                for quarter in range(QUARTERS)
+            ]
             for g in range(GROUPS)
         ]
 
@@ -335,8 +343,7 @@ def tile_list_pass_arbitration_scores_kernel(
         place_piece(3, "contest_2", "w1_raw_2_1", 4 * BANK)
         place_piece(4, "w1_grouped_2", None)
         add_board(1, "board_1_room")
-        reserve("group_0_room", 4 * S + 2 * PACK * PACKED)
-        z_grouped_0 = alloc([P, PACKED, PACK], BF16, "z_grouped_0", "group_0_room", 4 * S)
+        z_grouped_0 = alloc([P, PACKED, PACK], BF16, "z_grouped_0", "group_0_room", 6 * KB)
         turn_back(0, z_grouped_0, ())
         place_piece(5, "contest_3", None)
         reserve("z_codes_0_room", 4 * PACKED)
@@ -393,7 +400,7 @@ def tile_list_pass_arbitration_scores_kernel(
         prio_places = (("board_1", 0), ("board_2", 0), ("board_2", 4 * S))
         wgo_sb = load(wgo, [P, S], "wgo_sb", "v_words_0_0")
         prios = [load(prio[P * n : P * (n + 1), :], [P, S], "prio_%d" % n, *prio_places[n]) for n in range(OUT_BLOCKS)]
-        first_weight = alloc([P, S], F32, "first_weight", "group_0_room", 4 * T)
+        first_weight = alloc([P, S], F32, "first_weight", "group_0_room", 4 * T + 4 * KB)
         nc.gpsimd.tensor_tensor(first_weight[:], prios[0][:], wgo_sb[:], ALU.mult)
         first_result = zeroed_window("result_0", "group_0_room")
 

@@ -114,8 +114,8 @@ def tile_list_pass_arbitration_scores_kernel(
         def cast_w1(grouped, raw):
             for a in range(PASSES):
                 nc.scalar.copy(
-                    grouped[:, a, :, :].rearrange("p (c i) j -> p c j i", i=4),
-                    raw[a][:].rearrange("p j (c i) -> p c j i", i=4),
+                    grouped[:, a, :, :].rearrange("p (c i) j -> p c j i", i=2),
+                    raw[a][:].rearrange("p j (c i) -> p c j i", i=2),
                 )
 
         def quantise(codes, plane, grouped):

import math
from contextlib import ExitStack

import concourse.mybir as mybir
from concourse.masks import make_identity

K, H, N, T, S = 1024, 512, 384, 2048, 1024
FLOPS = 2 * (2 * K * H * S + H * N * T)

F32 = mybir.dt.float32
BF16 = mybir.dt.bfloat16
I32 = mybir.dt.int32
U32 = mybir.dt.uint32
U16 = mybir.dt.uint16
U8 = mybir.dt.uint8
FP8X4 = mybir.dt.float8_e4m3fn_x4
FP4X4 = mybir.dt.float4_e2m1fn_x4
ACT = mybir.ActivationFunctionType
ALU = mybir.AluOpType

P = 128
HALF = P // 2
PACK = 4
K_PASS = P * PACK
PASSES = K // K_PASS
QUADRANT = 32
QUADRANTS = P // QUADRANT
SCALE_ROW0 = P - PASSES * K_PASS // 32
LIST_ROWS = 16
BANK = 512
TILES = BANK // P
LOW, HIGH = 0, 4
ROW_BLOCKS = H // P
OUT_BLOCKS = N // P
CHUNKS = T // BANK
GROUPS = 2
PACKED = T // 2
QUARTERS = 4
QUARTER = PACKED // QUARTERS
PIECES = ((256, 256, 512), (512, 512), (512, 512), (512, 512))
VECTOR_PIECES = 2
PAGES = 2
KB = 1024
ALIGN = 64
ITEM_BYTES = {F32: 4, U32: 4, BF16: 2, U8: 1}


def tile_list_pass_arbitration_scores_kernel(
    tc, tab_words, tab_scales, offs, w1, w2_words, w2_scales, wgs, offs2, board,
    w3_words, w3_scales, offs3, prio, wgo, offs4, out,
):
    nc = tc.nc
    with ExitStack() as ctx:
        lists = ctx.enter_context(tc.tile_pool(name="lists", bufs=1))
        sbuf = ctx.enter_context(tc.tile_pool(name="sbuf", bufs=1))
        psum = ctx.enter_context(tc.psum_pool(name="psum", bufs=1))
        place = {"free": 0}

        def reserve(name, size):
            place[name] = place["free"]
            place["free"] = place[name] + -(-size // ALIGN) * ALIGN

        def alloc(shape, dtype, name, after=None, at=0):
            if after:
                place[name] = place[after] + at
            else:
                reserve(name, math.prod(shape[1:]) * ITEM_BYTES[dtype])
            return sbuf.tile(shape, dtype, name=name, offset=place[name], align_bytes=ALIGN)

        def bank(index, name):
            return psum.tile([P, BANK], F32, name=name, tag="bank%d" % index)

        def load_list(src, name):
            dst = lists.tile([P, S // LIST_ROWS], U16, name=name)
            nc.sync.dma_start(dst[:], src)
            return dst

        def entries_of(list_tile, first, last):
            return list_tile[:, first // LIST_ROWS : last // LIST_ROWS]

        def load(src, shape, name, after, at=0):
            dst = alloc(shape, F32, name, after, at)
            nc.sync.dma_start(dst[:], src)
            return dst

        def zeroed_plane(engine, width, name, after=None):
            plane = alloc([P, width], U8, name, after)
            engine.memset(plane[:].bitcast(I32), 0)
            return plane

        def zeroed_window(name, after=None, at=0):
            window = alloc([P, T], F32, name, after, at)
            nc.gpsimd.memset(window[:], 0.0)
            return window

        def live_rows(plane, q):
            return plane[QUADRANT * q : QUADRANT * q + PACK, :]

        def load_table_pass(a):
            words = alloc([P, T], U32, "tab_words_%d" % a)
            nc.sync.dma_start(words[:].bitcast(I32), tab_words[a].rearrange("p t i -> p (t i)").bitcast(I32))
            return words

        def load_w1(name, first, last, after=None, at=0, passes=range(PASSES)):
            tiles = []
            for a in passes:
                pass_bytes = 4 * PACK * (last - first)
                dst = alloc([P, PACK, last - first], F32, "%s_%d" % (name, a), after, at + pass_bytes * a)
                src = w1[K_PASS * a : K_PASS * (a + 1), first:last].rearrange("(p j) c -> p j c", j=PACK)
                nc.sync.dma_start(dst[:], src)
                tiles.append(dst)
            return tiles

        def cast_w1(grouped, raw):
            for a in range(PASSES):
                nc.scalar.copy(
                    grouped[:, a, :, :].rearrange("p (c i) j -> p c j i", i=2),
                    raw[a][:].rearrange("p j (c i) -> p c j i", i=2),
                )

        def quantise(codes, plane, grouped):
            nc.vector.quantize_mx(out=codes.bitcast(FP8X4), scales=plane, in_=grouped)

        w2_plane = zeroed_plane(nc.gpsimd, PASSES * H, "w2_plane")
        for q in range(QUADRANTS):
            nc.gpsimd.dma_start(
                live_rows(w2_plane, q).rearrange("p (a c) -> p a c", a=PASSES).bitcast(I32),
                w2_scales[:, PACK * q : PACK * (q + 1), :].rearrange("a r c -> r a c").bitcast(I32),
            )
        warmup_in = alloc([P, 1], F32, "warmup_in")
        nc.vector.memset(warmup_in[:], 0.0)
        table_warmup = alloc([P, 1], F32, "table_warmup")
        nc.scalar.activation(table_warmup[:], warmup_in[:], ACT.Sigmoid)

        idx = load_list(offs, "idx")
        tab_plane = alloc([P, 12 * KB], U8, "second_room")[:, 0:T]
        nc.sync.dma_start(
            tab_plane[SCALE_ROW0:P, :].bitcast(I32), tab_scales.rearrange("a q c -> q a c").bitcast(I32)
        )
        nc.vector.memset(tab_plane[0:SCALE_ROW0, :].bitcast(I32), 0)
        tab_tiles = [load_table_pass(a) for a in range(PASSES)]
        reserve("board_1_room", 4 * T)
        w1_raw = [load_w1("w1_raw_0", 0, P, "board_1_room")]
        w2_codes = alloc([P, PASSES, 2 * H], U8, "w2_codes")
        nc.sync.dma_start(w2_codes[:].bitcast(I32), w2_words.rearrange("a p c -> p a c").bitcast(I32))
        w1_raw.append(load_w1("w1_raw_1", P, 2 * P, passes=(0,)))
        wgs_sb = alloc([P, S], F32, "wgs_sb")
        nc.sync.dma_start(wgs_sb[:, 0:BANK], wgs[:, 0:BANK])
        idx2 = load_list(offs2, "idx2")

        ident = alloc([P, P], F32, "ident")
        make_identity(nc, ident[:])
        pages = [zeroed_window("page_0")]
        z_planes = [zeroed_plane(nc.gpsimd, PACKED, "z_plane_%d" % g) for g in range(GROUPS)]

        v_plane = zeroed_plane(nc.vector, PASSES * S, "v_plane")
        picked_scales = alloc([P, S], U8, "picked_scales")
        nc.vector.tensor_copy(picked_scales[:], tab_plane.indirect(idx[:]))
        quadrant_rows = PASSES * PACK
        for q in range(QUADRANTS):
            nc.scalar.dma_start(
                live_rows(v_plane, q).bitcast(I32),
                picked_scales[SCALE_ROW0 + quadrant_rows * q : SCALE_ROW0 + quadrant_rows * (q + 1), :].bitcast(I32),
            )

        v_words = {}

        def pick_words(a, h, after=None, at=0):
            v_words[(a, h)] = alloc([P, BANK], U32, "v_words_%d_%d" % (a, h), after, at)
            nc.vector.tensor_copy(v_words[(a, h)][:], tab_tiles[a][:].indirect(entries_of(idx, BANK * h, BANK * (h + 1))))

        def v_run(a, first, last):
            return v_words[(a, first // BANK)][:, first % BANK : first % BANK + last - first].bitcast(FP8X4)

        pick_words(0, 0)
        pick_words(0, 1)
        pick_words(1, 0)
        reserve("page_1_room", 4 * T + 4 * BANK)
        reserve("board_0_room", 4 * T)
        grouped = alloc([P, PASSES, P, PACK], BF16, "w1_grouped_0", "page_1_room", 4 * T - KB)
        cast_w1(grouped, w1_raw[0])
        codes = alloc([P, PASSES * P], U32, "w1_codes_0", "board_0_room")
        reserve("grouped_1_room", 2 * KB)
        plane = alloc([P, PASSES * P], U8, "w1_plane_0", "grouped_1_room")
        for a in range(PASSES):
            columns = slice(P * a, P * (a + 1))
            quantise(codes[:, columns], plane[:, columns], grouped[:, a, :, :].rearrange("p c j -> p (c j)"))
        w1_mx = [(codes, plane, 0, P)]
        pick_words(1, 1, "page_1_room", 4 * T)
        pages.append(zeroed_window("page_1", "page_1_room"))

        w1_raw[1].extend(load_w1("w1_raw_1", P, 2 * P, "second_room", passes=(1,)))
        nc.sync.dma_start(wgs_sb[:, BANK:S], wgs[:, BANK:S])
        w1_raw.append(load_w1("w1_raw_2", 2 * P, H, "second_room", 4 * S))
        idx3 = load_list(offs3, "idx3")
        idx4 = load_list(offs4, "idx4")

        pieces = [(b, sum(widths[:i]), width) for b, widths in enumerate(PIECES) for i, width in enumerate(widths)]
        last = len(pieces) - 1
        squares, contests, weighted = {}, {}, {}

        def project(k, bank0, after=None):
            b, start, width = pieces[k]
            w1_codes, w1_plane, column0, pass_columns = w1_mx[b]
            a_bank, b_bank = bank(bank0, "a_bank"), bank(bank0 + 1, "b_bank")
            step = width
            for a in range(PASSES):
                columns = slice(column0 + pass_columns * a, column0 + pass_columns * a + P)
                nc.tensor.matmul_mx(
                    out=a_bank[:, 0:width],
                    lhsT=w1_codes[:, columns].bitcast(FP8X4),
                    lhsT_scale=w1_plane[:, columns],
                    rhs=v_run(a, start, start + width),
                    rhs_scale=v_plane[:, S * a + start : S * a + start + width],
                    start=(a == 0),
                    stop=(a == PASSES - 1),
                )
                for offset in range(0, width, step):
                    first = start + offset
                    nc.tensor.matmul_mx(
                        out=b_bank[:, offset : offset + step],
                        lhsT=w2_codes[:, a, 2 * P * b : 2 * P * (b + 1)].bitcast(FP4X4),
                        lhsT_scale=w2_plane[:, H * a + P * b : H * a + P * (b + 1)],
                        rhs=v_run(a, first, first + step),
                        rhs_scale=v_plane[:, S * a + first : S * a + first + step],
                        start=(a == 0 and offset == 0),
                        stop=(a == PASSES - 1 and offset + step == width),
                    )
            squares[k] = [alloc([P, width], F32, "%s_sq_%d" % (x, k), after, 4 * width * i) for i, x in enumerate("ab")]
            for square, source in zip(squares[k], (a_bank, b_bank)):
                nc.scalar.activation(square[:], source[:, 0:width], ACT.Square)

        def pair_of_banks(k):
            return HIGH + 2 * (k % 2)

        def forms(k):
            return nc.vector if k < VECTOR_PIECES else nc.gpsimd

        def subtract(k, after=None):
            contests[k] = alloc([P, pieces[k][2]], F32, "contest_%d" % k, after)
            forms(k).tensor_tensor(contests[k][:], squares[k][0][:], squares[k][1][:], ALU.subtract)

        def weigh(k, after=None, at=0):
            b, start, width = pieces[k]
            weighted[k] = alloc([P, width], F32, "weighted_%d" % k, after, at)
            forms(k).tensor_tensor(weighted[k][:], contests[k][:], wgs_sb[:, start : start + width], ALU.mult)

        def scatter(k):
            b, start, width = pieces[k]
            window = pages[b % PAGES][:].indirect(entries_of(idx2, start, start + width))
            nc.vector.tensor_copy(window, weighted[k][:])

        def place_piece(k, contest_after, weighted_after, weighted_at=0):
            subtract(k, contest_after)
            weigh(k, weighted_after, weighted_at)
            scatter(k)

        reserve("group_0_room", 4 * T + 4 * KB + 4 * S)
        held = {(1, 2): 4 * T, (1, 3): 4 * T + 2 * KB}
        z_turned = [
            [
                alloc(
                    [P, 2, 2, P, 2], BF16, "z_turned_%d_%d" % (g, quarter),
                    "group_0_room" if (g, quarter) in held else None, held.get((g, quarter), 0),
                )
                for quarter in range(QUARTERS)
            ]
            for g in range(GROUPS)
        ]

        def add_board(b, board_after):
            g, c = divmod(b, 2)
            board_sb = load(board[P * b : P * (b + 1), :], [P, T], "board_%d" % b, board_after)
            sums = [bank((LOW, HIGH)[g] + quarter, "z_bank") for quarter in range(QUARTERS)]

            def turn(source, quarter, opens):
                h, a = divmod(quarter, 2)
                for index in range(TILES):
                    s, j = divmod(index, 2)
                    slot0 = BANK * (2 * h + j) + QUARTER * a + P * s
                    nc.tensor.matmul(
                        sums[quarter][:, P * index : P * (index + 1)], source[:, slot0 : slot0 + P], ident[:],
                        start=(opens and index == 0), stop=(not opens and index == TILES - 1), is_transpose=True,
                    )

            for quarter in range(QUARTERS):
                turn(board_sb, quarter, True)
            for quarter in range(QUARTERS):
                turn(pages[b % PAGES], quarter, False)
                dst = z_turned[g][quarter][:].rearrange("p u s (j c i) e -> p c (s j) u i e", j=2, c=2)[:, c]
                src = sums[quarter][:].rearrange("p (n i u e) -> p n u i e", n=TILES, u=2, e=2)
                copy_out = nc.vector.tensor_copy if b == ROW_BLOCKS - 1 and quarter % 2 else nc.scalar.copy
                copy_out(dst, src)

        def turn_back(g, z_grouped, vector_quarters):
            pair_banks = [bank((LOW, HIGH)[g] + quarter, "pair_bank") for quarter in range(QUARTERS)]
            for quarter, pair_bank in enumerate(pair_banks):
                z_pairs = z_turned[g][quarter][:].rearrange("p u s r e -> p (u s r e)").bitcast(F32)
                for i in range(TILES):
                    nc.tensor.transpose(pair_bank[:, P * i : P * (i + 1)], z_pairs[:, P * i : P * (i + 1)], ident[:])
            for quarter, pair_bank in enumerate(pair_banks):
                dst = z_grouped[:, QUARTER * quarter : QUARTER * (quarter + 1), :]
                dst = dst.rearrange("p c j -> p (c j)").bitcast(F32).rearrange("p (s c u) -> p s c u", s=2, u=2)
                src = pair_bank[:].rearrange("p (u s c) -> p s c u", s=2, u=2)
                copy_out = nc.vector.tensor_copy if quarter in vector_quarters else nc.scalar.copy
                copy_out(dst, src)

        def move_half(dst, dst_half, src, src_half):
            nc.sync.dma_start(
                dst[HALF * dst_half : HALF * (dst_half + 1), :].bitcast(I32),
                src[HALF * src_half : HALF * (src_half + 1), :].bitcast(I32),
            )

        project(0, pair_of_banks(0))
        project(1, pair_of_banks(1))
        project(2, LOW)
        grouped = alloc([P, PASSES, P, PACK], BF16, "w1_grouped_1", "grouped_1_room")
        cast_w1(grouped, w1_raw[1])
        reserve("contest_room", 4 * BANK)
        subtract(0, "contest_room")
        subtract(1)
        weigh(0)
        scatter(0)
        weigh(1, "w1_raw_1_1")
        codes = alloc([P, PASSES * P], U32, "w1_codes_1", "tab_words_0")
        plane = alloc([P, PASSES * P], U8, "w1_plane_1", "board_1_room")
        quantise(codes[:], plane[:], grouped[:].rearrange("p a c j -> p (a c j)"))
        w1_mx.append((codes, plane, 0, P))
        scatter(1)
        place_piece(2, "contest_room", "w1_grouped_1")
        grouped = alloc([P, PASSES, 2 * P, PACK], BF16, "w1_grouped_2")
        cast_w1(grouped, w1_raw[2])
        project(3, pair_of_banks(3))
        project(4, pair_of_banks(4), "w1_raw_2_0")
        codes = alloc([P, 2 * PASSES * P], U32, "w1_codes_2")
        plane = alloc([P, 2 * PASSES * P], U8, "w1_plane_2")
        quantise(codes[:], plane[:], grouped[:].rearrange("p a c j -> p (a c j)"))
        w1_mx.extend((codes, plane, P * i, 2 * P) for i in range(2))
        for k in range(5, last + 1):
            project(k, pair_of_banks(k))

        add_board(0, "board_0_room")
        place_piece(3, "contest_2", "w1_raw_2_1", 4 * BANK)
        place_piece(4, "w1_grouped_2", None)
        add_board(1, "board_1_room")
        z_grouped_0 = alloc([P, PACKED, PACK], BF16, "z_grouped_0", "group_0_room", 6 * KB)
        turn_back(0, z_grouped_0, ())
        place_piece(5, "contest_3", None)
        reserve("z_codes_0_room", 4 * PACKED)
        place_piece(6, "contest_4", "z_codes_0_room")
        add_board(2, "tab_words_0")

        w3_codes = alloc([P, N], U32, "w3_codes", "v_words_1_1")
        nc.sync.dma_start(w3_codes[:].bitcast(I32), w3_words[0].rearrange("p c i -> p (c i)").bitcast(I32))
        w3_plane = zeroed_plane(nc.gpsimd, N, "w3_plane", "w1_codes_2")
        for q in range(QUADRANTS):
            nc.sync.dma_start(
                live_rows(w3_plane, q).bitcast(I32), w3_scales[0, PACK * q : PACK * (q + 1), :].bitcast(I32)
            )
        swapped_plane = alloc([P, P], U8, "swapped_plane")
        for g in range(GROUPS):
            move_half(swapped_plane, 1 - g, w3_plane[:, 0:P], g)

        place_piece(last - 1, "contest_5", "weighted_4")
        subtract(last, "z_turned_0_3")
        weigh(last, "weighted_5")
        z_codes = [alloc([P, PACKED], U32, "z_codes_0", "z_codes_0_room")]
        quantise(z_codes[0][:], z_planes[0][:], z_grouped_0[:].rearrange("p c j -> p (c j)"))

        w3_halves = alloc([P, GROUPS, 2, P], U32, "w3_halves", "contest_6")
        nc.gpsimd.memset(w3_halves[:].bitcast(I32), 0)
        for g in range(GROUPS):
            for j in range(2):
                move_half(w3_halves[:, g, j, :], j, w3_codes[:, 0:P], g)

        y_banks = [bank(LOW + quarter, "y_bank") for quarter in range(QUARTERS)]

        def first_rows_passes(g, quarter):
            columns = slice(QUARTER * quarter, QUARTER * (quarter + 1))
            for j in range(2):
                nc.tensor.matmul_mx(
                    out=y_banks[quarter][:, QUARTER * j : QUARTER * (j + 1)],
                    lhsT=w3_halves[:, g, j, :].bitcast(FP8X4),
                    lhsT_scale=(w3_plane if j == g else swapped_plane)[:, 0:P],
                    rhs=z_codes[g][:, columns].bitcast(FP8X4),
                    rhs_scale=z_planes[g][:, columns],
                    start=(g == 0 and j == 0),
                    stop=(g == GROUPS - 1 and j == 1),
                )

        for quarter in range(QUARTERS):
            first_rows_passes(0, quarter)
        odd_codes = alloc([P, PACKED], U32, "odd_codes")
        odd_plane = alloc([P, PACKED], U8, "odd_plane")
        move_half(odd_codes, 0, z_codes[0], 1)
        move_half(odd_plane, 0, z_planes[0], 1)
        scatter(last)
        add_board(3, "board_0")

        prio_places = (("board_1", 0), ("board_2", 0), ("board_2", 4 * S))
        wgo_sb = load(wgo, [P, S], "wgo_sb", "v_words_0_0")
        prios = [load(prio[P * n : P * (n + 1), :], [P, S], "prio_%d" % n, *prio_places[n]) for n in range(OUT_BLOCKS)]
        first_weight = alloc([P, S], F32, "first_weight", "group_0_room", 4 * T + 4 * KB)
        nc.gpsimd.tensor_tensor(first_weight[:], prios[0][:], wgo_sb[:], ALU.mult)
        first_result = zeroed_window("result_0", "group_0_room")

        z_grouped_1 = alloc([P, PACKED, PACK], BF16, "z_grouped_1")
        turn_back(1, z_grouped_1, (1,))
        z_codes.append(alloc([P, PACKED], U32, "z_codes_1"))
        reserve("result_room", 2 * 4 * T)
        first_scores = alloc([P, T], F32, "first_scores", "result_room", 2 * T)
        by_quarter = first_scores[:].rearrange("p (h j a c) -> p h a j c", h=2, j=2, a=2)
        for quarter in range(QUARTERS):
            columns = slice(QUARTER * quarter, QUARTER * (quarter + 1))
            quantise(
                z_codes[1][:, columns], z_planes[1][:, columns], z_grouped_1[:, columns, :].rearrange("p c j -> p (c j)")
            )
            first_rows_passes(1, quarter)
            copy_out = nc.vector.tensor_copy if quarter == QUARTERS - 1 else nc.scalar.copy
            copy_out(by_quarter[:, quarter // 2, quarter % 2], y_banks[quarter][:].rearrange("p (j c) -> p j c", j=2))
        for j, joined in enumerate(((z_codes[0], z_planes[0]), (odd_codes, odd_plane))):
            for dst, src in zip(joined, (z_codes[1], z_planes[1])):
                move_half(dst, 1, src, j)

        def score(gates, n, c):
            h, j = divmod(c, 2)
            joined_codes, joined_plane = ((z_codes[0], z_planes[0]), (odd_codes, odd_plane))[j]
            columns = slice(BANK * h, BANK * (h + 1))
            y_bank = bank(HIGH + c, "y_bank")
            nc.tensor.matmul_mx(
                out=y_bank[:],
                lhsT=w3_codes[:, P * n : P * (n + 1)].bitcast(FP8X4),
                lhsT_scale=w3_plane[:, P * n : P * (n + 1)],
                rhs=joined_codes[:, columns].bitcast(FP8X4),
                rhs_scale=joined_plane[:, columns],
                start=True,
                stop=True,
            )
            nc.scalar.activation(gates[:, BANK * c : BANK * (c + 1)], y_bank[:], ACT.Sigmoid)

        second_gates = alloc([P, T], F32, "second_gates", "z_turned_1_0")
        for c in (0, 2, 1, 3):
            score(second_gates, 1, c)

        first_gates = []
        for h in range(2):
            picked = alloc([P, BANK], F32, "picked_scores_%d" % h, "a_sq_5", 4 * BANK * h)
            nc.vector.tensor_copy(picked[:], first_scores[:].indirect(entries_of(idx3, BANK * h, BANK * (h + 1))))
            first_gates.append(alloc([P, BANK], F32, "first_gates_%d" % h, "page_1", 4 * BANK * h))
            nc.scalar.activation(first_gates[h][:], picked[:], ACT.Sigmoid)
        second_result = zeroed_window("result_1", "result_room")
        last_result = zeroed_window("result_2", "result_room", 4 * T)
        last_gates = alloc([P, T], F32, "last_gates", "prio_0")
        for c in range(CHUNKS):
            score(last_gates, 2, c)
        for h in range(2):
            window = first_result[:].indirect(entries_of(idx4, BANK * h, BANK * (h + 1)))
            nc.vector.tensor_tensor(window, first_gates[h][:], first_weight[:, BANK * h : BANK * (h + 1)], ALU.mult)
        nc.sync.dma_start(out[0:P, :], first_result[:])
        picked_gates = []
        for n, gates, after in ((1, second_gates, "a_sq_6"), (2, last_gates, "page_0")):
            picked_gates.append(alloc([P, S], F32, "picked_gates_%d" % n, after))
            nc.vector.tensor_tensor(picked_gates[-1][:], gates[:].indirect(idx3[:]), prios[n][:], ALU.mult)
        for n, result, picked_gate in zip((1, 2), (second_result, last_result), picked_gates):
            nc.vector.tensor_tensor(result[:].indirect(idx4[:]), picked_gate[:], wgo_sb[:], ALU.mult)
            nc.sync.dma_start(out[P * n : P * (n + 1), :], result[:])
